import numpy as np, ml_dtypes
CORES = [1,5,17,21,33,37,49,53]
N = 8
BF = ml_dtypes.bfloat16
def gentries(a):
    return np.ascontiguousarray(a.reshape(8, 16, -1).transpose(0, 2, 1)).reshape(8, -1)
def gtable(e):
    e = np.asarray(e); return np.ascontiguousarray(e.reshape(8, -1, 16).transpose(0, 2, 1)).reshape(128, -1).astype(np.int32)
W, I, J, A, B, P, RO = 4096, 1536, 2048, 16, 8, 64, 5
def column(i, j):
    return ((((2 * i + 1) * (2 * j + 1)) >> 5) + 37 * i + j) & (W - 1)
def sized(rng, n, lo, hi, noise):
    b = np.exp2(lo + (hi - lo) * rng.random((N, 8, 1, n), dtype=np.float32))
    return (b * np.exp2(noise * (2 * rng.random((N, 8, 16, n), dtype=np.float32) - 1))).astype(np.int64)
def parts(rng):
    v = np.minimum(np.maximum(sized(rng, W, 2.6, 6.8, 0.5), 1), 127)
    rl = rng.integers(0, J, (N, 8, 16, I)); cl = rng.integers(0, I, (N, 8, 16, J))
    i = rng.integers(0, I, (N, 8, P)); j = rng.integers(0, J, (N, 8, P))
    return v, rl, cl, i, j, np.minimum(sized(rng, P, 1.0, 6.0, 0.5), 127)
def pack(v, rl, cl, i, j, z):
    return {"fig": np.ascontiguousarray(v.reshape(N, 128, W)).astype(np.float32).astype(BF), "rmate": np.ascontiguousarray(rl.reshape(N, 128, I)).astype(np.int32), "cmate": np.ascontiguousarray(cl.reshape(N, 128, J)).astype(np.int32),
            "prow": np.stack([gtable(a) for a in i]), "pcol": np.stack([gtable(a) for a in j]), "need": np.ascontiguousarray(z.reshape(N, 128, P)).astype(np.float32).astype(BF)}
def some(rng, good, free):
    n = np.flatnonzero(good & free)
    if len(n) == 0: n = np.flatnonzero(free)
    return n[rng.integers(0, len(n), 128)]
def fill(rng, v, rl, cl, i, j, z, g):
    v[:, g] = 40 + np.argsort(rng.random((N, 16, W)), axis=1); z[:, g] = 0
    seen = np.zeros((N, W), bool); rows = np.zeros((N, I), bool); cols = np.zeros((N, J), bool); ai = np.arange(I); aj = np.arange(J)
    for q in range(N):
        i[q, g] = rng.permutation(I)[:P]; j[q, g] = rng.permutation(J)[:P]; rows[q, i[q, g]] = True; cols[q, j[q, g]] = True
    x = np.array(i[:, g]); y = np.array(j[:, g])
    for t in range(RO):
        if t == RO - 1: rows[:] = False; cols[:] = False
        nx = np.zeros_like(x); ny = np.zeros_like(y)
        for q in range(N):
            to = (q + 1 + t % 3) % N
            for k in range(P):
                a, b = int(x[q, k]), int(y[q, k])
                u = some(rng, ~seen[q][column(a, aj)], ~cols[to]); w = some(rng, ~seen[q][column(ai, b)], ~rows[to])
                c = np.stack([column(a, u), column(w, b), column(w, u)])
                n = int(np.argmax(~seen[q][c[2]] & (c[0] != c[1]) & (c[0] != c[2]) & (c[1] != c[2])))
                seen[q, c[:, n]] = True; cols[to, u[n]] = True; rows[to, w[n]] = True
                rl[q, g, :, a] = u[n]; cl[q, g, :, b] = w[n]; nx[to, k] = w[n]; ny[to, k] = u[n]
        x, y = nx, ny
def setup_inputs(rng):
    return pack(*parts(rng))
def setup_inputs_ties(rng):
    v, rl, cl, i, j, z = parts(rng)
    v = rng.choice(np.array([8, 16, 32, 64]), (N, 8, 1, W)) + np.zeros((1, 1, 16, 1), np.int64)
    low = (rng.random((N, 8, 1, W)) < 0.3) & (np.arange(16)[:, None] == rng.integers(0, 16, (N, 8, 1, W)))
    z = rng.choice(np.array([0, 1, 8, 9, 16, 32, 33, 64, 65]), (N, 8, 1, P)) + np.zeros((1, 1, 16, 1), np.int64)
    v = v - low; fill(rng, v, rl, cl, i, j, z, 3)
    return pack(v, rl, cl, i, j, z)
def setup_inputs_none(rng):
    v, rl, cl, i, j, z = parts(rng)
    h = int(rng.integers(0, 8)); z[int(rng.integers(0, N))] = 0; z[:, h] = 127; v[:, h] = np.minimum(v[:, h], 126)
    for g, a, b in (((h + 1) % 8, A - 1, B - 1), ((h + 2) % 8, 0, 0)):
        v[:, g] = np.minimum(v[:, g], 10); z[:, g] = rng.integers(20, 30, (N, 16, P))
        for q in range(N):
            for k in range(8):
                x, y = int(i[q, g, k]), int(j[q, g, k]); u, w = int(rl[q, g, a, x]), int(cl[q, g, b, y])
                for c in (column(x, u), column(w, y), column(w, u)): v[q, g, :, c] = 127
    return pack(v, rl, cl, i, j, z)
def setup_inputs_alike(rng):
    v, rl, cl, i, j, z = parts(rng); z = z // 4
    i[:, [0, 4]] = i[:, [0, 4], :1]; j[:, [0, 4]] = j[:, [0, 4], :1]; z[:, [0, 4]] = z[:, [0, 4], :, :1]
    rl[:, [1, 5]] = rng.choice(np.array([0, 5, J - 1]), (N, 2, 16, I)); cl[:, [1, 5]] = rng.choice(np.array([0, 7, I - 1]), (N, 2, 16, J))
    i[:, 2] = rng.choice(np.array([0, 1, I // 2, I - 1]), (N, P)); j[:, 2] = rng.choice(np.array([0, 1, J // 2, J - 1]), (N, P))
    rl[:, 6] = rl[:, 6, :1]; cl[:, 6] = cl[:, 6, :1]
    for q in range(N):
        rl[q, 7, 0, i[q, 7]] = j[q, 7]; cl[q, 7, 0, j[q, 7]] = i[q, 7]
        cl[q, 4, :, int(j[q, 4, 0])] = int(i[q, 4, 0])
    z[:, 4] = 0
    rl[:, 3] = np.where(rng.random((N, 16, I)) < 0.5, rng.choice(np.array([0, J - 1]), (N, 16, I)), rl[:, 3])
    cl[:, 3] = np.where(rng.random((N, 16, J)) < 0.5, rng.choice(np.array([0, I - 1]), (N, 16, J)), cl[:, 3])
    i[:, 3] = np.where(rng.random((N, P)) < 0.5, rng.choice(np.array([0, I - 1]), (N, P)), i[:, 3])
    j[:, 3] = np.where(rng.random((N, P)) < 0.5, rng.choice(np.array([0, J - 1]), (N, P)), j[:, 3])
    return pack(v, rl, cl, i, j, z)
def setup_inputs_late(rng):
    v, rl, cl, i, j, z = parts(rng); z = z // 4
    for g in range(8):
        s = rng.permutation(16)
        for q in range(N):
            a, b = int(s[q % 2]), int(s[1 - q % 2])
            v[q, g, a] = np.minimum(v[q, g, a], 12); z[q, g, a] = rng.integers(13, 30, P); z[q, g, b] = np.minimum(z[q, g, b], 6)
    return pack(v, rl, cl, i, j, z)
def setup_inputs_spread(rng):
    v, rl, cl, i, j, z = parts(rng)
    v = np.minimum(np.maximum(sized(rng, W, 0.0, 7.3, 0.3), 1), 127)
    z = np.minimum(sized(rng, P, -1.0, 7.2, 0.2), 127)
    v[:, 2] = rng.integers(123, 128, (N, 16, W)); z[:, 2] = np.minimum(z[:, 2], 60)
    v[:, 5] = np.where(rng.random((N, 1, W)) < 0.5, 127, 1); z[:, 5] = 127
    return pack(v, rl, cl, i, j, z)
def check_inputs(d):
    bad = []
    for k, lo, hi in (("fig", 1, 127), ("rmate", 0, J - 1), ("cmate", 0, I - 1), ("prow", 0, I - 1), ("pcol", 0, J - 1), ("need", 0, 127)):
        v = np.asarray(d[k]).astype(np.float64)
        if not (np.all(v >= lo) and np.all(v <= hi) and np.all(v == np.floor(v))): bad.append("range of " + k)
    return bad
def look(h, c, z):
    m = c.shape[1]; v = np.take_along_axis(h, c.reshape(8, 1, m * P), 2).reshape(8, 16, m, P)
    return np.all(np.abs(v) >= z[:, :, None, :], axis=1), np.sum(np.maximum(v, 0), axis=1)
def reference(fig, rmate, cmate, prow, pcol, need):
    h = fig.astype(np.float32).astype(np.int32).reshape(N, 8, 16, W); z = need.astype(np.float32).astype(np.int32).reshape(N, 8, 16, P)
    rm = rmate.astype(np.int64).reshape(N, 8, 16, I); cm = cmate.astype(np.int64).reshape(N, 8, 16, J)
    i = np.stack([gentries(a) for a in prow]).astype(np.int64); j = np.stack([gentries(a) for a in pcol]).astype(np.int64)
    cost = np.zeros((N, 8, RO, P), np.float32); gi = np.arange(8)[:, None] + np.zeros((1, P), np.int64)
    for t in range(RO):
        ra = A * (t % (16 // A)); rb = B * (t % (16 // B)); sh = 1 + t % 3
        ni, nj, nz = [None] * N, [None] * N, [None] * N
        for q in range(N):
            x, y = i[q], j[q]
            jm = np.take_along_axis(rm[q][:, ra:ra + A], x[:, None, :], 2)
            im = np.take_along_axis(cm[q][:, rb:rb + B], y[:, None, :], 2)
            ok1, c1 = look(h[q], column(x[:, None, :], jm), z[q]); ok2, c2 = look(h[q], column(im, y[:, None, :]), z[q])
            ok3, c3 = look(h[q], column(im[:, None, :, :], jm[:, :, None, :]).reshape(8, A * B, P), z[q])
            ok = (ok1[:, :, None, :] & ok2[:, None, :, :]).reshape(8, A * B, P) & ok3
            total = (c1[:, :, None, :] + c2[:, None, :, :]).reshape(8, A * B, P) + c3
            total = np.where(ok, total, 2 ** 20)
            best = np.argmin(total, axis=1); good = np.any(ok, axis=1)
            cost[q, :, t] = np.where(good, np.take_along_axis(total, best[:, None, :], 1)[:, 0], -1)
            u = np.take_along_axis(jm, (best // B)[:, None, :], 1)[:, 0]; w = np.take_along_axis(im, (best % B)[:, None, :], 1)[:, 0]
            far = column(w, u); hit = np.zeros((8, W), bool)
            for c in (column(x, u), column(w, y), far): hit[gi[good], c[good]] = True
            size = np.abs(h[q]); fresh = np.take_along_axis(size, far[:, None, :], 2) >> 1
            h[q] = np.where(hit[:, None, :], -size, h[q])
            to = (q + sh) % N
            ni[to] = np.where(good, w, x); nj[to] = np.where(good, u, y); nz[to] = np.where(good[:, None, :], fresh, z[q])
        i = np.stack(ni); j = np.stack(nj); z = np.stack(nz)
    yp = np.stack([gtable(np.concatenate([i[q], j[q]], axis=1)) for q in range(N)])
    return {"yf": h.reshape(N, 128, W).astype(np.float32).astype(BF), "yp": yp.astype(np.float32), "yz": z.reshape(N, 128, P).astype(np.float32).astype(BF), "yc": cost.reshape(N, 8, RO * P)}

@@ -1,0 +1,359 @@
+from concourse.mybir import AluOpType as Op, AxisListType, ActivationFunctionType as Act
+
+W, P, RO = 4096, 64, 5
+ROT = 315
+BAD = float(1 << 20)
+BIG = float(1 << 27)
+OUT = 16384.0
+SCRATCH = {}
+
+
+def _bufs(dtype, text, where="sbuf"):
+    for item in text.split(","):
+        f = item.split()
+        SCRATCH[f[0]] = (where, [int(f[2]) if len(f) > 2 else 128, int(f[1])], dtype)
+
+
+_bufs("bfloat16", "GF2 512, GP2 512, C2f 64 64, EXf 128 64, FA 4160, PP 4160, NA 4096, ND 64, MM 384, NS 320, NR 1024, GF 9216, GP 9216, AB 768, MN 768, ZER 64, YZo 64")
+_bufs("bfloat16", "TBf 32, E8 512, LIDX 128 2, IDXR 512 2, INDF 64, INDP 64, IND1 64, DIAG 192, RS16 192, RS64 768, ONE 128 2, XPRE 256 1, JPRE 160 2, MPRE 192 1")
+_bufs("int32", "RM 1536, CM 2048, PR 8, PI 1, QI 4, CI 192, TI 256, DI 12, GPi 1, SPi 1, MG 128, MS 192, M7 128, M1 128, MH 128 64, M8 64, Pc 608, Pi 608, KM 160, T32 32, PF 192, FI 192, YI 80")
+_bufs("uint16", "LL 48, LS 40, OF 608, TNu 4, TS 12")
+_bufs("float16", "C2p 64 64, EXp 128 64, IJ 768, IS 640, IJD 128, BLK 128, BLKo 128, SEL 2048, DUP 512, M2S 256, TMP 512, ID 128, I2 128, I2h 256, EI 128, EJ 128, SELW 128, SELJ 128, TRI 256, Xf 64, UAW 128, B01 64, VD 192")
+_bufs("float32", "PRf 8, GPf 1, SPf 1, PIf 1, QP 4, SPQ 16, SPm 2, SY 32, cX 1, cW 1, cJ 1, ownA 1, ownB 1, ownT 1, RS2 32, DUM 12, Yp 64, YM 128, Y2 32, S1 32, ST 32, LD 128, LSc 128, UWs 128, SL 192, TN 4, DU 12, DV 12, DW 12, YT 80, YC 80, YPo 8")
+_bufs("float32", "XB0 512, XB1 512, JI 512, MB 512, KT 512, TAB 512, UW 512, KEY 512", "psum")
+SCRATCH["KEY"] = ("psum", [128, 8, 64], "float32")
+SCRATCH["YO"] = ("sbuf", [8, 4, 80], "float32")
+SEMAPHORES = ["sV", "sS", "sT", "sP", "ls", "out", "gd", "gd2"] + ["ld%d" % k for k in range(7)] + ["%s%d" % (m, t) for m in "lin" for t in range(1, RO + 1)]
+
+
+def rank_program(g, core, T, topo):
+    rank = T.rank_of(core)
+    if rank is None:
+        return
+    n_ranks = len(T.cores)
+    QS = {"V": g.vector, "S": g.scalar, "T": g.tensor, "P": g, "D": g.sync}
+    cnt = {q: 0 for q in "VSTP"}
+    known = {q: {} for q in QS}
+    snaps = {}
+    hist = {}
+
+    def v(name, lo=0, hi=None, st=1, r=None):
+        hi = SCRATCH[name][1][1] if hi is None else hi
+        return T[name][0:(r or SCRATCH[name][1][0]), lo:hi:st], [(name, lo, hi, st)]
+    def w(name, lo, n, st=1): return v(name, lo, lo + n * st, st)
+    def ix(name, hi, lst): return T[name][:, 0:hi].indirect(lst[0]), [(name, 0, hi, 1)] + lst[1]
+    def key(ap): return ap, [("KEY", 0, 512, 1)]
+    def ext(ap, name=None): return ap, [(name, 0, 1, 1)] if name else []
+
+    def wait(q, ev, n):
+        if known[q].get(ev, 0) < n:
+            QS[q].wait_ge(T.sem["s" + ev if ev in cnt else ev], n)
+            known[q][ev] = n
+            for e2, n2 in snaps.get((ev, n), {}).items(): known[q][e2] = max(known[q].get(e2, 0), n2)
+
+    def order(q, rd, wr, ev, n):
+        need = {}
+        acc = [(x, False) for o in rd for x in o[1]] + [(x, True) for x in wr[1]]
+        for (name, lo, hi, st), write in acc:
+            bank = SCRATCH[name][0] == "psum" if name in SCRATCH else False
+            for a in hist.get(name, []):
+                apart = a[1] <= lo or hi <= a[0] or (a[2] == st > 1 and (a[0] - lo) % st)
+                if bank and a[3] != q: apart = False
+                elif not (write or a[5]) or (q == a[3] == "T"): continue
+                if not apart: need[a[3]] = max(need.get(a[3], 0), a[4])
+        for e, c in sorted(need.items(), key=lambda x: (x[0] == q, x[0])): wait(q, e, c)
+        snaps[(ev, n)] = dict(known[q])
+        for (name, lo, hi, st), write in acc:
+            bank = SCRATCH[name][0] == "psum" if name in SCRATCH else False
+            hist[name] = [a for a in hist.get(name, []) if not ((bank and a[3] != q) or (lo <= a[0] and a[1] <= hi and a[2] % st == 0 and (a[0] - lo) % st == 0 and (write or (a[3] == ev and not a[5]))))]
+            hist[name].append([lo, hi, st, ev, n, write])
+
+    def do(q, fn, out, ins, args, **kw):
+        order(q, ins, out, q, cnt[q] + 1)
+        cnt[q] += 1
+        fn(out[0], *args, **kw).then_inc(T.sem["s" + q], 1)
+
+    def dma(q, ev, n, out, in_, **kw):
+        order(q, [in_], out, ev, n)
+        QS[q].dma_start(out[0], in_[0], **kw).then_inc(T.sem[ev], 16)
+
+    def vc(out, a): do("V", g.vector.tensor_copy, out, [a], (a[0],))
+    def tt(out, a, b, op): do("V", g.vector.tensor_tensor, out, [a, b], (a[0], b[0], op))
+    def ts(out, a, s1, op0, s2=None, op1=None):
+        col = isinstance(s1, tuple)
+        do("V", g.vector.tensor_scalar, out, [a, s1] if col else [a], (a[0], s1[0] if col else s1, s2, op0) + ((op1,) if op1 else ()))
+    def scan(out, d0, d1, op0, op1): do("V", g.vector.tensor_tensor_scan, out, [d0, d1], (d0[0], d1[0], 0.0, op0, op1))
+    def act(out, a, f=Act.Identity, bias=0.0, scale=1.0):
+        col = isinstance(bias, tuple)
+        do("S", g.scalar.activation, out, [a, bias] if col else [a], (a[0], f), bias=bias[0] if col else bias, scale=scale)
+    def mm(out, l, r, st, sp): do("T", g.tensor.matmul, out, [l, r], (l[0], r[0], st, sp))
+    def fill(out, c): do("V", g.vector.memset, out, [], (c,))
+    def iota(name, pattern, base, cm, **kw): do("P", g.iota, v(name), [], (pattern, base, cm), **kw)
+
+    sent = [0]
+
+    def send(what, t, out, in_):
+        dst = T.cores[(rank + 1 + t % 3) % n_ranks]
+        eng = topo.engines(core, dst)[:8]
+        sent[0] += len(eng)
+        order("P", [in_], ext(None), "ls", sent[0])
+        rid, pid, _ = topo.addr(dst)
+        g.remote_dma(out[0], in_[0], T.sem["%s%d" % (what, t + 1)], T.sem.ls, pid, rid, sum(1 << e for e in eng))
+
+    def landed(what, t, name, n):
+        src = T.cores[(rank - 1 - (t - 1) % 3) % n_ranks]
+        hist.setdefault(name, []).append([n * t, n * t + n, 1, "%s%d" % (what, t), len(topo.engines(src, core)[:8]), True])
+
+    dma("D", "ld0", 16, w("PR", 0, 4), ext(T.pcol[:]))
+    dma("D", "ld1", 16, w("PR", 4, 4), ext(T.prow[:]))
+    dma("S", "ld4", 16, v("RM"), ext(T.rmate[:]))
+    dma("D", "ld3", 16, v("CM"), ext(T.cmate[:]))
+    dma("D", "ld2", 16, v("ND"), ext(T.need[:]))
+    dma("D", "ld5", 16, v("FA", ROT, W), ext(T.fig[:, 0:W - ROT]))
+    dma("D", "ld6", 16, v("FA", 0, ROT), ext(T.fig[:, W - ROT:W]))
+
+    iota("PI", [[0, 1]], 0, 1)
+    iota("CI", [[1, 192]], 0, 0)
+    iota("QI", [[-32, 4]], 0, 1)
+    fill(v("RS64"), BIG)
+    iota("IDXR", [[0, 8], [1, 8], [8, 8]], 0, 64, allow_small_or_imprecise_dtypes=True)
+    iota("TI", [[-16, 4], [1, 64]], 0, 0)
+    iota("DI", [[0, 3], [16, 4]], W - 2048, 0)
+    do("P", g.affine_select, v("RS64"), [v("RS64")], (T.RS64[:], [[0, 12], [1, 64]], Op.is_equal, 0.0, 0, 0))
+    for name, c in (("ONE", 1.0), ("XPRE", 17.0), ("JPRE", 1.0), ("MPRE", -2048.0), ("ZER", 0.0), ("S1", 0.0)): fill(v(name), c)
+    fill(v("JPRE", 0, 64, 1, 1), 16.0)
+    fill(v("JPRE", 64, 160, 1, 1), 592.0)
+    c128, SP, GP_, PI = v("CI", 0, 128), v("SPf"), v("GPf"), v("PIf")
+    ts(v("SPi"), v("PI"), 15, Op.bitwise_and)
+    ts(v("GPi"), v("PI"), 4, Op.logical_shift_right)
+    ts(v("MG"), c128, 4, Op.logical_shift_right)
+    ts(v("MS"), v("CI"), 15, Op.bitwise_and)
+    vc(SP, v("SPi")); vc(GP_, v("GPi")); vc(PI, v("PI")); vc(v("QP"), v("QI"))
+    ts(v("BLK"), v("MG"), GP_, Op.is_equal)
+    ts(v("SPQ"), v("CI", 0, 16), SP, Op.is_equal, 2.0, Op.mult)
+    ts(v("DIAG"), v("MS"), SP, Op.is_equal)
+    ts(v("M7"), c128, 7, Op.bitwise_and)
+    ts(v("M1"), c128, 1, Op.bitwise_and)
+    for s in range(8): ts(w("SEL", 128 * s, 128), v("BLK"), w("SPQ", s, 1), Op.mult)
+    ts(v("cX"), SP, 8.0, Op.is_ge, 100.0, Op.mult)
+    ts(w("SPm", 1, 1), SP, -8.0, Op.add)
+    tt(w("SPm", 0, 1), SP, v("cX"), Op.add)
+    ts(v("ID"), c128, PI, Op.is_equal)
+    ts(v("I2"), c128, PI, Op.is_equal, 2.0, Op.mult)
+    ts(w("I2h", 0, 128), w("MS", 0, 128), 8.0, Op.is_lt)
+    ts(w("I2h", 128, 128), w("MS", 0, 128), 8.0, Op.is_ge)
+    for p in range(2):
+        ts(w("TMP", 128 * p, 128), v("M7"), w("SPm", p, 1), Op.is_equal, 2.0, Op.mult)
+        ts(w("TMP", 256 + 128 * p, 128), w("MS", 0, 128), w("SPm", p, 1), Op.is_equal)
+        tt(w("TMP", 128 * p, 128), w("TMP", 128 * p, 128), v("BLK"), Op.mult)
+        tt(w("M2S", 128 * p, 128), w("TMP", 256 + 128 * p, 128), v("BLK"), Op.mult)
+        for h in range(2): tt(w("DUP", 256 * p + 128 * h, 128), w("TMP", 128 * p, 128), w("I2h", 128 * h, 128), Op.mult)
+    for h in range(2): tt(w("I2h", 128 * h, 128), w("I2h", 128 * h, 128), v("I2"), Op.mult)
+    for h, name in ((0, "EI"), (1, "EJ")):
+        ts(w("TMP", 128 * h, 128), w("MS", 0, 128), 8.0 + h, Op.is_equal)
+        tt(v(name), w("TMP", 128 * h, 128), v("ID"), Op.mult)
+    ts(v("M8"), w("CI", 0, 64), 3, Op.logical_shift_right)
+    ts(v("MH"), v("CI", 0, 128, 1, 64), 1, Op.logical_shift_right)
+    p64 = v("PIf", 0, 1, 1, 64)
+    ts(v("EXp"), v("MH"), p64, Op.is_equal, 64.0, Op.mult)
+    ts(v("EXf"), v("MH"), p64, Op.is_equal, BAD, Op.mult)
+    ts(v("INDF"), v("M8"), GP_, Op.is_equal, BAD, Op.mult)
+    ts(v("INDP"), v("M8"), GP_, Op.is_equal, 64.0, Op.mult)
+    ts(v("IND1"), v("M8"), GP_, Op.is_equal)
+    ts(v("LIDX"), v("M1", 0, 128, 1, 2), v("PIf", 0, 1, 1, 2), Op.is_equal)
+    vc(w("LL", 0, 8), v("PR"))
+    vc(v("PRf"), v("PR"))
+    for q in range(8): ts(w("IJD", 16 * q, 16), w("DIAG", 0, 16), w("PRf", q, 1), Op.mult)
+    mm(w("UW", 0, 128), v("BLK"), v("IJD"), True, True)
+    ts(w("MM", 0, 64), v("ND"), 128.0, Op.add)
+    for q in range(4): ts(w("E8", 128 * q, 128), v("MG"), w("QP", q, 1), Op.is_equal)
+    vc(w("IJ", 0, 128), w("UW", 0, 128))
+    ts(v("RS16"), v("MS"), 0.0, Op.is_gt)
+    ts(v("RS2"), w("M1", 0, 32), 0.0, Op.is_equal, BAD, Op.mult)
+    ts(v("ownA"), SP, 8.0, Op.mult)
+    ts(v("ownT"), SP, 8.0, Op.is_ge, 2 * BAD, Op.mult)
+    ts(v("cW"), SP, 8.0, Op.is_le)
+    tt(v("ownB"), SP, v("ownT"), Op.add)
+    ts(v("cJ"), SP, 9.0, Op.is_equal)
+    ts(v("ownB"), v("ownB"), BAD, Op.min)
+    ts(v("SELW"), v("BLK"), v("cW"), Op.mult)
+    ts(v("SELJ"), v("BLK"), v("cJ"), Op.mult)
+    ts(v("BLKo"), v("BLK"), OUT / 16, Op.mult)
+
+    def late_constants():
+        ts(v("TRI"), v("TI"), SP, Op.is_ge, 32768.0, Op.mult)
+        ts(v("DUM"), v("DI"), SP, Op.add)
+        for s in range(8, 16): ts(w("SEL", 128 * s, 128), v("BLK"), w("SPQ", s, 1), Op.mult)
+        for q in range(4): ts(w("SY", 8 * q, 8), v("CI", 0, 8), w("QP", q, 1), Op.is_equal)
+
+    one1 = v("ONE", 0, 128, 1, 1)
+    BANKS = ("XB0", "XB1", "KT")
+    for t in range(RO):
+        par, last = t % 2, t == RO - 1
+        jw, iw = w("IJ", 128 * t, 64), w("IJ", 128 * t + 64, 64)
+        need = w("MM", 64 * t, 64)
+        if t:
+            landed("l", t, "LL", 8); landed("i", t, "IJ", 128); landed("n", t, "MM", 64)
+
+        for h in range(2): mm(w("XB%d" % h, 0, 256), one1, v("XPRE"), True, False)
+        vc(v("Xf"), ix("CM", 2048, w("LL", 8 * t, 4)))
+        ts(v("Yp"), ix("RM", 1536, w("LL", 8 * t + 4, 4)), 2.0, Op.mult, 593.0, Op.add)
+        for b in range(8): mm(w("XB%d" % (b // 4), 64 * (b % 4), 64), w("SEL", 128 * (8 * par + b), 128), v("Xf"), False, b % 4 == 3)
+
+        def prod(b): tt(w("Pc", 64 * b, 64), w("XB%d" % (b // 4), 64 * (b % 4), 64), v("Yp"), Op.mult)
+        def shift(lo, hi): ts(v("Pi", lo, hi), v("Pc", lo, hi), 5, Op.logical_shift_right, W - 1, Op.bitwise_and)
+        def conv(lo, hi): vc(v("OF", lo, hi), v("Pi", lo, hi))
+
+        for b in range(4): prod(b)
+        shift(0, 128)
+        for b in range(4, 8): prod(b)
+        conv(0, 128)
+        shift(128, 512)
+        conv(128, 512)
+        mm(w("JI", 0, 160), v("ONE"), v("JPRE"), True, False)
+        mm(w("KT", 0, 32), one1, v("XPRE", 0, 32), True, False)
+        mm(key(T.KEY[:]), v("LIDX"), v("IDXR"), True, False)
+        for h in range(2): mm(w("KT", 0, 32), w("DUP", 256 * par + 128 * h, 128), v("Xf", h, 64, 2), False, h == 1)
+        mm(w("MB", 320, 64), w("M2S", 128 * par, 128), v("Xf"), True, False)
+        mm(w("JI", 0, 64), v("I2"), iw, False, False)
+        mm(w("JI", 64, 64), v("I2"), jw, False, False)
+        for h in range(2): mm(w("JI", 128, 32), w("I2h", 128 * h, 128), v("IJ", 128 * t + h, 128 * t + 64, 2), False, h == 1)
+        mm(w("MB", 320, 64), v("EI"), iw, False, False)
+        mm(w("MB", 320, 64), v("EJ"), jw, False, True)
+        for a in range(16): act(v("NR", a, 1024, 16), need, bias=-128.0)
+        act(w("FA", W, P), need, scale=2.0, bias=-255.0)
+
+        def pos(lo, hi):
+            out, off = (v("GP2"), v("OF", 576, 608)) if lo == 9 else (v("GP", 1024 * lo, 1024 * hi), v("OF", 64 * lo, 64 * hi))
+            act(out, ix("PP" if t else "FA", W, off), scale=1.0 if t else 2.0)
+        def fails(b):
+            if b == 9: tt(v("GF2"), ix("FA", W, v("OF", 576, 608)), v("NR", 0, 1024, 2), Op.is_lt)
+            else: tt(w("GF", 1024 * b, 1024), ix("FA", W, w("OF", 64 * b, 64)), v("NR"), Op.is_lt)
+        def keys(which):
+            for b in which:
+                for n, bank in (("P", "UW"), ("F", "TAB")):
+                    for c in range(8):
+                        if b < 8:
+                            mm(key(T.KEY[:, :, 8 * b + c]), v("G" + n, 1024 * b + c, 1024 * b + 1024, 8), v("IND" + n, 0, 64, 8), False, (n, b, c) == ("F", 7, 7))
+                        elif b == 8:
+                            mm(key(T.KEY[:, :, c:64:8]), v("G" + n, 8192 + c, 9216, 8), v("IND" + n), False, False)
+                        else:
+                            mm(v(bank, 256 + c, 320, 8, 64), v("G" + n + "2", c, 512, 8), v("IND1", 0, 64, 8), True, True)
+
+        pos(0, 1); pos(1, 2)
+        act(v("Y2"), w("JI", 128, 32))
+        fails(0); fails(1)
+        tt(w("Pc", 512, 64), w("JI", 0, 64), v("Yp"), Op.mult)
+        tt(w("Pc", 576, 32), w("KT", 0, 32), v("Y2"), Op.mult)
+        shift(512, 608)
+        conv(512, 608)
+        pos(2, 3); pos(8, 9); pos(9, 10); pos(3, 5)
+        for b in (2, 8, 9, 3): fails(b)
+        keys((0, 1, 2, 8, 9, 3))
+        act(v("C2f"), v("TAB", 256, 320, 1, 64))
+        vc(v("C2p"), v("UW", 256, 320, 1, 64))
+        pos(5, 7); pos(7, 8)
+        for b in (4, 5, 6, 7): fails(b)
+        for c in range(8):
+            mm(key(T.KEY[:, :, c:64:8]), v("EXp"), v("C2p"), False, False)
+            mm(key(T.KEY[:, :, c:64:8]), v("EXf"), v("C2f"), False, False)
+        keys((4, 5, 6, 7))
+        act(w("YM", 0, 64), v("Yp"), bias=-296.5, scale=0.5)
+        act(w("YM", 64, 64), w("MB", 320, 64))
+        mm(w("MB", 0, 192), one1, v("MPRE"), True, False)
+        if t == 0: act(v("PP", 0, W), v("FA", 0, W), scale=2.0)
+
+        for k in range(8): do("V", g.vector.tensor_reduce, w("S1", k, 1), [key(None)], (T.KEY[:, k, :], AxisListType.X, Op.min))
+        do("V", g.vector.transpose, v("ST"), [v("S1")], (T.S1[:],))
+        scan(w("KM", 32 * t, 32), v("RS2"), v("ST"), Op.max, Op.min)
+        km = v("KM", 32 * t + 1, 32 * t + 32, 2)
+        ts(v("T32", 0, 32, 2), km, 0x7FF00078, Op.bitwise_and)
+        ts(v("T32", 1, 32, 2), km, 0x7FF00007, Op.bitwise_and)
+        vc(v("TBf"), v("T32"))
+        for q in range(4): mm(w("TAB", 32 * q, 32), w("E8", 128 * q, 128), v("TBf"), True, True)
+        ts(w("KT", 256, 64), v("TAB", 0, 128, 2), v("ownA"), Op.is_equal)
+        ts(w("KT", 320, 64), v("TAB", 1, 128, 2), v("ownB"), Op.is_equal)
+        ts(v("B01"), v("TAB", 1, 128, 2), BAD, Op.is_ge)
+        tt(v("UAW"), w("KT", 256, 128), v("YM"), Op.mult)
+        def names(bank, o):
+            mm(w(bank, o, 64), v("BLK"), w("UAW", 0, 64), True, False)
+            mm(w(bank, o, 64), v("SELJ"), w("UAW", 64, 64), False, True)
+            mm(w(bank, o + 64, 64), v("SELW"), w("UAW", 64, 64), True, True)
+        names("UW", 0)
+        for k in range(3): mm(w("MB", 64 * k, 64), v("BLKo"), v("B01"), False, k == 2)
+        names("MB", 192)
+        if t == 0: late_constants()
+        for bank in BANKS: mm(w(bank, 0, 256), v("ID"), v("TRI"), True, False)
+        tt(v("LD"), w("UW", 0, 128), w("DIAG", 0, 128), Op.mult)
+        scan(v("LSc"), w("RS16", 0, 128), v("LD"), Op.mult, Op.add)
+        vc(w("LS", 8 * t, 8), v("LSc", 15, 128, 16))
+        send("l", t, w("LL", 8 * t + 8, 8), w("LS", 8 * t, 8))
+
+        act(w("UWs", 0, 64), w("MB", 192, 64), scale=2.0, bias=593.0)
+        act(w("UWs", 64, 64), w("MB", 256, 64), scale=2.0, bias=17.0)
+        def f_col(k): ts(w("FI", 64 * k, 64), w("PF", 64 * k, 64), 5, Op.logical_shift_right, W - 1, Op.bitwise_and)
+        def f_out(k): tt(w("TAB", 192 + 64 * k, 64), w("FI", 64 * k, 64), w("MB", 64 * k, 64), Op.add)
+        def f_own(k): tt(w("VD", 64 * k, 64), w("TAB", 192 + 64 * k, 64), w("DIAG", 0, 64), Op.mult)
+        def f_list(k): scan(w("SL", 64 * k, 64), w("RS16", 0, 64), w("VD", 64 * k, 64), Op.mult, Op.add)
+
+        def compare(k):
+            for q in range(4): mm(w(BANKS[k], 64 * q, 64), v("BLK"), w("VD", 64 * k, 64), False, q == 3)
+            for q in range(4):
+                c = 4 * k + q
+                act(w("AB", 64 * c, 64), w(BANKS[k], 64 * q, 64), Act.Abs, scale=-1.0, bias=w("SL", 16 * c + 15, 1))
+
+        def need1(): tt(v("TN"), v("SL", 15, 64, 16), w("DUM", 0, 4), Op.min)
+        def need2(): ts(v("TNu"), v("TN"), 2048.0, Op.add)
+        def need3():
+            ts(w("NS", 64 * t, 64), ix("FA", W + P, v("TNu")), 0.5, Op.mult, 127.75, Op.add)
+            send("n", t, w("MM", 64 * t + 64, 64), w("NS", 64 * t, 64))
+
+        tt(w("PF", 0, 64), w("UWs", 0, 64), w("UWs", 64, 64), Op.mult)
+        tt(w("PF", 64, 128), v("UWs"), w("JI", 0, 128), Op.mult)
+        f_col(0); f_col(1); f_out(0); f_col(2); f_own(0); f_out(1); f_list(0); f_own(1)
+        compare(0)
+        if not last: need1()
+        f_list(1)
+        compare(1)
+        if not last: need2()
+        f_out(2)
+        if not last: need3()
+        f_own(2); f_list(2)
+        compare(2)
+
+        if not last:
+            vc(w("IS", 128 * t, 128), w("UW", 0, 128))
+            send("i", t, w("IJ", 128 * t + 128, 128), w("IS", 128 * t, 128))
+            act(w("NA", 1024 * t, 1024), w("FA", 1024 * t, 1024), scale=-1.0)
+        for lo, n in ((0, 512), (512, 256)): scan(w("MN", lo, n), w("RS64", lo, n), w("AB", lo, n), Op.max, Op.min)
+        ts(v("DU"), v("MN", 63, 768, 64), 0.0, Op.is_equal, OUT, Op.mult)
+        tt(v("DV"), v("DU"), v("SL", 15, 192, 16), Op.add)
+        tt(v("DW"), v("DV"), v("DUM"), Op.min)
+        ts(v("TS"), v("DW"), 2048.0, Op.add)
+        for k in range(3): vc(ix("PP", W + P, w("TS", 4 * k, 4)), v("ZER"))
+        y1, y2 = ext(T.yf[:, 0:W - ROT], "yf1"), ext(T.yf[:, W - ROT:W], "yf2")
+        if t == RO - 2:
+            dma("P", "gd", 32, y1, v("NA", ROT, W))
+            dma("P", "gd", 32, y2, v("NA", 0, ROT))
+        if last:
+            dma("P", "gd2", 32, y1, v("PP", ROT, W), accum_op=Op.add, max_dma_last_dim=4096)
+            dma("P", "gd2", 32, y2, v("PP", 0, ROT), accum_op=Op.add, max_dma_last_dim=4096)
+            need1(); need2(); need3()
+
+    ts(v("YI"), v("KM", 1, 160, 2), 7, Op.logical_shift_right)
+    ts(v("YT"), v("YI"), 8192.0, Op.is_ge, -8193.0, Op.mult)
+    tt(v("YC"), v("YI"), v("YT"), Op.add)
+    for q in range(4):
+        mm(v("KT", 80 * q, 80 * q + 80, 1, 8), w("SY", 8 * q, 8), v("YC"), True, True)
+    for q in range(4): do("V", g.vector.tensor_copy, (T.YO[:, q, :], [("YO", q, q + 1, 1)]), [v("KT", 80 * q, 80 * q + 80, 1, 8)], (T.KT[0:8, 80 * q:80 * q + 80],))
+    for t in range(RO): dma("D", "out", 112, ext(T.yc[:, 64 * t:64 * t + 64], "yc%d" % t), (T.YO[:, :, 16 * t:16 * t + 16], [("YO", 0, 4, 1)]))
+    landed("l", RO, "LL", 8); landed("n", RO, "MM", 64)
+    vc(w("YPo", 0, 4), w("LL", 44, 4))
+    vc(w("YPo", 4, 4), w("LL", 40, 4))
+    ts(v("YZo"), w("MM", 320, 64), -128.0, Op.add)
+    dma("D", "out", 112, ext(T.yp[:], "yp"), v("YPo"))
+    dma("D", "out", 112, ext(T.yz[:], "yz"), v("YZo"))
+    wait("P", "ls", sent[0])
+    wait("P", "gd2", 32)
+    wait("D", "out", 112)
+    for q in "VSTP": wait("D", q, cnt[q])

@@ -1,10 +1,12 @@
-from concourse.mybir import AluOpType as Op, AxisListType, ActivationFunctionType as Act
+from concourse.mybir import AluOpType as Op, ActivationFunctionType as Act
 
 W, P, RO = 4096, 64, 5
 ROT = 315
-BAD = float(1 << 20)
+PAD = 288
 BIG = float(1 << 27)
-OUT = 16384.0
+UNIT = 2.0 ** -13
+MASK = 3 | 15 << 9
+NV = (4, 4, 4, 5)
 SCRATCH = {}
 
 
@@ -14,16 +16,18 @@ def _bufs(dtype, text, where="sbuf"):
         SCRATCH[f[0]] = (where, [int(f[2]) if len(f) > 2 else 128, int(f[1])], dtype)
 
 
-_bufs("bfloat16", "GF2 512, GP2 512, C2f 64 64, EXf 128 64, FA 4160, PP 4160, NA 4096, ND 64, MM 384, NS 320, NR 1024, GF 9216, GP 9216, AB 768, MN 768, ZER 64, YZo 64")
-_bufs("bfloat16", "TBf 32, E8 512, LIDX 128 2, IDXR 512 2, INDF 64, INDP 64, IND1 64, DIAG 192, RS16 192, RS64 768, ONE 128 2, XPRE 256 1, JPRE 160 2, MPRE 192 1")
-_bufs("int32", "RM 1536, CM 2048, PR 8, PI 1, QI 4, CI 192, TI 256, DI 12, GPi 1, SPi 1, MG 128, MS 192, M7 128, M1 128, MH 128 64, M8 64, Pc 608, Pi 608, KM 160, T32 32, PF 192, FI 192, YI 80")
-_bufs("uint16", "LL 48, LS 40, OF 608, TNu 4, TS 12")
-_bufs("float16", "C2p 64 64, EXp 128 64, IJ 768, IS 640, IJD 128, BLK 128, BLKo 128, SEL 2048, DUP 512, M2S 256, TMP 512, ID 128, I2 128, I2h 256, EI 128, EJ 128, SELW 128, SELJ 128, TRI 256, Xf 64, UAW 128, B01 64, VD 192")
-_bufs("float32", "PRf 8, GPf 1, SPf 1, PIf 1, QP 4, SPQ 16, SPm 2, SY 32, cX 1, cW 1, cJ 1, ownA 1, ownB 1, ownT 1, RS2 32, DUM 12, Yp 64, YM 128, Y2 32, S1 32, ST 32, LD 128, LSc 128, UWs 128, SL 192, TN 4, DU 12, DV 12, DW 12, YT 80, YC 80, YPo 8")
-_bufs("float32", "XB0 512, XB1 512, JI 512, MB 512, KT 512, TAB 512, UW 512, KEY 512", "psum")
-SCRATCH["KEY"] = ("psum", [128, 8, 64], "float32")
-SCRATCH["YO"] = ("sbuf", [8, 4, 80], "float32")
-SEMAPHORES = ["sV", "sS", "sT", "sP", "ls", "out", "gd", "gd2"] + ["ld%d" % k for k in range(7)] + ["%s%d" % (m, t) for m in "lin" for t in range(1, RO + 1)]
+_bufs("bfloat16", "FA 4176, YF 4176, ND 64, MM 384, NS 320, AV 192, EQ 192, HALF 16, NEG 16, YZo 64, TBf 32, E8 512, OWN 128, CNT 128 1")
+_bufs("bfloat16", "L3 128 3, IDK 512 3, RSM 256, ONE 128 2, XPRE 256 1, JPRE 192 2, DM 2048, EX 512 64")
+_bufs("bfloat16", "CI 128, CG 128, C1 128, C2 128, MS 256, MG 128, MG4 128, M7 128")
+_bufs("int32", "RM 1536, CM 2336, PR 8, PI 1, GPi 1, SPi 1, OPi 1, Pc 608, Pi 608, II 256, MI 256, PF 12, FI 12")
+_bufs("uint16", "LL 48, LS 40, OF 608, TNu 12, TS 24, KL 64")
+_bufs("float16", "G 8192, G1 1024, G2 512, NR 1024, CD 160, W16 16, WZ 128, IJ 768, IS 640, PRh 8, SEL 2048, DUP 512, M2S 256")
+_bufs("float16", "ID 128, I2 128, I2h 256, EI 128, EJ 128, BLK2 128, SELW 128, SELJ 128, SELP 128, CK 64, NDG 320, TRI 192, Xf 64, YM 128, UAW 128, TNh 12")
+_bufs("float32", "RC 32, GPf 1, SPf 1, QP 4, SY 32, cW 1, cI 1, cJ 2, c0 1, cS 1, cN 2, cH 1, cP 1, cL 2, cK 3, cO 1, ownA 2, ownB 3")
+_bufs("float32", "NB 64, Yp 64, RS8 128, Y2 32, UU 256, KK 512, SC 512, ST 128, KF 384, ZS 256, FS 192, RT 192, FL 192, YI 80, YT 80, YC 80, YPo 8, YO 320 8")
+_bufs("float32", "XB0 512, XB1 512, JI 512, D 512", "psum")
+for _b in ("K0", "K1", "K2", "CB"): SCRATCH[_b] = ("psum", [128, 32, 16], "float32")
+SEMAPHORES = ["sV", "sS", "sT", "sP", "ls", "out"] + ["ld%d" % k for k in range(9)] + ["%s%d" % (m, t) for m in "lin" for t in range(1, RO + 1)]
 
 
 def rank_program(g, core, T, topo):
@@ -38,11 +42,14 @@ def rank_program(g, core, T, topo):
     hist = {}
 
     def v(name, lo=0, hi=None, st=1, r=None):
+        if len(SCRATCH[name][1]) == 3:
+            ap = T[name][0:r or 128, lo // 16:(hi + 15) // 16:st // 16, lo % 16] if st % 16 == 0 else T[name][0:r or 128, lo // 16:hi // 16, lo % 16:16:st]
+            return ap, [(name, lo, hi, st)]
         hi = SCRATCH[name][1][1] if hi is None else hi
         return T[name][0:(r or SCRATCH[name][1][0]), lo:hi:st], [(name, lo, hi, st)]
     def w(name, lo, n, st=1): return v(name, lo, lo + n * st, st)
-    def ix(name, hi, lst): return T[name][:, 0:hi].indirect(lst[0]), [(name, 0, hi, 1)] + lst[1]
-    def key(ap): return ap, [("KEY", 0, 512, 1)]
+    def ix(name, hi, lst, lo=0): return T[name][:, lo:hi].indirect(lst[0]), [(name, lo, hi, 1)] + lst[1]
+    def k3(name, r0, r1, rs, c, n, p0=0, p1=128): return T[name][p0:p1, r0:r1:rs, c:c + n], [(name, 0, 512, 1)]
     def ext(ap, name=None): return ap, [(name, 0, 1, 1)] if name else []
 
     def wait(q, ev, n):
@@ -69,7 +76,7 @@ def rank_program(g, core, T, topo):
             hist[name].append([lo, hi, st, ev, n, write])
 
     def do(q, fn, out, ins, args, **kw):
-        order(q, ins, out, q, cnt[q] + 1)
+        order(q, ins + [(None, out[1][1:])], (None, out[1][:1]), q, cnt[q] + 1)
         cnt[q] += 1
         fn(out[0], *args, **kw).then_inc(T.sem["s" + q], 1)
 
@@ -77,18 +84,24 @@ def rank_program(g, core, T, topo):
         order(q, [in_], out, ev, n)
         QS[q].dma_start(out[0], in_[0], **kw).then_inc(T.sem[ev], 16)
 
+    def col(x): return isinstance(x, tuple)
     def vc(out, a): do("V", g.vector.tensor_copy, out, [a], (a[0],))
     def tt(out, a, b, op): do("V", g.vector.tensor_tensor, out, [a, b], (a[0], b[0], op))
     def ts(out, a, s1, op0, s2=None, op1=None):
-        col = isinstance(s1, tuple)
-        do("V", g.vector.tensor_scalar, out, [a, s1] if col else [a], (a[0], s1[0] if col else s1, s2, op0) + ((op1,) if op1 else ()))
+        do("V", g.vector.tensor_scalar, out, [a] + [s for s in (s1, s2) if col(s)],
+           (a[0], s1[0] if col(s1) else s1, s2[0] if col(s2) else s2, op0) + ((op1,) if op1 else ()))
     def scan(out, d0, d1, op0, op1): do("V", g.vector.tensor_tensor_scan, out, [d0, d1], (d0[0], d1[0], 0.0, op0, op1))
     def act(out, a, f=Act.Identity, bias=0.0, scale=1.0):
-        col = isinstance(bias, tuple)
-        do("S", g.scalar.activation, out, [a, bias] if col else [a], (a[0], f), bias=bias[0] if col else bias, scale=scale)
+        do("S", g.scalar.activation, out, [a] + [s for s in (bias, scale) if col(s)], (a[0], f),
+           bias=bias[0] if col(bias) else bias, scale=scale[0] if col(scale) else scale)
     def mm(out, l, r, st, sp): do("T", g.tensor.matmul, out, [l, r], (l[0], r[0], st, sp))
     def fill(out, c): do("V", g.vector.memset, out, [], (c,))
-    def iota(name, pattern, base, cm, **kw): do("P", g.iota, v(name), [], (pattern, base, cm), **kw)
+    def iota(name, pattern, base, cm): do("P", g.iota, v(name), [], (pattern, base, cm), allow_small_or_imprecise_dtypes=True)
+    def pick(name, pattern, op, other, cm): do("P", g.affine_select, v(name), [v(name)], (T[name][:], pattern, op, other, 0, cm))
+    def weave(first, second=()):
+        for n in range(max(len(first), len(second))):
+            for calls in (first, second):
+                if n < len(calls) and calls[n]: calls[n]()
 
     sent = [0]
 
@@ -105,89 +118,95 @@ def rank_program(g, core, T, topo):
         hist.setdefault(name, []).append([n * t, n * t + n, 1, "%s%d" % (what, t), len(topo.engines(src, core)[:8]), True])
 
     dma("D", "ld0", 16, w("PR", 0, 4), ext(T.pcol[:]))
-    dma("D", "ld1", 16, w("PR", 4, 4), ext(T.prow[:]))
-    dma("S", "ld4", 16, v("RM"), ext(T.rmate[:]))
-    dma("D", "ld3", 16, v("CM"), ext(T.cmate[:]))
+    dma("S", "ld1", 16, w("PR", 4, 4), ext(T.prow[:]))
     dma("D", "ld2", 16, v("ND"), ext(T.need[:]))
-    dma("D", "ld5", 16, v("FA", ROT, W), ext(T.fig[:, 0:W - ROT]))
-    dma("D", "ld6", 16, v("FA", 0, ROT), ext(T.fig[:, W - ROT:W]))
+    dma("S", "ld3", 16, v("CM", PAD), ext(T.cmate[:]))
+    dma("D", "ld4", 16, v("RM"), ext(T.rmate[:]))
+    for k, name in ((5, "FA"), (7, "YF")):
+        dma("D", "ld%d" % k, 16, v(name, ROT, W), ext(T.fig[:, 0:W - ROT]))
+        dma("D", "ld%d" % (k + 1), 16, v(name, 0, ROT), ext(T.fig[:, W - ROT:W]))
 
-    iota("PI", [[0, 1]], 0, 1)
-    iota("CI", [[1, 192]], 0, 0)
-    iota("QI", [[-32, 4]], 0, 1)
-    fill(v("RS64"), BIG)
-    iota("IDXR", [[0, 8], [1, 8], [8, 8]], 0, 64, allow_small_or_imprecise_dtypes=True)
-    iota("TI", [[-16, 4], [1, 64]], 0, 0)
-    iota("DI", [[0, 3], [16, 4]], W - 2048, 0)
-    do("P", g.affine_select, v("RS64"), [v("RS64")], (T.RS64[:], [[0, 12], [1, 64]], Op.is_equal, 0.0, 0, 0))
-    for name, c in (("ONE", 1.0), ("XPRE", 17.0), ("JPRE", 1.0), ("MPRE", -2048.0), ("ZER", 0.0), ("S1", 0.0)): fill(v(name), c)
-    fill(v("JPRE", 0, 64, 1, 1), 16.0)
-    fill(v("JPRE", 64, 160, 1, 1), 592.0)
-    c128, SP, GP_, PI = v("CI", 0, 128), v("SPf"), v("GPf"), v("PIf")
+    do("P", g.iota, v("PI"), [], ([[0, 1]], 0, 1))
+    iota("RC", [[128, 2], [-1, 16]], 0, 1)
+    iota("CG", [[16, 8], [0, 16]], 0, 0)
+    iota("MG", [[1, 8], [0, 16]], 0, 0)
+    iota("CI", [[1, 128]], 0, 0)
+    iota("MS", [[0, 16], [1, 16]], 0, 0)
+    iota("C1", [[16, 8], [128, 2], [1, 8]], 0, 0)
+    iota("C2", [[16, 8], [136, 2], [1, 8]], 0, 0)
+    iota("M7", [[0, 16], [1, 8]], 0, 0)
+    iota("QP", [[-32, 4]], 0, 1)
+    iota("MG4", [[4, 8], [0, 16]], 3, 0)
+    iota("IDK", [[0, 16], [8, 16], [0, 2]], 0, 8)
+    iota("EX", [[0, 512]], 1, 0)
+    pick("EX", [[1, 64], [0, 8]], Op.is_equal, 0.0, -1)
+    iota("DM", [[0, 2048]], -1, 0)
+    pick("DM", [[-1, 16], [-16, 8], [0, 16]], Op.is_equal, 0.0, 1)
+    pick("DM", [[0, 16], [-16, 8], [-1, 16]], Op.not_equal, 1.0, 1)
+    SP, GP_, PI = v("SPf"), v("GPf"), w("RC", 0, 1)
+    def match(out, pattern, c, k=1.0): return lambda: ts(out, pattern, c, Op.is_equal, k, Op.mult)
+    rows = [match(v("E8", 128 * q + h, 128 * q + 128, 2), v("MG4", h, 128, 2), w("QP", q, 1), (1 - 2 * h) * 2.0 ** 34) for q in range(4) for h in range(2)]
+    def twice(p):
+        return [match(w("DUP", 256 * p + 128 * h, 128), v("C1"), w("RC", 16 * h + 8 * p, 1), 2.0) for h in range(2)] + [
+            match(w("M2S", 128 * p, 128), v("C2"), w("RC", 8 * p, 1))]
+    for name, c in (("ONE", 1.0), ("XPRE", 17.0), ("JPRE", 1.0)): fill(v(name), c)
     ts(v("SPi"), v("PI"), 15, Op.bitwise_and)
     ts(v("GPi"), v("PI"), 4, Op.logical_shift_right)
-    ts(v("MG"), c128, 4, Op.logical_shift_right)
-    ts(v("MS"), v("CI"), 15, Op.bitwise_and)
-    vc(SP, v("SPi")); vc(GP_, v("GPi")); vc(PI, v("PI")); vc(v("QP"), v("QI"))
-    ts(v("BLK"), v("MG"), GP_, Op.is_equal)
-    ts(v("SPQ"), v("CI", 0, 16), SP, Op.is_equal, 2.0, Op.mult)
-    ts(v("DIAG"), v("MS"), SP, Op.is_equal)
-    ts(v("M7"), c128, 7, Op.bitwise_and)
-    ts(v("M1"), c128, 1, Op.bitwise_and)
-    for s in range(8): ts(w("SEL", 128 * s, 128), v("BLK"), w("SPQ", s, 1), Op.mult)
-    ts(v("cX"), SP, 8.0, Op.is_ge, 100.0, Op.mult)
-    ts(w("SPm", 1, 1), SP, -8.0, Op.add)
-    tt(w("SPm", 0, 1), SP, v("cX"), Op.add)
-    ts(v("ID"), c128, PI, Op.is_equal)
-    ts(v("I2"), c128, PI, Op.is_equal, 2.0, Op.mult)
-    ts(w("I2h", 0, 128), w("MS", 0, 128), 8.0, Op.is_lt)
-    ts(w("I2h", 128, 128), w("MS", 0, 128), 8.0, Op.is_ge)
-    for p in range(2):
-        ts(w("TMP", 128 * p, 128), v("M7"), w("SPm", p, 1), Op.is_equal, 2.0, Op.mult)
-        ts(w("TMP", 256 + 128 * p, 128), w("MS", 0, 128), w("SPm", p, 1), Op.is_equal)
-        tt(w("TMP", 128 * p, 128), w("TMP", 128 * p, 128), v("BLK"), Op.mult)
-        tt(w("M2S", 128 * p, 128), w("TMP", 256 + 128 * p, 128), v("BLK"), Op.mult)
-        for h in range(2): tt(w("DUP", 256 * p + 128 * h, 128), w("TMP", 128 * p, 128), w("I2h", 128 * h, 128), Op.mult)
-    for h in range(2): tt(w("I2h", 128 * h, 128), w("I2h", 128 * h, 128), v("I2"), Op.mult)
-    for h, name in ((0, "EI"), (1, "EJ")):
-        ts(w("TMP", 128 * h, 128), w("MS", 0, 128), 8.0 + h, Op.is_equal)
-        tt(v(name), w("TMP", 128 * h, 128), v("ID"), Op.mult)
-    ts(v("M8"), w("CI", 0, 64), 3, Op.logical_shift_right)
-    ts(v("MH"), v("CI", 0, 128, 1, 64), 1, Op.logical_shift_right)
-    p64 = v("PIf", 0, 1, 1, 64)
-    ts(v("EXp"), v("MH"), p64, Op.is_equal, 64.0, Op.mult)
-    ts(v("EXf"), v("MH"), p64, Op.is_equal, BAD, Op.mult)
-    ts(v("INDF"), v("M8"), GP_, Op.is_equal, BAD, Op.mult)
-    ts(v("INDP"), v("M8"), GP_, Op.is_equal, 64.0, Op.mult)
-    ts(v("IND1"), v("M8"), GP_, Op.is_equal)
-    ts(v("LIDX"), v("M1", 0, 128, 1, 2), v("PIf", 0, 1, 1, 2), Op.is_equal)
-    vc(w("LL", 0, 8), v("PR"))
-    vc(v("PRf"), v("PR"))
-    for q in range(8): ts(w("IJD", 16 * q, 16), w("DIAG", 0, 16), w("PRf", q, 1), Op.mult)
-    mm(w("UW", 0, 128), v("BLK"), v("IJD"), True, True)
-    ts(w("MM", 0, 64), v("ND"), 128.0, Op.add)
-    for q in range(4): ts(w("E8", 128 * q, 128), v("MG"), w("QP", q, 1), Op.is_equal)
-    vc(w("IJ", 0, 128), w("UW", 0, 128))
-    ts(v("RS16"), v("MS"), 0.0, Op.is_gt)
-    ts(v("RS2"), w("M1", 0, 32), 0.0, Op.is_equal, BAD, Op.mult)
-    ts(v("ownA"), SP, 8.0, Op.mult)
-    ts(v("ownT"), SP, 8.0, Op.is_ge, 2 * BAD, Op.mult)
-    ts(v("cW"), SP, 8.0, Op.is_le)
-    tt(v("ownB"), SP, v("ownT"), Op.add)
-    ts(v("cJ"), SP, 9.0, Op.is_equal)
-    ts(v("ownB"), v("ownB"), BAD, Op.min)
-    ts(v("SELW"), v("BLK"), v("cW"), Op.mult)
-    ts(v("SELJ"), v("BLK"), v("cJ"), Op.mult)
-    ts(v("BLKo"), v("BLK"), OUT / 16, Op.mult)
+    fill(v("JPRE", 0, 128, 1, 1), 16.0)
+    fill(v("JPRE", 128, 192), 0.0)
+    ts(v("OPi"), v("PI"), 1, Op.bitwise_and)
+    vc(SP, v("SPi")); vc(GP_, v("GPi"))
+    ts(v("cO"), v("OPi"), -2.0, Op.mult, 1.0, Op.add)
+    fill(v("JPRE", 64, 96, 1, 1), 592.0)
+    fill(v("CM", 0, PAD), 0)
+    for s in range(16): match(w("SEL", 128 * s, 128), v("CG"), w("RC", s, 1), 2.0)()
+    ts(w("LL", 0, 4), w("PR", 0, 4), float(PAD), Op.add)
+    vc(w("LL", 4, 4), w("PR", 4, 4))
+    vc(v("PRh"), v("PR"))
+    for s in range(16): mm(v("D", s, 128, 16), w("SEL", 128 * s, 128), v("PRh"), True, True)
+    ts(v("c0"), SP, 0.0, Op.is_equal)
+    ts(v("cI"), SP, 8.0, Op.is_equal)
+    for h in range(2): match(w("cJ", h, 1), SP, 10.0, 1.0 + h)()
+    for h in range(2): ts(w("cK", h, 1), SP, 12.0 + 2 * h, Op.is_equal)
+    ts(w("ownB", 0, 1), SP, 8.0, Op.min, -4096.0, Op.mult)
+    ts(v("cW"), SP, 8.0, Op.is_le, 2.0, Op.mult)
+    for out, a, k, c in ((w("cN", 0, 1), v("c0"), 0.1875, 128.0625), (w("cN", 1, 1), v("c0"), -0.1875, -128.0625), (v("cS"), v("c0"), 8188.0, -8192.0),
+                         (w("cL", 0, 1), PI, 2.0 ** -24, -1.5 * 2.0 ** -24), (w("cL", 1, 1), PI, -312.0 * 2.0 ** -25, 476.0 * 2.0 ** -25),
+                         (v("cH"), v("c0"), 0.5, 0.0), (w("ownA", 0, 1), SP, -65536.0, 8 * 65536.0), (w("ownB", 1, 1), w("ownB", 0, 1), 1.0, 16384.0),
+                         (v("cP"), SP, 1.0, W + 64.0), (w("cK", 2, 1), w("cK", 0, 1), float(W), w("cK", 1, 1)),
+                         (w("ownA", 1, 1), w("ownA", 0, 1), v("cO"), 0.0), (w("ownB", 2, 1), w("ownB", 1, 1), v("cO"), 0.0),
+                         (v("CK"), w("CI", 0, 64), w("cK", 1, 1), w("cK", 0, 1)),
+                         (v("L3"), v("M7", 0, 128, 1, 3), v("cL", 0, 1, 1, 3), v("cL", 1, 2, 1, 3)),
+                         (v("RSM"), v("MS"), -BIG, BIG / 2), (v("RS8"), v("M7"), -BIG, 1 + 2.0 ** -15 + 2.0 ** -20),
+                         (w("OWN", 0, 64), w("CI", 0, 64), 0.0, w("ownB", 2, 1)), (w("OWN", 64, 64), w("CI", 0, 64), 0.0, w("ownA", 1, 1)),
+                         (v("HALF"), w("CI", 0, 16), 0.0, v("cH"))):
+        act(out, a, scale=k, bias=c)
+    vc(v("KL"), w("CI", 0, 64))
+    for name, c in (("ID", 1.0), ("I2", 2.0), ("EI", v("cI")), ("EJ", w("cJ", 0, 1))): match(v(name), v("CI"), PI, c)()
+    match(v("WZ"), v("MG"), GP_, UNIT)()
+    match(v("W16", 0, 16, 2), w("CI", 0, 8), GP_, v("cS"))()
+    match(v("W16", 1, 16, 2), w("CI", 0, 8), GP_, UNIT)()
+    weave(twice(0), [match(w("I2h", 128 * h, 128), v("C2"), w("RC", 16 * h, 1), 2.0) for h in range(2)])
+    act(w("MM", 0, 64), v("ND"), bias=128.0)
+    act(w("IJ", 0, 128), w("D", 0, 128), scale=0.5)
+    fill(v("IDK", 0, 512, 2, 1), 0.0)
+    fill(v("IDK", 1, 512, 2, 1), -2.0)
+    fill(v("L3", 0, 128, 1, 1), 1.0)
+    for name, c in (("NEG", -1.0), ("RT", 0.0)): fill(v(name), c)
+    for name in ("FA", "YF"): fill(v(name, W), 1.0)
+    for h in range(2): fill(v("CNT", 64 * h, 64 * h + 64), -65536.0 / (1 + h))
+    fill(v("RT", 0, 192, 16), -BIG)
+    ts(w("NDG", 128, 192), w("MS", 0, 192), SP, Op.not_equal, 16384.0, Op.mult)
+    ts(v("TRI"), w("MS", 0, 192), SP, Op.is_ge, 16384.0, Op.mult)
+    for h, c in ((0, 593.0), (1, 17.0)): ts(w("NDG", 64 * h, 64), w("NDG", 128, 64), c, Op.max)
+    for name, c in (("BLK2", 2.0), ("SELW", v("cW")), ("SELJ", w("cJ", 1, 1)), ("SELP", w("cK", 2, 1))): match(v(name), v("MG"), GP_, c)()
 
-    def late_constants():
-        ts(v("TRI"), v("TI"), SP, Op.is_ge, 32768.0, Op.mult)
-        ts(v("DUM"), v("DI"), SP, Op.add)
-        for s in range(8, 16): ts(w("SEL", 128 * s, 128), v("BLK"), w("SPQ", s, 1), Op.mult)
-        for q in range(4): ts(w("SY", 8 * q, 8), v("CI", 0, 8), w("QP", q, 1), Op.is_equal)
+    def strikes(name, op, other):
+        return [lambda c=c: tt(ix(name, W + 80, w("TS", 2 * c, 1)), w("AV", 16 * c, 16), v(other), op) for c in range(12)]
 
     one1 = v("ONE", 0, 128, 1, 1)
-    BANKS = ("XB0", "XB1", "KT")
+    TN = v("RT", 15, 192, 16)
+    KB = (("K0", 0), ("K0", 256), ("K1", 0), ("K2", 0))
     for t in range(RO):
         par, last = t % 2, t == RO - 1
         jw, iw = w("IJ", 128 * t, 64), w("IJ", 128 * t + 64, 64)
@@ -196,164 +215,155 @@ def rank_program(g, core, T, topo):
             landed("l", t, "LL", 8); landed("i", t, "IJ", 128); landed("n", t, "MM", 64)
 
         for h in range(2): mm(w("XB%d" % h, 0, 256), one1, v("XPRE"), True, False)
-        vc(v("Xf"), ix("CM", 2048, w("LL", 8 * t, 4)))
-        ts(v("Yp"), ix("RM", 1536, w("LL", 8 * t + 4, 4)), 2.0, Op.mult, 593.0, Op.add)
+        act(v("Xf"), ix("CM", PAD + 2048, w("LL", 8 * t, 4)))
+        act(v("Yp"), ix("RM", 1536, w("LL", 8 * t + 4, 4)), scale=2.0, bias=593.0)
         for b in range(8): mm(w("XB%d" % (b // 4), 64 * (b % 4), 64), w("SEL", 128 * (8 * par + b), 128), v("Xf"), False, b % 4 == 3)
 
-        def prod(b): tt(w("Pc", 64 * b, 64), w("XB%d" % (b // 4), 64 * (b % 4), 64), v("Yp"), Op.mult)
-        def shift(lo, hi): ts(v("Pi", lo, hi), v("Pc", lo, hi), 5, Op.logical_shift_right, W - 1, Op.bitwise_and)
-        def conv(lo, hi): vc(v("OF", lo, hi), v("Pi", lo, hi))
+        def prod(b): return lambda: tt(v("Pc", b, 512, 8), w("XB%d" % (b // 4), 64 * (b % 4), 64), v("Yp"), Op.mult)
+        def shift(lo, hi): return lambda: ts(v("Pi", lo, hi), v("Pc", lo, hi), 5, Op.logical_shift_right, W - 1, Op.bitwise_and)
+        def conv(lo, hi): return lambda: vc(v("OF", lo, hi), v("Pi", lo, hi))
 
-        for b in range(4): prod(b)
-        shift(0, 128)
-        for b in range(4, 8): prod(b)
-        conv(0, 128)
-        shift(128, 512)
-        conv(128, 512)
-        mm(w("JI", 0, 160), v("ONE"), v("JPRE"), True, False)
-        mm(w("KT", 0, 32), one1, v("XPRE", 0, 32), True, False)
-        mm(key(T.KEY[:]), v("LIDX"), v("IDXR"), True, False)
-        for h in range(2): mm(w("KT", 0, 32), w("DUP", 256 * par + 128 * h, 128), v("Xf", h, 64, 2), False, h == 1)
-        mm(w("MB", 320, 64), w("M2S", 128 * par, 128), v("Xf"), True, False)
+        weave(strikes("FA", Op.add, "HALF") if t else [], [None] + [prod(b) for b in range(8)] + [None, shift(0, 128), None, conv(0, 128)])
+        act(v("NB"), need, scale=-1.0, bias=w("cN", 0, 1))
+        act(v("NR"), ix("MM", 64 * t + 64, v("KL"), 64 * t), bias=w("cN", 1, 1))
+        mm(w("JI", 0, 192), v("ONE"), v("JPRE"), True, False)
+        for h in range(2): mm(w("JI", 96, 32), w("DUP", 256 * par + 128 * h, 128), v("Xf", h, 64, 2), False, False)
+        mm(w("JI", 128, 64), w("M2S", 128 * par, 128), v("Xf"), False, False)
+        mm(w("JI", 128, 64), v("ID"), v("CK"), False, False)
         mm(w("JI", 0, 64), v("I2"), iw, False, False)
-        mm(w("JI", 64, 64), v("I2"), jw, False, False)
-        for h in range(2): mm(w("JI", 128, 32), w("I2h", 128 * h, 128), v("IJ", 128 * t + h, 128 * t + 64, 2), False, h == 1)
-        mm(w("MB", 320, 64), v("EI"), iw, False, False)
-        mm(w("MB", 320, 64), v("EJ"), jw, False, True)
-        for a in range(16): act(v("NR", a, 1024, 16), need, bias=-128.0)
+        for h in range(2): mm(w("JI", 64, 32), w("I2h", 128 * h, 128), v("IJ", 128 * t + h, 128 * t + 64, 2), False, False)
+        mm(w("JI", 128, 64), v("EI"), iw, False, False)
+        mm(w("JI", 128, 64), v("EJ"), jw, False, True)
+        act(v("Y2"), w("JI", 64, 32))
+        for bank, n in (("K0", 512), ("K1", 256), ("K2", 256)): mm(w(bank, 0, n), v("L3"), v("IDK", 0, n), True, False)
+        for h in range(2): mm(w("D", 256 * h, 256), v("L3"), v("IDK", 0, 512, 2), h == 0, False)
+        mm(w("CB", 0, 320), one1, v("IDK", 0, 320, 1, 1), True, False)
+
+        def slots(q, eng):
+            n = 14 - NV[q]
+            return [16 * q + k for k in (list(range(n)) + [12, 13] if eng == "S" else list(range(n, 12)) + [14, 15])]
+        def far(q, eng):
+            def one(k):
+                out, src = w("G", 128 * k, 128), ix("FA", W, w("OF", 8 * k, 8))
+                if eng == "S": act(out, src, Act.Relu, bias=w("NB", k, 1))
+                else: ts(out, src, w("NB", k, 1), Op.add, 0.0, Op.max)
+            return [lambda k=k: one(k) for k in slots(q, eng)]
+        def sums(q, sp, lo=0, hi=16):
+            bank, r = KB[q]
+            for a in range(16):
+                mm(k3(bank, r // 16 + a // 8, r // 16 + 16, 2, 2 * a % 16, 2, 8 * lo, 8 * hi),
+                   v("G", 2048 * q + 128 * lo + a, 2048 * q + 128 * hi, 16), v("W16"), False, sp and a == 15)
+        def bits(bank, n, base):
+            return [lambda: ts(w("II", 0, n), v(bank, 0, 2 * n, 2), base, Op.add),
+                    lambda: ts(w("MI", 0, n), w("II", 0, n), MASK, Op.bitwise_and),
+                    lambda: tt(w("UU", 0, n), w("MI", 0, n), v(bank, 1, 2 * n, 2), Op.add)]
+        def keys(bank, q, m):
+            lo, n = 128 * q, 128 * m
+            return bits(bank, n, 8191.0) + [
+                lambda: tt(w("KK", lo, n), w("UU", 0, n), w("D", lo, n), Op.max),
+                lambda: scan(w("SC", lo, n), w("RSM", 0, n), w("KK", lo, n), Op.max, Op.min)]
+        def plus(q, m):
+            low = v("SC", 128 * q + 15, 128 * (q + m), 16)
+            return [lambda: tt(low, low, w("CD", 128 + 8 * q, 8 * m), Op.add)]
+
+        weave(far(0, "S"))
+        weave([shift(128, 512), lambda: tt(w("Pc", 512, 64), w("JI", 0, 64), v("Yp"), Op.mult), conv(128, 512),
+               lambda: tt(w("Pc", 576, 32), w("JI", 96, 32), v("Y2"), Op.mult), shift(512, 608), conv(512, 608)], [None, None, None] + far(0, "V"))
+        tt(v("G1"), ix("FA", W, w("OF", 512, 64)), v("NR"), Op.max)
+        tt(v("G2"), ix("FA", W, w("OF", 576, 32)), v("NR", 0, 1024, 2), Op.max)
+        for q in range(4):
+            mm(v(KB[q][0], KB[q][1] + 1, KB[q][1] + 256, 2), v("NR", 256 * q, 256 * q + 256, 2), v("WZ"), False, False)
+        sums(0, False)
+        for a in range(16): mm(k3("CB", a // 8, 16, 2, 2 * a % 16, 2, 0, 64), v("G1", a, 1024, 16), v("W16"), False, False)
+        for q in range(4): mm(w("CB", 256 + 16 * q, 16), w("G2", 128 * q, 128), v("W16"), False, q == 3)
+        weave(far(1, "S"))
+        weave(far(1, "V"), bits("CB", 160, 510.0) + [lambda: ts(v("CD"), w("UU", 0, 160), 0.0, Op.max)])
+        sums(1, False)
+        c1 = v("CD", 0, 128, 1, 64)
+        for q in range(4):
+            mm(v(KB[q][0], KB[q][1] + 1, KB[q][1] + 256, 2), w("EX", 128 * q, 128), c1, False, q == 1)
+            mm(w("D", 128 * q, 128), w("EX", 128 * q, 128), c1, False, False)
+        for a in range(16):
+            mm(v("D", 384 + a, 512, 16), v("ID"), w("CD", 152, 8), False, a == 15)
+        weave(far(2, "S"))
+        weave(far(2, "V"), [None] + keys("K0", 0, 2) + plus(0, 2))
+        for a in range(16): mm(v("K2", 2 * a + 1, 256, 32), v("ID"), w("CD", 152, 8), False, False)
+        sums(2, True)
+        mm(w("XB0", 0, 128), v("ID"), w("NDG", 0, 128), True, False)
+        mm(w("XB0", 0, 128), one1, v("CNT"), False, False)
+        mm(w("CB", 0, 128), v("ID"), v("OWN"), True, False)
+        mm(w("XB1", 0, 192), v("ID"), v("TRI"), True, False)
+        weave(far(3, "S"))
+        weave(far(3, "V"), keys("K1", 2, 1) + plus(2, 1))
+        sums(3, True, 0, 12)
+        sums(3, True, 12, 16)
+        act(w("YM", 64, 64), v("Yp"), bias=-296.5, scale=0.5)
+        act(w("YM", 0, 64), w("JI", 128, 64))
+        mm(w("CB", 0, 128), v("ID"), v("YM"), False, False)
+        if not last: mm(w("JI", 256, 128), one1, v("CNT"), True, False)
         act(w("FA", W, P), need, scale=2.0, bias=-255.0)
 
-        def pos(lo, hi):
-            out, off = (v("GP2"), v("OF", 576, 608)) if lo == 9 else (v("GP", 1024 * lo, 1024 * hi), v("OF", 64 * lo, 64 * hi))
-            act(out, ix("PP" if t else "FA", W, off), scale=1.0 if t else 2.0)
-        def fails(b):
-            if b == 9: tt(v("GF2"), ix("FA", W, v("OF", 576, 608)), v("NR", 0, 1024, 2), Op.is_lt)
-            else: tt(w("GF", 1024 * b, 1024), ix("FA", W, w("OF", 64 * b, 64)), v("NR"), Op.is_lt)
-        def keys(which):
-            for b in which:
-                for n, bank in (("P", "UW"), ("F", "TAB")):
-                    for c in range(8):
-                        if b < 8:
-                            mm(key(T.KEY[:, :, 8 * b + c]), v("G" + n, 1024 * b + c, 1024 * b + 1024, 8), v("IND" + n, 0, 64, 8), False, (n, b, c) == ("F", 7, 7))
-                        elif b == 8:
-                            mm(key(T.KEY[:, :, c:64:8]), v("G" + n, 8192 + c, 9216, 8), v("IND" + n), False, False)
-                        else:
-                            mm(v(bank, 256 + c, 320, 8, 64), v("G" + n + "2", c, 512, 8), v("IND1", 0, 64, 8), True, True)
-
-        pos(0, 1); pos(1, 2)
-        act(v("Y2"), w("JI", 128, 32))
-        fails(0); fails(1)
-        tt(w("Pc", 512, 64), w("JI", 0, 64), v("Yp"), Op.mult)
-        tt(w("Pc", 576, 32), w("KT", 0, 32), v("Y2"), Op.mult)
-        shift(512, 608)
-        conv(512, 608)
-        pos(2, 3); pos(8, 9); pos(9, 10); pos(3, 5)
-        for b in (2, 8, 9, 3): fails(b)
-        keys((0, 1, 2, 8, 9, 3))
-        act(v("C2f"), v("TAB", 256, 320, 1, 64))
-        vc(v("C2p"), v("UW", 256, 320, 1, 64))
-        pos(5, 7); pos(7, 8)
-        for b in (4, 5, 6, 7): fails(b)
-        for c in range(8):
-            mm(key(T.KEY[:, :, c:64:8]), v("EXp"), v("C2p"), False, False)
-            mm(key(T.KEY[:, :, c:64:8]), v("EXf"), v("C2f"), False, False)
-        keys((4, 5, 6, 7))
-        act(w("YM", 0, 64), v("Yp"), bias=-296.5, scale=0.5)
-        act(w("YM", 64, 64), w("MB", 320, 64))
-        mm(w("MB", 0, 192), one1, v("MPRE"), True, False)
-        if t == 0: act(v("PP", 0, W), v("FA", 0, W), scale=2.0)
-
-        for k in range(8): do("V", g.vector.tensor_reduce, w("S1", k, 1), [key(None)], (T.KEY[:, k, :], AxisListType.X, Op.min))
-        do("V", g.vector.transpose, v("ST"), [v("S1")], (T.S1[:],))
-        scan(w("KM", 32 * t, 32), v("RS2"), v("ST"), Op.max, Op.min)
-        km = v("KM", 32 * t + 1, 32 * t + 32, 2)
-        ts(v("T32", 0, 32, 2), km, 0x7FF00078, Op.bitwise_and)
-        ts(v("T32", 1, 32, 2), km, 0x7FF00007, Op.bitwise_and)
-        vc(v("TBf"), v("T32"))
-        for q in range(4): mm(w("TAB", 32 * q, 32), w("E8", 128 * q, 128), v("TBf"), True, True)
-        ts(w("KT", 256, 64), v("TAB", 0, 128, 2), v("ownA"), Op.is_equal)
-        ts(w("KT", 320, 64), v("TAB", 1, 128, 2), v("ownB"), Op.is_equal)
-        ts(v("B01"), v("TAB", 1, 128, 2), BAD, Op.is_ge)
-        tt(v("UAW"), w("KT", 256, 128), v("YM"), Op.mult)
+        kf = v("KF", 7, 128, 8)
+        def parts():
+            ts(v("KF", 135, 256, 8), kf, 48.0, Op.add, -48.0, Op.add)
+            ts(v("KF", 263, 384, 8), kf, 1536.0, Op.add, -1536.0, Op.add)
+        def spread():
+            mm(w("D", 0, 192), v("ID"), w("NDG", 128, 192), True, False)
+            tt(v("TBf"), v("KF", 7, 256, 8), v("KF", 135, 384, 8), Op.subtract)
+            for q in range(4): mm(k3("CB", 0, 8, 1, 4 * q, 4), w("E8", 128 * q, 128), v("TBf"), False, q == 3)
+        own = [lambda: ts(v("ZS", 15, 64, 16), w("LL", 8 * t + 4, 4), 2.0, Op.mult, 17.0, Op.add),
+               lambda: ts(v("ZS", 207, 256, 16), w("LL", 8 * t, 4), 2.0, Op.mult, 17.0, Op.add)]
+        old = strikes("YF", Op.mult, "NEG") if t else [None] + rows + twice(1)
+        weave(own, old[:1])
+        turn = v("SC", 3, 512, 4)
+        weave(keys("K2", 3, 1) + [lambda: do("V", g.vector.transpose, v("ST"), [turn], (turn[0],)),
+                                  lambda: scan(w("KF", 0, 128), v("RS8"), v("ST"), Op.max, Op.min), parts, spread], old[1:10])
+        act(w("YI", 16 * t, 16), v("KF", 263, 384, 8), scale=8192.0)
+        weave(old[10:11])
+        ts(v("UAW"), w("CB", 0, 128), 0.0, Op.max, 4096.0, Op.min)
         def names(bank, o):
-            mm(w(bank, o, 64), v("BLK"), w("UAW", 0, 64), True, False)
-            mm(w(bank, o, 64), v("SELJ"), w("UAW", 64, 64), False, True)
-            mm(w(bank, o + 64, 64), v("SELW"), w("UAW", 64, 64), True, True)
-        names("UW", 0)
-        for k in range(3): mm(w("MB", 64 * k, 64), v("BLKo"), v("B01"), False, k == 2)
-        names("MB", 192)
-        if t == 0: late_constants()
-        for bank in BANKS: mm(w(bank, 0, 256), v("ID"), v("TRI"), True, False)
-        tt(v("LD"), w("UW", 0, 128), w("DIAG", 0, 128), Op.mult)
-        scan(v("LSc"), w("RS16", 0, 128), v("LD"), Op.mult, Op.add)
-        vc(w("LS", 8 * t, 8), v("LSc", 15, 128, 16))
+            mm(w(bank, o, 64), v("BLK2"), w("UAW", 64, 64), False, False)
+            mm(w(bank, o, 64), v("SELJ"), w("UAW", 0, 64), False, False)
+            mm(w(bank, o + 64, 64), v("SELW"), w("UAW", 0, 64), False, True)
+        names("XB0", 0)
+        for k in range(3): mm(w("D", 64 * k, 64), v("SELP"), w("UAW", 0, 64), False, k == 2)
+        if not last: names("JI", 256)
+        weave(old[11:])
+        scan(w("ZS", 64, 128), w("RSM", 0, 128), w("XB0", 0, 128), Op.max, Op.min)
+        ts(w("LS", 8 * t, 8), v("ZS", 79, 192, 16), 0.5, Op.mult, -8.5, Op.add)
         send("l", t, w("LL", 8 * t + 8, 8), w("LS", 8 * t, 8))
 
-        act(w("UWs", 0, 64), w("MB", 192, 64), scale=2.0, bias=593.0)
-        act(w("UWs", 64, 64), w("MB", 256, 64), scale=2.0, bias=17.0)
-        def f_col(k): ts(w("FI", 64 * k, 64), w("PF", 64 * k, 64), 5, Op.logical_shift_right, W - 1, Op.bitwise_and)
-        def f_out(k): tt(w("TAB", 192 + 64 * k, 64), w("FI", 64 * k, 64), w("MB", 64 * k, 64), Op.add)
-        def f_own(k): tt(w("VD", 64 * k, 64), w("TAB", 192 + 64 * k, 64), w("DIAG", 0, 64), Op.mult)
-        def f_list(k): scan(w("SL", 64 * k, 64), w("RS16", 0, 64), w("VD", 64 * k, 64), Op.mult, Op.add)
+        if not last: act(w("IS", 128 * t, 128), w("JI", 256, 128), scale=0.5)
+        tt(v("PF"), v("ZS", 15, 192, 16), v("ZS", 79, 256, 16), Op.mult)
+        scan(v("FS"), w("RSM", 0, 192), w("D", 0, 192), Op.max, Op.min)
+        ts(v("FI"), v("PF"), 5, Op.logical_shift_right, W - 1, Op.bitwise_and)
+        tt(TN, v("FI"), v("FS", 15, 192, 16), Op.max)
+        vc(v("TNu"), TN)
+        act(v("TNh"), TN, bias=-2048.0)
+        act(w("NS", 64 * t, 64), ix("FA", W + P, w("TNu", 4, 4)), scale=0.5, bias=127.625)
+        send("n", t, w("MM", 64 * t + 64, 64), w("NS", 64 * t, 64))
+        if not last: send("i", t, w("IJ", 128 * t + 128, 128), w("IS", 128 * t, 128))
+        act(v("AV"), ix("YF", W + P, v("TNu")), Act.Abs)
+        for s in range(15): mm(v("XB1", s, 192, 16), w("DM", 128 * s, 128), v("TNh"), False, s == 14)
+        ts(v("EQ"), w("XB1", 0, 192), 0.0, Op.is_equal, 8192.0, Op.mult)
+        scan(v("FL"), v("RT"), v("EQ"), Op.add, Op.max)
+        ts(v("TS", 0, 24, 2), v("FL", 15, 192, 16), v("cP"), Op.min)
 
-        def compare(k):
-            for q in range(4): mm(w(BANKS[k], 64 * q, 64), v("BLK"), w("VD", 64 * k, 64), False, q == 3)
-            for q in range(4):
-                c = 4 * k + q
-                act(w("AB", 64 * c, 64), w(BANKS[k], 64 * q, 64), Act.Abs, scale=-1.0, bias=w("SL", 16 * c + 15, 1))
-
-        def need1(): tt(v("TN"), v("SL", 15, 64, 16), w("DUM", 0, 4), Op.min)
-        def need2(): ts(v("TNu"), v("TN"), 2048.0, Op.add)
-        def need3():
-            ts(w("NS", 64 * t, 64), ix("FA", W + P, v("TNu")), 0.5, Op.mult, 127.75, Op.add)
-            send("n", t, w("MM", 64 * t + 64, 64), w("NS", 64 * t, 64))
-
-        tt(w("PF", 0, 64), w("UWs", 0, 64), w("UWs", 64, 64), Op.mult)
-        tt(w("PF", 64, 128), v("UWs"), w("JI", 0, 128), Op.mult)
-        f_col(0); f_col(1); f_out(0); f_col(2); f_own(0); f_out(1); f_list(0); f_own(1)
-        compare(0)
-        if not last: need1()
-        f_list(1)
-        compare(1)
-        if not last: need2()
-        f_out(2)
-        if not last: need3()
-        f_own(2); f_list(2)
-        compare(2)
-
-        if not last:
-            vc(w("IS", 128 * t, 128), w("UW", 0, 128))
-            send("i", t, w("IJ", 128 * t + 128, 128), w("IS", 128 * t, 128))
-            act(w("NA", 1024 * t, 1024), w("FA", 1024 * t, 1024), scale=-1.0)
-        for lo, n in ((0, 512), (512, 256)): scan(w("MN", lo, n), w("RS64", lo, n), w("AB", lo, n), Op.max, Op.min)
-        ts(v("DU"), v("MN", 63, 768, 64), 0.0, Op.is_equal, OUT, Op.mult)
-        tt(v("DV"), v("DU"), v("SL", 15, 192, 16), Op.add)
-        tt(v("DW"), v("DV"), v("DUM"), Op.min)
-        ts(v("TS"), v("DW"), 2048.0, Op.add)
-        for k in range(3): vc(ix("PP", W + P, w("TS", 4 * k, 4)), v("ZER"))
-        y1, y2 = ext(T.yf[:, 0:W - ROT], "yf1"), ext(T.yf[:, W - ROT:W], "yf2")
-        if t == RO - 2:
-            dma("P", "gd", 32, y1, v("NA", ROT, W))
-            dma("P", "gd", 32, y2, v("NA", 0, ROT))
-        if last:
-            dma("P", "gd2", 32, y1, v("PP", ROT, W), accum_op=Op.add, max_dma_last_dim=4096)
-            dma("P", "gd2", 32, y2, v("PP", 0, ROT), accum_op=Op.add, max_dma_last_dim=4096)
-            need1(); need2(); need3()
-
-    ts(v("YI"), v("KM", 1, 160, 2), 7, Op.logical_shift_right)
-    ts(v("YT"), v("YI"), 8192.0, Op.is_ge, -8193.0, Op.mult)
-    tt(v("YC"), v("YI"), v("YT"), Op.add)
-    for q in range(4):
-        mm(v("KT", 80 * q, 80 * q + 80, 1, 8), w("SY", 8 * q, 8), v("YC"), True, True)
-    for q in range(4): do("V", g.vector.tensor_copy, (T.YO[:, q, :], [("YO", q, q + 1, 1)]), [v("KT", 80 * q, 80 * q + 80, 1, 8)], (T.KT[0:8, 80 * q:80 * q + 80],))
-    for t in range(RO): dma("D", "out", 112, ext(T.yc[:, 64 * t:64 * t + 64], "yc%d" % t), (T.YO[:, :, 16 * t:16 * t + 16], [("YO", 0, 4, 1)]))
+    def costs():
+        for k in range(16): mm(v("JI", k, 320, 16, 8), w("SY", 8 * (k // 4), 8), v("YC", k % 4, 80, 4), True, True)
+    weave(strikes("YF", Op.mult, "NEG"), [match(w("SY", 8 * q, 8), v("CI", 3, 32, 4), w("QP", q, 1)) for q in range(4)] + [
+        lambda: ts(v("YT"), v("YI"), 8192.0, Op.is_ge, -8193.0, Op.mult),
+        lambda: tt(v("YC"), v("YI"), v("YT"), Op.add), costs])
+    dma("D", "out", 80, ext(T.yf[:, 0:W - ROT], "yf1"), v("YF", ROT, W))
+    dma("S", "out", 80, ext(T.yf[:, W - ROT:W], "yf2"), v("YF", 0, ROT))
+    act(v("YO"), v("JI", 0, 320, 1, 8))
+    dma("S", "out", 80, ext(T.yc[:], "yc"), v("YO"))
     landed("l", RO, "LL", 8); landed("n", RO, "MM", 64)
     vc(w("YPo", 0, 4), w("LL", 44, 4))
-    vc(w("YPo", 4, 4), w("LL", 40, 4))
+    ts(w("YPo", 4, 4), w("LL", 40, 4), -float(PAD), Op.add)
     ts(v("YZo"), w("MM", 320, 64), -128.0, Op.add)
-    dma("D", "out", 112, ext(T.yp[:], "yp"), v("YPo"))
-    dma("D", "out", 112, ext(T.yz[:], "yz"), v("YZo"))
+    dma("D", "out", 80, ext(T.yp[:], "yp"), v("YPo"))
+    dma("D", "out", 80, ext(T.yz[:], "yz"), v("YZo"))
     wait("P", "ls", sent[0])
-    wait("P", "gd2", 32)
-    wait("D", "out", 112)
+    wait("D", "out", 80)
     for q in "VSTP": wait("D", q, cnt[q])

@@ -6,7 +6,8 @@ PAD = 288
 BIG = float(1 << 27)
 UNIT = 2.0 ** -13
 MASK = 3 | 15 << 9
-NV = (4, 4, 4, 5)
+NV = (4, 4, 6, 5)
+LEAD = (1, 2, 1)
 SCRATCH = {}
 
 
@@ -20,11 +21,11 @@ _bufs("bfloat16", "FA 4176, YF 4176, ND 64, MM 384, NS 320, AV 192, EQ 192, HALF
 _bufs("bfloat16", "L3 128 3, IDK 512 3, RSM 256, ONE 128 2, XPRE 256 1, JPRE 192 2, DM 2048, EX 512 64")
 _bufs("bfloat16", "CI 128, CG 128, C1 128, C2 128, MS 256, MG 128, MG4 128, M7 128")
 _bufs("int32", "RM 1536, CM 2336, PR 8, PI 1, GPi 1, SPi 1, OPi 1, Pc 608, Pi 608, II 256, MI 256, PF 12, FI 12")
-_bufs("uint16", "LL 48, LS 40, OF 608, TNu 12, TS 24, KL 64")
+_bufs("uint16", "LL 48, LS 40, OF 608, TNu 12, TNf 4, TS 24, KL 64")
 _bufs("float16", "G 8192, G1 1024, G2 512, NR 1024, CD 160, W16 16, WZ 128, IJ 768, IS 640, PRh 8, SEL 2048, DUP 512, M2S 256")
-_bufs("float16", "ID 128, I2 128, I2h 256, EI 128, EJ 128, BLK2 128, SELW 128, SELJ 128, SELP 128, CK 64, NDG 320, TRI 192, Xf 64, YM 128, UAW 128, TNh 12")
+_bufs("float16", "ID 128, I2 128, I2h 256, EI 128, EJ 128, BLK2 128, SELW 128, SELJ 128, SELP 128, CK 64, NDG 192, TRI 192, Xf 64, YM 128, UAW 128, TNh 12")
 _bufs("float32", "RC 32, GPf 1, SPf 1, QP 4, SY 32, cW 1, cI 1, cJ 2, c0 1, cS 1, cN 2, cH 1, cP 1, cL 2, cK 3, cO 1, ownA 2, ownB 3")
-_bufs("float32", "NB 64, Yp 64, RS8 128, Y2 32, UU 256, KK 512, SC 512, ST 128, KF 384, ZS 256, FS 192, RT 192, FL 192, YI 80, YT 80, YC 80, YPo 8, YO 320 8")
+_bufs("float32", "NB 64, Yp 64, RS8 128, Y2 32, UU 256, KK 512, SC 512, ST 128, KF 384, ZS 256, FS 64, RT 192, FL 192, YI 80, YT 80, YC 80, YPo 8, YO 320 8")
 _bufs("float32", "XB0 512, XB1 512, JI 512, D 512", "psum")
 for _b in ("K0", "K1", "K2", "CB"): SCRATCH[_b] = ("psum", [128, 32, 16], "float32")
 SEMAPHORES = ["sV", "sS", "sT", "sP", "ls", "out"] + ["ld%d" % k for k in range(9)] + ["%s%d" % (m, t) for m in "lin" for t in range(1, RO + 1)]
@@ -123,6 +124,7 @@ def rank_program(g, core, T, topo):
     dma("S", "ld3", 16, v("CM", PAD), ext(T.cmate[:]))
     dma("D", "ld4", 16, v("RM"), ext(T.rmate[:]))
     for k, name in ((5, "FA"), (7, "YF")):
+        if name == "YF": wait("D", "ld5", 16)
         dma("D", "ld%d" % k, 16, v(name, ROT, W), ext(T.fig[:, 0:W - ROT]))
         dma("D", "ld%d" % (k + 1), 16, v(name, 0, ROT), ext(T.fig[:, W - ROT:W]))
 
@@ -170,36 +172,38 @@ def rank_program(g, core, T, topo):
     for h in range(2): ts(w("cK", h, 1), SP, 12.0 + 2 * h, Op.is_equal)
     ts(w("ownB", 0, 1), SP, 8.0, Op.min, -4096.0, Op.mult)
     ts(v("cW"), SP, 8.0, Op.is_le, 2.0, Op.mult)
-    for out, a, k, c in ((w("cN", 0, 1), v("c0"), 0.1875, 128.0625), (w("cN", 1, 1), v("c0"), -0.1875, -128.0625), (v("cS"), v("c0"), 8188.0, -8192.0),
-                         (w("cL", 0, 1), PI, 2.0 ** -24, -1.5 * 2.0 ** -24), (w("cL", 1, 1), PI, -312.0 * 2.0 ** -25, 476.0 * 2.0 ** -25),
-                         (v("cH"), v("c0"), 0.5, 0.0), (w("ownA", 0, 1), SP, -65536.0, 8 * 65536.0), (w("ownB", 1, 1), w("ownB", 0, 1), 1.0, 16384.0),
-                         (v("cP"), SP, 1.0, W + 64.0), (w("cK", 2, 1), w("cK", 0, 1), float(W), w("cK", 1, 1)),
-                         (w("ownA", 1, 1), w("ownA", 0, 1), v("cO"), 0.0), (w("ownB", 2, 1), w("ownB", 1, 1), v("cO"), 0.0),
-                         (v("CK"), w("CI", 0, 64), w("cK", 1, 1), w("cK", 0, 1)),
-                         (v("L3"), v("M7", 0, 128, 1, 3), v("cL", 0, 1, 1, 3), v("cL", 1, 2, 1, 3)),
-                         (v("RSM"), v("MS"), -BIG, BIG / 2), (v("RS8"), v("M7"), -BIG, 1 + 2.0 ** -15 + 2.0 ** -20),
-                         (w("OWN", 0, 64), w("CI", 0, 64), 0.0, w("ownB", 2, 1)), (w("OWN", 64, 64), w("CI", 0, 64), 0.0, w("ownA", 1, 1)),
-                         (v("HALF"), w("CI", 0, 16), 0.0, v("cH"))):
-        act(out, a, scale=k, bias=c)
+    def affine(*items):
+        for out, a, k, c in items: act(out, a, scale=k, bias=c)
+    affine((w("cN", 0, 1), v("c0"), 0.1875, 128.0625), (w("cN", 1, 1), v("c0"), -0.1875, -128.0625), (w("MM", 0, 64), v("ND"), 1.0, 128.0),
+           (w("IJ", 0, 128), w("D", 0, 128), 0.5, 0.0), (v("CK"), w("CI", 0, 64), w("cK", 1, 1), w("cK", 0, 1)), (v("cS"), v("c0"), 8188.0, -8192.0),
+           (w("cL", 0, 1), PI, 2.0 ** -24, -1.5 * 2.0 ** -24), (w("cL", 1, 1), PI, -312.0 * 2.0 ** -25, 476.0 * 2.0 ** -25),
+           (w("cK", 2, 1), w("cK", 0, 1), float(W), w("cK", 1, 1)),
+           (v("L3"), v("M7", 0, 128, 1, 3), v("cL", 0, 1, 1, 3), v("cL", 1, 2, 1, 3)), (v("RSM"), v("MS"), -BIG, BIG / 2))
     vc(v("KL"), w("CI", 0, 64))
     for name, c in (("ID", 1.0), ("I2", 2.0), ("EI", v("cI")), ("EJ", w("cJ", 0, 1))): match(v(name), v("CI"), PI, c)()
-    match(v("WZ"), v("MG"), GP_, UNIT)()
-    match(v("W16", 0, 16, 2), w("CI", 0, 8), GP_, v("cS"))()
-    match(v("W16", 1, 16, 2), w("CI", 0, 8), GP_, UNIT)()
     weave(twice(0), [match(w("I2h", 128 * h, 128), v("C2"), w("RC", 16 * h, 1), 2.0) for h in range(2)])
-    act(w("MM", 0, 64), v("ND"), bias=128.0)
-    act(w("IJ", 0, 128), w("D", 0, 128), scale=0.5)
-    fill(v("IDK", 0, 512, 2, 1), 0.0)
-    fill(v("IDK", 1, 512, 2, 1), -2.0)
-    fill(v("L3", 0, 128, 1, 1), 1.0)
-    for name, c in (("NEG", -1.0), ("RT", 0.0)): fill(v(name), c)
-    for name in ("FA", "YF"): fill(v(name, W), 1.0)
-    for h in range(2): fill(v("CNT", 64 * h, 64 * h + 64), -65536.0 / (1 + h))
-    fill(v("RT", 0, 192, 16), -BIG)
-    ts(w("NDG", 128, 192), w("MS", 0, 192), SP, Op.not_equal, 16384.0, Op.mult)
-    ts(v("TRI"), w("MS", 0, 192), SP, Op.is_ge, 16384.0, Op.mult)
-    for h, c in ((0, 593.0), (1, 17.0)): ts(w("NDG", 64 * h, 64), w("NDG", 128, 64), c, Op.max)
-    for name, c in (("BLK2", 2.0), ("SELW", v("cW")), ("SELJ", w("cJ", 1, 1)), ("SELP", w("cK", 2, 1))): match(v(name), v("MG"), GP_, c)()
+
+    def for_the_sums():
+        match(v("WZ"), v("MG"), GP_, UNIT)()
+        match(v("W16", 0, 16, 2), w("CI", 0, 8), GP_, v("cS"))()
+        match(v("W16", 1, 16, 2), w("CI", 0, 8), GP_, UNIT)()
+        fill(v("IDK", 0, 512, 2, 1), 0.0)
+        fill(v("IDK", 1, 512, 2, 1), -2.0)
+        fill(v("L3", 0, 128, 1, 1), 1.0)
+        ts(w("NDG", 128, 64), w("MS", 0, 64), SP, Op.not_equal, 16384.0, Op.mult)
+        ts(v("TRI"), w("MS", 0, 192), SP, Op.is_ge, 16384.0, Op.mult)
+        for h, c in ((0, 593.0), (1, 17.0)): ts(w("NDG", 64 * h, 64), w("NDG", 128, 64), c, Op.max)
+        for name, c in (("BLK2", 2.0), ("SELW", v("cW")), ("SELJ", w("cJ", 1, 1)), ("SELP", w("cK", 2, 1))): match(v(name), v("MG"), GP_, c)()
+
+    def for_the_choice():
+        affine((w("ownA", 0, 1), SP, -65536.0, 8 * 65536.0), (w("ownB", 1, 1), w("ownB", 0, 1), 1.0, 16384.0),
+               (v("RS8"), v("M7"), -BIG, 1 + 2.0 ** -15 + 2.0 ** -20),
+               (w("ownA", 1, 1), w("ownA", 0, 1), v("cO"), 0.0), (w("ownB", 2, 1), w("ownB", 1, 1), v("cO"), 0.0),
+               (w("CNT", 0, 64), v("CI", 0, 64, 1, 1), 0.0, -65536.0), (w("CNT", 64, 64), v("CI", 0, 64, 1, 1), 0.0, -32768.0),
+               (w("OWN", 0, 64), w("CI", 0, 64), 0.0, w("ownB", 2, 1)), (w("OWN", 64, 64), w("CI", 0, 64), 0.0, w("ownA", 1, 1)),
+               (v("cH"), v("c0"), 0.5, 0.0), (v("cP"), SP, 1.0, W + 64.0), (v("RT"), w("MS", 0, 192), 0.0, 0.0), (v("NEG"), w("CI", 0, 16), 0.0, -1.0),
+               (v("YF", W), w("CI", 0, 80), 0.0, 1.0), (w("FA", W + P, 16), w("CI", 0, 16), 0.0, 1.0),
+               (v("HALF"), w("CI", 0, 16), 0.0, v("cH")), (v("RT", 0, 192, 16), w("CI", 0, 12), 0.0, -BIG))
 
     def strikes(name, op, other):
         return [lambda c=c: tt(ix(name, W + 80, w("TS", 2 * c, 1)), w("AV", 16 * c, 16), v(other), op) for c in range(12)]
@@ -223,7 +227,7 @@ def rank_program(g, core, T, topo):
         def shift(lo, hi): return lambda: ts(v("Pi", lo, hi), v("Pc", lo, hi), 5, Op.logical_shift_right, W - 1, Op.bitwise_and)
         def conv(lo, hi): return lambda: vc(v("OF", lo, hi), v("Pi", lo, hi))
 
-        weave(strikes("FA", Op.add, "HALF") if t else [], [None] + [prod(b) for b in range(8)] + [None, shift(0, 128), None, conv(0, 128)])
+        weave(strikes("FA", Op.add, "HALF") if t else [], [None, None] + [prod(b) for b in range(8)] + [shift(0, 128), conv(0, 128)])
         act(v("NB"), need, scale=-1.0, bias=w("cN", 0, 1))
         act(v("NR"), ix("MM", 64 * t + 64, v("KL"), 64 * t), bias=w("cN", 1, 1))
         mm(w("JI", 0, 192), v("ONE"), v("JPRE"), True, False)
@@ -235,13 +239,14 @@ def rank_program(g, core, T, topo):
         mm(w("JI", 128, 64), v("EI"), iw, False, False)
         mm(w("JI", 128, 64), v("EJ"), jw, False, True)
         act(v("Y2"), w("JI", 64, 32))
+        if t == 0: for_the_sums()
         for bank, n in (("K0", 512), ("K1", 256), ("K2", 256)): mm(w(bank, 0, n), v("L3"), v("IDK", 0, n), True, False)
         for h in range(2): mm(w("D", 256 * h, 256), v("L3"), v("IDK", 0, 512, 2), h == 0, False)
         mm(w("CB", 0, 320), one1, v("IDK", 0, 320, 1, 1), True, False)
 
         def slots(q, eng):
-            n = 14 - NV[q]
-            return [16 * q + k for k in (list(range(n)) + [12, 13] if eng == "S" else list(range(n, 12)) + [14, 15])]
+            mine = [15, 13, 11, 9, 7, 5, 3, 1][:NV[q]]
+            return [16 * q + k for k in range(16) if (k in mine) == (eng == "V")]
         def far(q, eng):
             def one(k):
                 out, src = w("G", 128 * k, 128), ix("FA", W, w("OF", 8 * k, 8))
@@ -259,6 +264,8 @@ def rank_program(g, core, T, topo):
                     lambda: tt(w("UU", 0, n), w("MI", 0, n), v(bank, 1, 2 * n, 2), Op.add)]
         def keys(bank, q, m):
             lo, n = 128 * q, 128 * m
+            if t == 0:
+                return bits(bank, n, 8191.0) + [lambda: scan(w("SC", lo, n), w("RSM", 0, n), w("UU", 0, n), Op.max, Op.min)]
             return bits(bank, n, 8191.0) + [
                 lambda: tt(w("KK", lo, n), w("UU", 0, n), w("D", lo, n), Op.max),
                 lambda: scan(w("SC", lo, n), w("RSM", 0, n), w("KK", lo, n), Op.max, Op.min)]
@@ -267,8 +274,9 @@ def rank_program(g, core, T, topo):
             return [lambda: tt(low, low, w("CD", 128 + 8 * q, 8 * m), Op.add)]
 
         weave(far(0, "S"))
-        weave([shift(128, 512), lambda: tt(w("Pc", 512, 64), w("JI", 0, 64), v("Yp"), Op.mult), conv(128, 512),
-               lambda: tt(w("Pc", 576, 32), w("JI", 96, 32), v("Y2"), Op.mult), shift(512, 608), conv(512, 608)], [None, None, None] + far(0, "V"))
+        tt(w("Pc", 512, 64), w("JI", 0, 64), v("Yp"), Op.mult)
+        tt(w("Pc", 576, 32), w("JI", 96, 32), v("Y2"), Op.mult)
+        weave(far(0, "V"), [shift(128, 608), conv(128, 608)])
         tt(v("G1"), ix("FA", W, w("OF", 512, 64)), v("NR"), Op.max)
         tt(v("G2"), ix("FA", W, w("OF", 576, 32)), v("NR", 0, 1024, 2), Op.max)
         for q in range(4):
@@ -277,7 +285,7 @@ def rank_program(g, core, T, topo):
         for a in range(16): mm(k3("CB", a // 8, 16, 2, 2 * a % 16, 2, 0, 64), v("G1", a, 1024, 16), v("W16"), False, False)
         for q in range(4): mm(w("CB", 256 + 16 * q, 16), w("G2", 128 * q, 128), v("W16"), False, q == 3)
         weave(far(1, "S"))
-        weave(far(1, "V"), bits("CB", 160, 510.0) + [lambda: ts(v("CD"), w("UU", 0, 160), 0.0, Op.max)])
+        weave(far(1, "V"), [None] * LEAD[0] + bits("CB", 160, 510.0) + [lambda: ts(v("CD"), w("UU", 0, 160), 0.0, Op.max)])
         sums(1, False)
         c1 = v("CD", 0, 128, 1, 64)
         for q in range(4):
@@ -286,35 +294,34 @@ def rank_program(g, core, T, topo):
         for a in range(16):
             mm(v("D", 384 + a, 512, 16), v("ID"), w("CD", 152, 8), False, a == 15)
         weave(far(2, "S"))
-        weave(far(2, "V"), [None] + keys("K0", 0, 2) + plus(0, 2))
+        weave(far(2, "V"), [None] * LEAD[1] + keys("K0", 0, 2))
         for a in range(16): mm(v("K2", 2 * a + 1, 256, 32), v("ID"), w("CD", 152, 8), False, False)
         sums(2, True)
-        mm(w("XB0", 0, 128), v("ID"), w("NDG", 0, 128), True, False)
-        mm(w("XB0", 0, 128), one1, v("CNT"), False, False)
-        mm(w("CB", 0, 128), v("ID"), v("OWN"), True, False)
-        mm(w("XB1", 0, 192), v("ID"), v("TRI"), True, False)
         weave(far(3, "S"))
-        weave(far(3, "V"), keys("K1", 2, 1) + plus(2, 1))
-        sums(3, True, 0, 12)
-        sums(3, True, 12, 16)
+        weave([None] * LEAD[2] + keys("K1", 2, 1), far(3, "V"))
+        for lo, hi in ((0, 8), (8, 12), (12, 16)): sums(3, True, lo, hi)
         act(w("YM", 64, 64), v("Yp"), bias=-296.5, scale=0.5)
         act(w("YM", 0, 64), w("JI", 128, 64))
-        mm(w("CB", 0, 128), v("ID"), v("YM"), False, False)
+        if t == 0: for_the_choice()
+        mm(w("CB", 0, 128), v("ID"), v("YM"), True, False)
+        mm(w("CB", 0, 128), v("ID"), v("OWN"), False, False)
+        mm(w("XB0", 0, 128), v("ID"), w("NDG", 0, 128), True, False)
+        mm(w("XB0", 0, 128), one1, v("CNT"), False, False)
+        mm(w("XB1", 0, 192), v("ID"), v("TRI"), True, False)
         if not last: mm(w("JI", 256, 128), one1, v("CNT"), True, False)
         act(w("FA", W, P), need, scale=2.0, bias=-255.0)
+        for lo, names_ in ((15, w("LL", 8 * t + 4, 4)), (207, w("LL", 8 * t, 4))): act(v("ZS", lo, lo + 49, 16), names_, scale=2.0, bias=17.0)
 
         kf = v("KF", 7, 128, 8)
         def parts():
             ts(v("KF", 135, 256, 8), kf, 48.0, Op.add, -48.0, Op.add)
             ts(v("KF", 263, 384, 8), kf, 1536.0, Op.add, -1536.0, Op.add)
         def spread():
-            mm(w("D", 0, 192), v("ID"), w("NDG", 128, 192), True, False)
+            mm(w("D", 0, 64), v("ID"), w("NDG", 128, 64), True, False)
             tt(v("TBf"), v("KF", 7, 256, 8), v("KF", 135, 384, 8), Op.subtract)
             for q in range(4): mm(k3("CB", 0, 8, 1, 4 * q, 4), w("E8", 128 * q, 128), v("TBf"), False, q == 3)
-        own = [lambda: ts(v("ZS", 15, 64, 16), w("LL", 8 * t + 4, 4), 2.0, Op.mult, 17.0, Op.add),
-               lambda: ts(v("ZS", 207, 256, 16), w("LL", 8 * t, 4), 2.0, Op.mult, 17.0, Op.add)]
-        old = strikes("YF", Op.mult, "NEG") if t else [None] + rows + twice(1)
-        weave(own, old[:1])
+        old = strikes("YF", Op.mult, "NEG") if t else rows + twice(1) + [None]
+        weave(old[:1], plus(0, 3))
         turn = v("SC", 3, 512, 4)
         weave(keys("K2", 3, 1) + [lambda: do("V", g.vector.transpose, v("ST"), [turn], (turn[0],)),
                                   lambda: scan(w("KF", 0, 128), v("RS8"), v("ST"), Op.max, Op.min), parts, spread], old[1:10])
@@ -326,22 +333,25 @@ def rank_program(g, core, T, topo):
             mm(w(bank, o, 64), v("SELJ"), w("UAW", 0, 64), False, False)
             mm(w(bank, o + 64, 64), v("SELW"), w("UAW", 0, 64), False, True)
         names("XB0", 0)
-        for k in range(3): mm(w("D", 64 * k, 64), v("SELP"), w("UAW", 0, 64), False, k == 2)
+        mm(w("D", 0, 64), v("SELP"), w("UAW", 0, 64), False, True)
+        for k in range(3): mm(w("XB1", 64 * k, 64), v("SELP"), w("UAW", 0, 64), False, False)
         if not last: names("JI", 256)
         weave(old[11:])
         scan(w("ZS", 64, 128), w("RSM", 0, 128), w("XB0", 0, 128), Op.max, Op.min)
-        ts(w("LS", 8 * t, 8), v("ZS", 79, 192, 16), 0.5, Op.mult, -8.5, Op.add)
+        act(w("LS", 8 * t, 8), v("ZS", 79, 192, 16), scale=0.5, bias=-8.5)
         send("l", t, w("LL", 8 * t + 8, 8), w("LS", 8 * t, 8))
 
-        if not last: act(w("IS", 128 * t, 128), w("JI", 256, 128), scale=0.5)
+        scan(v("FS"), w("RSM", 0, 64), w("D", 0, 64), Op.max, Op.min)
         tt(v("PF"), v("ZS", 15, 192, 16), v("ZS", 79, 256, 16), Op.mult)
-        scan(v("FS"), w("RSM", 0, 192), w("D", 0, 192), Op.max, Op.min)
         ts(v("FI"), v("PF"), 5, Op.logical_shift_right, W - 1, Op.bitwise_and)
-        tt(TN, v("FI"), v("FS", 15, 192, 16), Op.max)
+        act(v("TNh"), v("FI"), bias=-2048.0)
+        for k in (1, 0): tt(v("RT", 64 * k + 15, 64 * k + 64, 16), w("FI", 4 * k, 4), v("FS", 15, 64, 16), Op.max)
+        vc(v("TNf"), v("RT", 79, 128, 16))
+        tt(v("RT", 143, 192, 16), w("FI", 8, 4), v("FS", 15, 64, 16), Op.max)
+        act(w("NS", 64 * t, 64), ix("FA", W + P, v("TNf")), scale=0.5, bias=127.625)
         vc(v("TNu"), TN)
-        act(v("TNh"), TN, bias=-2048.0)
-        act(w("NS", 64 * t, 64), ix("FA", W + P, w("TNu", 4, 4)), scale=0.5, bias=127.625)
         send("n", t, w("MM", 64 * t + 64, 64), w("NS", 64 * t, 64))
+        if not last: act(w("IS", 128 * t, 128), w("JI", 256, 128), scale=0.5)
         if not last: send("i", t, w("IJ", 128 * t + 128, 128), w("IS", 128 * t, 128))
         act(v("AV"), ix("YF", W + P, v("TNu")), Act.Abs)
         for s in range(15): mm(v("XB1", s, 192, 16), w("DM", 128 * s, 128), v("TNh"), False, s == 14)

@@ -6,8 +6,8 @@ PAD = 288
 BIG = float(1 << 27)
 UNIT = 2.0 ** -13
 MASK = 3 | 15 << 9
-NV = (4, 4, 6, 5)
-LEAD = (1, 2, 1)
+PLAN = ("gcgcggg", "ggcgcgcgc", "ggggccgcgcc", "gggcgcgcgc")
+FEWER = 1
 SCRATCH = {}
 
 
@@ -17,17 +17,17 @@ def _bufs(dtype, text, where="sbuf"):
         SCRATCH[f[0]] = (where, [int(f[2]) if len(f) > 2 else 128, int(f[1])], dtype)
 
 
-_bufs("bfloat16", "FA 4176, YF 4176, ND 64, MM 384, NS 320, AV 192, EQ 192, HALF 16, NEG 16, YZo 64, TBf 32, E8 512, OWN 128, CNT 128 1")
-_bufs("bfloat16", "L3 128 3, IDK 512 3, RSM 256, ONE 128 2, XPRE 256 1, JPRE 192 2, DM 2048, EX 512 64")
-_bufs("bfloat16", "CI 128, CG 128, C1 128, C2 128, MS 256, MG 128, MG4 128, M7 128")
-_bufs("int32", "RM 1536, CM 2336, PR 8, PI 1, GPi 1, SPi 1, OPi 1, Pc 608, Pi 608, II 256, MI 256, PF 12, FI 12")
-_bufs("uint16", "LL 48, LS 40, OF 608, TNu 12, TNf 4, TS 24, KL 64")
-_bufs("float16", "G 8192, G1 1024, G2 512, NR 1024, CD 160, W16 16, WZ 128, IJ 768, IS 640, PRh 8, SEL 2048, DUP 512, M2S 256")
-_bufs("float16", "ID 128, I2 128, I2h 256, EI 128, EJ 128, BLK2 128, SELW 128, SELJ 128, SELP 128, CK 64, NDG 192, TRI 192, Xf 64, YM 128, UAW 128, TNh 12")
-_bufs("float32", "RC 32, GPf 1, SPf 1, QP 4, SY 32, cW 1, cI 1, cJ 2, c0 1, cS 1, cN 2, cH 1, cP 1, cL 2, cK 3, cO 1, ownA 2, ownB 3")
-_bufs("float32", "NB 64, Yp 64, RS8 128, Y2 32, UU 256, KK 512, SC 512, ST 128, KF 384, ZS 256, FS 64, RT 192, FL 192, YI 80, YT 80, YC 80, YPo 8, YO 320 8")
-_bufs("float32", "XB0 512, XB1 512, JI 512, D 512", "psum")
-for _b in ("K0", "K1", "K2", "CB"): SCRATCH[_b] = ("psum", [128, 32, 16], "float32")
+_bufs("bfloat16", "FA 4864, YF 4864, ND 64, MM 384, NS 320, AV 192, AY 384, EQ 192, HALF 16, YZo 64, TBf 32, E8 512, OWN 128, CNT 128 1")
+_bufs("bfloat16", "L3 128 3, IDK 640 3, RSM 128, ONE 128 2, XPRE 128 1, JPRE 192 2, DM 2048, EX 1024")
+_bufs("bfloat16", "CI 128, C1 128, C2 128, MS 256, MG 128, M7 128")
+_bufs("int32", "RM 1536, CM 2336, PR 8, PI 1, PB 3, Pc 608, Pi 608, II 256, MI 96, MX 512, PF 12, FI 12")
+_bufs("uint16", "LL 48, LS 40, OF 608, TNu 12, TS 384, RT 192, KL 64")
+_bufs("float16", "G 8192, G1 1024, G2 512, NR 1024, CD 96, CR 128, W16 16, WK 16, WZ 128, IJ 768, IS 640, PRh 8, SEL 2048, DUP 512, M2S 256")
+_bufs("float16", "ID 128, I2 128, I2h 256, EI 128, EJ 128, BLK2 128, SELW 128, SELJ 128, SELP 128, SELQ 128, CK 192, NDG 192, TRI 192, Xf 64, YM 128, UAW 128, TNh 12")
+_bufs("float32", "RC 32, GPf 1, SPf 1, QP 4, SY 32, SQ 16, cW 1, cS 1, cN 2, cH 3, cP 1, cL 2, cK 1, cO 1, ownA 2, ownB 3")
+_bufs("float32", "NB 64, YY 96, RS8 128, UU 96, KK 1024, SC 512, ST 128, KF 384, ZS 256, FS 64, YI 80, YT 80, YC 80, YPo 8, YO 320 8")
+_bufs("float32", "XB0 512, XB1 512, JI 512, K0 512, K1 512, K2 512, K3 512", "psum")
+SCRATCH["CB"] = ("psum", [128, 32, 16], "float32")
 SEMAPHORES = ["sV", "sS", "sT", "sP", "ls", "out"] + ["ld%d" % k for k in range(9)] + ["%s%d" % (m, t) for m in "lin" for t in range(1, RO + 1)]
 
 
@@ -44,13 +44,12 @@ def rank_program(g, core, T, topo):
 
     def v(name, lo=0, hi=None, st=1, r=None):
         if len(SCRATCH[name][1]) == 3:
-            ap = T[name][0:r or 128, lo // 16:(hi + 15) // 16:st // 16, lo % 16] if st % 16 == 0 else T[name][0:r or 128, lo // 16:hi // 16, lo % 16:16:st]
-            return ap, [(name, lo, hi, st)]
+            return T[name][:, lo // 16:hi // 16, lo % 16:16:st], [(name, lo, hi, st)]
         hi = SCRATCH[name][1][1] if hi is None else hi
         return T[name][0:(r or SCRATCH[name][1][0]), lo:hi:st], [(name, lo, hi, st)]
-    def w(name, lo, n, st=1): return v(name, lo, lo + n * st, st)
+    def w(name, lo, n): return v(name, lo, lo + n)
     def ix(name, hi, lst, lo=0): return T[name][:, lo:hi].indirect(lst[0]), [(name, lo, hi, 1)] + lst[1]
-    def k3(name, r0, r1, rs, c, n, p0=0, p1=128): return T[name][p0:p1, r0:r1:rs, c:c + n], [(name, 0, 512, 1)]
+    def cb(c, n): return T.CB[:, 0:8, c:c + n], [("CB", 0, 512, 1)]
     def ext(ap, name=None): return ap, [(name, 0, 1, 1)] if name else []
 
     def wait(q, ev, n):
@@ -91,18 +90,21 @@ def rank_program(g, core, T, topo):
     def ts(out, a, s1, op0, s2=None, op1=None):
         do("V", g.vector.tensor_scalar, out, [a] + [s for s in (s1, s2) if col(s)],
            (a[0], s1[0] if col(s1) else s1, s2[0] if col(s2) else s2, op0) + ((op1,) if op1 else ()))
-    def scan(out, d0, d1, op0, op1): do("V", g.vector.tensor_tensor_scan, out, [d0, d1], (d0[0], d1[0], 0.0, op0, op1))
+    def scan(out, d0, d1, op0, op1, first=0.0): do("V", g.vector.tensor_tensor_scan, out, [d0, d1], (d0[0], d1[0], first, op0, op1))
     def act(out, a, f=Act.Identity, bias=0.0, scale=1.0):
         do("S", g.scalar.activation, out, [a] + [s for s in (bias, scale) if col(s)], (a[0], f),
            bias=bias[0] if col(bias) else bias, scale=scale[0] if col(scale) else scale)
     def mm(out, l, r, st, sp): do("T", g.tensor.matmul, out, [l, r], (l[0], r[0], st, sp))
     def fill(out, c): do("V", g.vector.memset, out, [], (c,))
-    def iota(name, pattern, base, cm): do("P", g.iota, v(name), [], (pattern, base, cm), allow_small_or_imprecise_dtypes=True)
-    def pick(name, pattern, op, other, cm): do("P", g.affine_select, v(name), [v(name)], (T[name][:], pattern, op, other, 0, cm))
+    def iota(out, pattern, base, cm): do("P", g.iota, out if col(out) else v(out), [], (pattern, base, cm), allow_small_or_imprecise_dtypes=True)
+    def pick(name, src, pattern, op, other, base, cm): do("P", g.affine_select, v(name), [v(src)], (T[src][:], pattern, op, other, base, cm))
     def weave(first, second=()):
         for n in range(max(len(first), len(second))):
             for calls in (first, second):
                 if n < len(calls) and calls[n]: calls[n]()
+    def turns(plan, gathers, calls):
+        lists = {"g": list(gathers), "c": list(calls)}
+        for x in plan: lists[x].pop(0)()
 
     sent = [0]
 
@@ -123,94 +125,104 @@ def rank_program(g, core, T, topo):
     dma("D", "ld2", 16, v("ND"), ext(T.need[:]))
     dma("S", "ld3", 16, v("CM", PAD), ext(T.cmate[:]))
     dma("D", "ld4", 16, v("RM"), ext(T.rmate[:]))
-    for k, name in ((5, "FA"), (7, "YF")):
+    for k, name, q in ((5, "FA", "S"), (7, "YF", "D")):
         if name == "YF": wait("D", "ld5", 16)
         dma("D", "ld%d" % k, 16, v(name, ROT, W), ext(T.fig[:, 0:W - ROT]))
-        dma("D", "ld%d" % (k + 1), 16, v(name, 0, ROT), ext(T.fig[:, W - ROT:W]))
+        dma(q, "ld%d" % (k + 1), 16, v(name, 0, ROT), ext(T.fig[:, W - ROT:W]))
 
     do("P", g.iota, v("PI"), [], ([[0, 1]], 0, 1))
     iota("RC", [[128, 2], [-1, 16]], 0, 1)
-    iota("CG", [[16, 8], [0, 16]], 0, 0)
     iota("MG", [[1, 8], [0, 16]], 0, 0)
     iota("CI", [[1, 128]], 0, 0)
     iota("MS", [[0, 16], [1, 16]], 0, 0)
     iota("C1", [[16, 8], [128, 2], [1, 8]], 0, 0)
     iota("C2", [[16, 8], [136, 2], [1, 8]], 0, 0)
     iota("M7", [[0, 16], [1, 8]], 0, 0)
+    for h in range(2): iota(v("IDK", h, 640, 2), [[0, 20], [8, 8], [64, 2]], 0, 8)
+    for lo, hi, st, c in ((0, 256, 1, -32768), (256, 640, 2, -2), (257, 640, 2, 0)): iota(v("IDK", lo, hi, st, 1), [[0, len(range(lo, hi, st))]], c, 0)
+    iota(v("MX", 0, 512, 2), [[0, 256]], -(1 << 23), 0)
+    iota("EX", [[0, 1024]], 1, 0)
+    pick("EX", "EX", [[1, 2], [2, 64], [0, 8]], Op.is_equal, 0.0, 0, -1)
     iota("QP", [[-32, 4]], 0, 1)
-    iota("MG4", [[4, 8], [0, 16]], 3, 0)
-    iota("IDK", [[0, 16], [8, 16], [0, 2]], 0, 8)
-    iota("EX", [[0, 512]], 1, 0)
-    pick("EX", [[1, 64], [0, 8]], Op.is_equal, 0.0, -1)
-    iota("DM", [[0, 2048]], -1, 0)
-    pick("DM", [[-1, 16], [-16, 8], [0, 16]], Op.is_equal, 0.0, 1)
-    pick("DM", [[0, 16], [-16, 8], [-1, 16]], Op.not_equal, 1.0, 1)
+    iota("E8", [[0, 256], [-2, 2]], 1, 0)
+    pick("E8", "E8", [[-32, 4], [-4, 8], [0, 16]], Op.is_equal, 0.0, -3, 1)
     SP, GP_, PI = v("SPf"), v("GPf"), w("RC", 0, 1)
     def match(out, pattern, c, k=1.0): return lambda: ts(out, pattern, c, Op.is_equal, k, Op.mult)
-    rows = [match(v("E8", 128 * q + h, 128 * q + 128, 2), v("MG4", h, 128, 2), w("QP", q, 1), (1 - 2 * h) * 2.0 ** 34) for q in range(4) for h in range(2)]
     def twice(p):
         return [match(w("DUP", 256 * p + 128 * h, 128), v("C1"), w("RC", 16 * h + 8 * p, 1), 2.0) for h in range(2)] + [
             match(w("M2S", 128 * p, 128), v("C2"), w("RC", 8 * p, 1))]
-    for name, c in (("ONE", 1.0), ("XPRE", 17.0), ("JPRE", 1.0)): fill(v(name), c)
-    ts(v("SPi"), v("PI"), 15, Op.bitwise_and)
-    ts(v("GPi"), v("PI"), 4, Op.logical_shift_right)
-    fill(v("JPRE", 0, 128, 1, 1), 16.0)
-    fill(v("JPRE", 128, 192), 0.0)
-    ts(v("OPi"), v("PI"), 1, Op.bitwise_and)
-    vc(SP, v("SPi")); vc(GP_, v("GPi"))
-    ts(v("cO"), v("OPi"), -2.0, Op.mult, 1.0, Op.add)
-    fill(v("JPRE", 64, 96, 1, 1), 592.0)
-    fill(v("CM", 0, PAD), 0)
-    for s in range(16): match(w("SEL", 128 * s, 128), v("CG"), w("RC", s, 1), 2.0)()
-    ts(w("LL", 0, 4), w("PR", 0, 4), float(PAD), Op.add)
-    vc(w("LL", 4, 4), w("PR", 4, 4))
-    vc(v("PRh"), v("PR"))
-    for s in range(16): mm(v("D", s, 128, 16), w("SEL", 128 * s, 128), v("PRh"), True, True)
-    ts(v("c0"), SP, 0.0, Op.is_equal)
-    ts(v("cI"), SP, 8.0, Op.is_equal)
-    for h in range(2): match(w("cJ", h, 1), SP, 10.0, 1.0 + h)()
-    for h in range(2): ts(w("cK", h, 1), SP, 12.0 + 2 * h, Op.is_equal)
-    ts(w("ownB", 0, 1), SP, 8.0, Op.min, -4096.0, Op.mult)
-    ts(v("cW"), SP, 8.0, Op.is_le, 2.0, Op.mult)
     def affine(*items):
         for out, a, k, c in items: act(out, a, scale=k, bias=c)
-    affine((w("cN", 0, 1), v("c0"), 0.1875, 128.0625), (w("cN", 1, 1), v("c0"), -0.1875, -128.0625), (w("MM", 0, 64), v("ND"), 1.0, 128.0),
-           (w("IJ", 0, 128), w("D", 0, 128), 0.5, 0.0), (v("CK"), w("CI", 0, 64), w("cK", 1, 1), w("cK", 0, 1)), (v("cS"), v("c0"), 8188.0, -8192.0),
-           (w("cL", 0, 1), PI, 2.0 ** -24, -1.5 * 2.0 ** -24), (w("cL", 1, 1), PI, -312.0 * 2.0 ** -25, 476.0 * 2.0 ** -25),
-           (w("cK", 2, 1), w("cK", 0, 1), float(W), w("cK", 1, 1)),
-           (v("L3"), v("M7", 0, 128, 1, 3), v("cL", 0, 1, 1, 3), v("cL", 1, 2, 1, 3)), (v("RSM"), v("MS"), -BIG, BIG / 2))
+    def row(s): return w("SQ", s, 1)
+    for name, c in (("ONE", 1.0), ("XPRE", 17.0), ("JPRE", 1.0)): fill(v(name), c)
+    for n, (k, m) in enumerate(((0, 15), (4, 7), (0, 1))): ts(w("PB", n, 1), v("PI"), k, Op.logical_shift_right, m, Op.bitwise_and)
+    vc(SP, w("PB", 0, 1)); vc(GP_, w("PB", 1, 1))
+    fill(v("JPRE", 0, 128, 1, 1), 16.0)
+    fill(v("JPRE", 128, 192), 0.0)
+    match(v("BLK2"), v("MG"), GP_, 2.0)()
+    match(v("SQ"), w("CI", 0, 16), SP)()
+    fill(v("JPRE", 96, 128, 1, 1), 592.0)
+    fill(v("CM", 0, PAD), 0)
+    for s in range(8):
+        ts(w("SEL", 128 * s, 128), v("BLK2"), row(s), Op.mult)
+        act(w("SEL", 128 * s + 1024, 128), v("BLK2"), scale=row(s + 8))
+    pick("DM", "SEL", [[0, 16], [-16, 8], [-1, 16]], Op.not_equal, -2.0, 0, 1)
     vc(v("KL"), w("CI", 0, 64))
-    for name, c in (("ID", 1.0), ("I2", 2.0), ("EI", v("cI")), ("EJ", w("cJ", 0, 1))): match(v(name), v("CI"), PI, c)()
-    weave(twice(0), [match(w("I2h", 128 * h, 128), v("C2"), w("RC", 16 * h, 1), 2.0) for h in range(2)])
+    vc(v("PRh"), v("PR"))
+    ts(w("LL", 0, 4), w("PR", 0, 4), float(PAD), Op.add)
+    vc(w("LL", 4, 4), w("PR", 4, 4))
+    for s in range(16): mm(v("K3", s, 128, 16), w("SEL", 128 * s, 128), v("PRh"), True, True)
+    affine((w("cN", 0, 1), row(0), 0.1875, 128.0625), (w("cN", 1, 1), row(0), -0.1875, -128.0625), (w("MM", 0, 64), v("ND"), 1.0, 128.0),
+           (v("cS"), row(0), 8188.0, -8192.0))
+    ts(w("CK", 64, 64), w("MS", 0, 64), 15.0, Op.is_equal, 1024.0, Op.mult)
+    tt(w("CK", 64, 64), w("CK", 64, 64), w("CI", 0, 64), Op.add)
+    ts(w("CK", 128, 64), w("MS", 0, 64), 15.0, Op.not_equal, row(12), Op.mult)
+    for name, c in (("ID", 1.0), ("I2", 2.0)): match(v(name), v("CI"), PI, c)()
+    ts(w("CK", 0, 64), w("CK", 64, 64), row(14), Op.mult)
+    weave([match(v("EI"), v("CI"), PI, row(8)), match(v("EJ"), v("CI"), PI, row(10))] + twice(0) + [
+        match(w("I2h", 128 * h, 128), v("C2"), w("RC", 16 * h, 1), 2.0) for h in range(2)])
+    for out in (v("W16", 0, 16, 2), w("WK", 0, 8)): match(out, w("CI", 0, 8), GP_, v("cS"))()
+    for out in (v("W16", 1, 16, 2), w("WK", 8, 8)): match(out, w("CI", 0, 8), GP_, UNIT)()
 
     def for_the_sums():
-        match(v("WZ"), v("MG"), GP_, UNIT)()
-        match(v("W16", 0, 16, 2), w("CI", 0, 8), GP_, v("cS"))()
-        match(v("W16", 1, 16, 2), w("CI", 0, 8), GP_, UNIT)()
-        fill(v("IDK", 0, 512, 2, 1), 0.0)
-        fill(v("IDK", 1, 512, 2, 1), -2.0)
-        fill(v("L3", 0, 128, 1, 1), 1.0)
+        affine((w("IJ", 0, 128), w("K3", 0, 128), 0.5, 0.0), (w("cL", 0, 1), PI, 2.0 ** -24, -1.5 * 2.0 ** -24),
+               (w("cL", 1, 1), PI, -312.0 * 2.0 ** -25, 476.0 * 2.0 ** -25), (v("WZ"), v("BLK2"), UNIT / 2, 0.0),
+               (v("L3"), v("M7", 0, 128, 1, 3), v("cL", 0, 1, 1, 3), v("cL", 1, 2, 1, 3)), (v("L3", 0, 128, 1, 1), v("CI", 0, 128, 1, 1), 0.0, 1.0),
+               (v("RSM"), w("MS", 0, 128), -BIG, BIG / 2))
+
+    def for_the_lists():
+        ts(w("ownB", 0, 1), SP, 8.0, Op.min, -4096.0, Op.mult)
+        ts(v("cW"), SP, 8.0, Op.is_le)
         ts(w("NDG", 128, 64), w("MS", 0, 64), SP, Op.not_equal, 16384.0, Op.mult)
         ts(v("TRI"), w("MS", 0, 192), SP, Op.is_ge, 16384.0, Op.mult)
         for h, c in ((0, 593.0), (1, 17.0)): ts(w("NDG", 64 * h, 64), w("NDG", 128, 64), c, Op.max)
-        for name, c in (("BLK2", 2.0), ("SELW", v("cW")), ("SELJ", w("cJ", 1, 1)), ("SELP", w("cK", 2, 1))): match(v(name), v("MG"), GP_, c)()
+        ts(v("TRI", 15, 192, 16), w("CI", 0, 12), 0.0, Op.mult)
 
     def for_the_choice():
-        affine((w("ownA", 0, 1), SP, -65536.0, 8 * 65536.0), (w("ownB", 1, 1), w("ownB", 0, 1), 1.0, 16384.0),
+        affine((v("cO"), w("PB", 2, 1), -2.0, 1.0), (w("FA", W, 4 * P), w("MS", 0, 4 * P), 0.0, 1.0),
+               (w("ownA", 0, 1), SP, -65536.0, 8 * 65536.0), (w("ownB", 1, 1), w("ownB", 0, 1), 1.0, 16384.0),
                (v("RS8"), v("M7"), -BIG, 1 + 2.0 ** -15 + 2.0 ** -20),
                (w("ownA", 1, 1), w("ownA", 0, 1), v("cO"), 0.0), (w("ownB", 2, 1), w("ownB", 1, 1), v("cO"), 0.0),
                (w("CNT", 0, 64), v("CI", 0, 64, 1, 1), 0.0, -65536.0), (w("CNT", 64, 64), v("CI", 0, 64, 1, 1), 0.0, -32768.0),
                (w("OWN", 0, 64), w("CI", 0, 64), 0.0, w("ownB", 2, 1)), (w("OWN", 64, 64), w("CI", 0, 64), 0.0, w("ownA", 1, 1)),
-               (v("cH"), v("c0"), 0.5, 0.0), (v("cP"), SP, 1.0, W + 64.0), (v("RT"), w("MS", 0, 192), 0.0, 0.0), (v("NEG"), w("CI", 0, 16), 0.0, -1.0),
-               (v("YF", W), w("CI", 0, 80), 0.0, 1.0), (w("FA", W + P, 16), w("CI", 0, 16), 0.0, 1.0),
-               (v("HALF"), w("CI", 0, 16), 0.0, v("cH")), (v("RT", 0, 192, 16), w("CI", 0, 12), 0.0, -BIG))
+               (v("E8"), v("E8"), 2.0 ** 34, 0.0), (w("cH", 1, 1), row(14), 2.0, 0.0), (w("cH", 2, 1), row(12), 8192.0, 0.0),
+               (v("cK"), row(12), W / 2, w("cH", 1, 1)), (v("SELW"), v("BLK2"), v("cW"), 0.0), (v("SELJ"), v("BLK2"), row(10), 0.0),
+               (v("SELP"), v("BLK2"), v("cK"), 0.0), (v("SELQ"), v("BLK2"), w("cH", 2, 1), 0.0))
 
-    def strikes(name, op, other):
-        return [lambda c=c: tt(ix(name, W + 80, w("TS", 2 * c, 1)), w("AV", 16 * c, 16), v(other), op) for c in range(12)]
+    for_the_strikes = [lambda: fill(v("RT"), 65535), lambda: ts(w("cH", 0, 1), row(0), 0.5, Op.mult, -128.0, Op.add),
+                       lambda: ts(v("cP"), SP, 32.0, Op.mult, W + 256.0, Op.add),
+                       lambda: ts(v("HALF"), w("CI", 0, 16), 0.0, Op.mult, w("cH", 0, 1), Op.add)]
+
+    for_the_costs = [match(w("SY", 8 * q, 8), v("CI", 3, 32, 4), w("QP", q, 1)) for q in range(4)]
+
+    def marks(t):
+        return [lambda c=c: tt(ix("FA", W + 768, w("TS", 192 * (t % 2) + 16 * c + 14, 1)), w("AV", 16 * c, 16), v("HALF"), Op.add) for c in range(12)]
+    def minus(t): act(w("AY", 192 * (t % 2), 192), v("AV"), scale=-1.0, bias=128.0)
+    def strikes(t):
+        return [lambda c=c: vc(ix("YF", W + 768, w("TS", 192 * (t % 2) + 16 * c + 14, 1)), w("AY", 192 * (t % 2) + 16 * c, 16)) for c in range(12)]
 
     one1 = v("ONE", 0, 128, 1, 1)
-    TN = v("RT", 15, 192, 16)
-    KB = (("K0", 0), ("K0", 256), ("K1", 0), ("K2", 0))
+    TN, YP, old = v("RT", 0, 192, 16), w("YY", 0, 64), []
     for t in range(RO):
         par, last = t % 2, t == RO - 1
         jw, iw = w("IJ", 128 * t, 64), w("IJ", 128 * t + 64, 64)
@@ -218,89 +230,84 @@ def rank_program(g, core, T, topo):
         if t:
             landed("l", t, "LL", 8); landed("i", t, "IJ", 128); landed("n", t, "MM", 64)
 
-        for h in range(2): mm(w("XB%d" % h, 0, 256), one1, v("XPRE"), True, False)
+        def needs():
+            act(v("NB"), need, scale=-1.0, bias=w("cN", 0, 1))
+            act(v("NR"), ix("MM", 64 * t + 64, v("KL"), 64 * t), bias=w("cN", 1, 1))
+        XB = [w(bank, 64 * h, 64) for bank in ("XB0", "K1", "K2", "XB1") for h in range(2)]
+        for bank in ("XB0", "K1", "K2", "XB1"): mm(w(bank, 0, 128), one1, v("XPRE"), True, False)
         act(v("Xf"), ix("CM", PAD + 2048, w("LL", 8 * t, 4)))
-        act(v("Yp"), ix("RM", 1536, w("LL", 8 * t + 4, 4)), scale=2.0, bias=593.0)
-        for b in range(8): mm(w("XB%d" % (b // 4), 64 * (b % 4), 64), w("SEL", 128 * (8 * par + b), 128), v("Xf"), False, b % 4 == 3)
+        if t:
+            act(YP, ix("RM", 1536, w("LL", 8 * t + 4, 4)), scale=2.0, bias=593.0)
+            minus(t - 1)
+        else:
+            needs()
+            ts(YP, ix("RM", 1536, w("LL", 4, 4)), 2.0, Op.mult, 593.0, Op.add)
+        for b in range(8): mm(XB[b], w("SEL", 128 * (8 * par + b), 128), v("Xf"), False, b % 2 == 1)
 
-        def prod(b): return lambda: tt(v("Pc", b, 512, 8), w("XB%d" % (b // 4), 64 * (b % 4), 64), v("Yp"), Op.mult)
+        def prod(b): return lambda: tt(v("Pc", b, 512, 8), XB[b], YP, Op.mult)
         def shift(lo, hi): return lambda: ts(v("Pi", lo, hi), v("Pc", lo, hi), 5, Op.logical_shift_right, W - 1, Op.bitwise_and)
         def conv(lo, hi): return lambda: vc(v("OF", lo, hi), v("Pi", lo, hi))
 
-        weave(strikes("FA", Op.add, "HALF") if t else [], [None, None] + [prod(b) for b in range(8)] + [shift(0, 128), conv(0, 128)])
-        act(v("NB"), need, scale=-1.0, bias=w("cN", 0, 1))
-        act(v("NR"), ix("MM", 64 * t + 64, v("KL"), 64 * t), bias=w("cN", 1, 1))
+        weave(marks(t - 1) if t else [], ([None] * 6 if t == 1 else old[11:]) + [prod(b) for b in range(8)] + [shift(0, 128), conv(0, 128)])
+        if t: needs()
+        else: for_the_sums()
         mm(w("JI", 0, 192), v("ONE"), v("JPRE"), True, False)
-        for h in range(2): mm(w("JI", 96, 32), w("DUP", 256 * par + 128 * h, 128), v("Xf", h, 64, 2), False, False)
+        for h in range(2): mm(w("JI", 64, 32), w("DUP", 256 * par + 128 * h, 128), v("Xf", h, 64, 2), False, False)
         mm(w("JI", 128, 64), w("M2S", 128 * par, 128), v("Xf"), False, False)
-        mm(w("JI", 128, 64), v("ID"), v("CK"), False, False)
+        for h in (0, 128): mm(w("JI", 128, 64), v("ID"), w("CK", h, 64), False, False)
         mm(w("JI", 0, 64), v("I2"), iw, False, False)
-        for h in range(2): mm(w("JI", 64, 32), w("I2h", 128 * h, 128), v("IJ", 128 * t + h, 128 * t + 64, 2), False, False)
+        for h in range(2): mm(w("JI", 96, 32), w("I2h", 128 * h, 128), v("IJ", 128 * t + h, 128 * t + 64, 2), False, False)
         mm(w("JI", 128, 64), v("EI"), iw, False, False)
         mm(w("JI", 128, 64), v("EJ"), jw, False, True)
-        act(v("Y2"), w("JI", 64, 32))
-        if t == 0: for_the_sums()
-        for bank, n in (("K0", 512), ("K1", 256), ("K2", 256)): mm(w(bank, 0, n), v("L3"), v("IDK", 0, n), True, False)
-        for h in range(2): mm(w("D", 256 * h, 256), v("L3"), v("IDK", 0, 512, 2), h == 0, False)
-        mm(w("CB", 0, 320), one1, v("IDK", 0, 320, 1, 1), True, False)
+        act(w("YY", 64, 32), w("JI", 96, 32))
 
-        def slots(q, eng):
-            mine = [15, 13, 11, 9, 7, 5, 3, 1][:NV[q]]
-            return [16 * q + k for k in range(16) if (k in mine) == (eng == "V")]
         def far(q, eng):
+            mine = [15, 13, 11, 9, 7, 5, 3, 1][:PLAN[q].count("g") - (FEWER if t + q == 0 else 0)]
             def one(k):
                 out, src = w("G", 128 * k, 128), ix("FA", W, w("OF", 8 * k, 8))
                 if eng == "S": act(out, src, Act.Relu, bias=w("NB", k, 1))
                 else: ts(out, src, w("NB", k, 1), Op.add, 0.0, Op.max)
-            return [lambda k=k: one(k) for k in slots(q, eng)]
+            return [lambda k=k: one(16 * q + k) for k in range(16) if (k in mine) == (eng == "V")]
         def sums(q, sp, lo=0, hi=16):
-            bank, r = KB[q]
             for a in range(16):
-                mm(k3(bank, r // 16 + a // 8, r // 16 + 16, 2, 2 * a % 16, 2, 8 * lo, 8 * hi),
-                   v("G", 2048 * q + 128 * lo + a, 2048 * q + 128 * hi, 16), v("W16"), False, sp and a == 15)
-        def bits(bank, n, base):
-            return [lambda: ts(w("II", 0, n), v(bank, 0, 2 * n, 2), base, Op.add),
-                    lambda: ts(w("MI", 0, n), w("II", 0, n), MASK, Op.bitwise_and),
-                    lambda: tt(w("UU", 0, n), w("MI", 0, n), v(bank, 1, 2 * n, 2), Op.add)]
-        def keys(bank, q, m):
-            lo, n = 128 * q, 128 * m
-            if t == 0:
-                return bits(bank, n, 8191.0) + [lambda: scan(w("SC", lo, n), w("RSM", 0, n), w("UU", 0, n), Op.max, Op.min)]
-            return bits(bank, n, 8191.0) + [
-                lambda: tt(w("KK", lo, n), w("UU", 0, n), w("D", lo, n), Op.max),
-                lambda: scan(w("SC", lo, n), w("RSM", 0, n), w("KK", lo, n), Op.max, Op.min)]
-        def plus(q, m):
-            low = v("SC", 128 * q + 15, 128 * (q + m), 16)
-            return [lambda: tt(low, low, w("CD", 128 + 8 * q, 8 * m), Op.add)]
+                mm((T["K%d" % q][8 * lo:8 * hi, 4 * (a % 8) + 2 * (a // 8):512:32], [("K%d" % q, 0, 512, 1)]),
+                   v("G", 2048 * q + 128 * lo + a, 2048 * q + 128 * hi, 16), v("WK"), False, sp and a == 15)
+        def keys(q, m):
+            n, on = 128 * m, range(q, q + m)
+            return [lambda c=c: ts(w("II", 128 * (c - q), 128), v("K%d" % c, 0, 256, 2), 8191.0 + 32768.0, Op.add) for c in on] + [
+                lambda: ts(v("MX", 1, 2 * n, 2), w("II", 0, n), MASK, Op.bitwise_and)] + [
+                lambda c=c: scan(w("KK", 256 * c, 256), w("MX", 256 * (c - q), 256), w("K%d" % c, 256, 256), Op.add, Op.max) for c in on]
+        def lowest(q):
+            return [lambda: scan(w("SC", 128 * q, 128), v("RSM"), v("KK", 256 * q + 1, 256 * q + 256, 2), Op.max, Op.min)]
 
         weave(far(0, "S"))
-        tt(w("Pc", 512, 64), w("JI", 0, 64), v("Yp"), Op.mult)
-        tt(w("Pc", 576, 32), w("JI", 96, 32), v("Y2"), Op.mult)
-        weave(far(0, "V"), [shift(128, 608), conv(128, 608)])
+        tt(w("Pc", 512, 96), w("JI", 0, 96), v("YY"), Op.mult)
+        if t: turns(PLAN[0], far(0, "V"), [shift(128, 608), conv(128, 608)])
+        else: weave([shift(128, 608), for_the_lists, conv(128, 608)] + far(0, "V"))
+        for q in range(4): mm(w("K%d" % q, 0, 512), v("L3"), v("IDK", 0, 512), True, False)
+        mm(w("CB", 0, 192), one1, v("IDK", 257, 449, 1, 1), True, False)
         tt(v("G1"), ix("FA", W, w("OF", 512, 64)), v("NR"), Op.max)
         tt(v("G2"), ix("FA", W, w("OF", 576, 32)), v("NR", 0, 1024, 2), Op.max)
         for q in range(4):
-            mm(v(KB[q][0], KB[q][1] + 1, KB[q][1] + 256, 2), v("NR", 256 * q, 256 * q + 256, 2), v("WZ"), False, False)
+            mm(v("K%d" % q, 256, 512, 2), v("NR", 256 * q, 256 * q + 256, 2), v("WZ"), False, False)
         sums(0, False)
-        for a in range(16): mm(k3("CB", a // 8, 16, 2, 2 * a % 16, 2, 0, 64), v("G1", a, 1024, 16), v("W16"), False, False)
-        for q in range(4): mm(w("CB", 256 + 16 * q, 16), w("G2", 128 * q, 128), v("W16"), False, q == 3)
+        for a in range(8): mm(cb(2 * a, 2), v("G1", a, 1024, 8), v("W16"), False, False)
+        for q in range(4): mm(w("CB", 128 + 16 * q, 16), w("G2", 128 * q, 128), v("W16"), False, q == 3)
         weave(far(1, "S"))
-        weave(far(1, "V"), [None] * LEAD[0] + bits("CB", 160, 510.0) + [lambda: ts(v("CD"), w("UU", 0, 160), 0.0, Op.max)])
+        turns(PLAN[1], far(1, "V"), [
+            lambda: ts(w("II", 0, 96), v("CB", 0, 192, 2), 510.0, Op.add), lambda: ts(v("MI"), w("II", 0, 96), MASK, Op.bitwise_and),
+            lambda: tt(v("UU"), v("MI"), v("CB", 1, 192, 2), Op.add), lambda: ts(v("CD"), v("UU"), 0.0, Op.max)])
         sums(1, False)
-        c1 = v("CD", 0, 128, 1, 64)
         for q in range(4):
-            mm(v(KB[q][0], KB[q][1] + 1, KB[q][1] + 256, 2), w("EX", 128 * q, 128), c1, False, q == 1)
-            mm(w("D", 128 * q, 128), w("EX", 128 * q, 128), c1, False, False)
-        for a in range(16):
-            mm(v("D", 384 + a, 512, 16), v("ID"), w("CD", 152, 8), False, a == 15)
-        weave(far(2, "S"))
-        weave(far(2, "V"), [None] * LEAD[1] + keys("K0", 0, 2))
-        for a in range(16): mm(v("K2", 2 * a + 1, 256, 32), v("ID"), w("CD", 152, 8), False, False)
+            for h in range(4): mm(v("K%d" % q, 256 + h, 512, 4), w("EX", 512 * (h // 2) + 128 * q, 128), w("CD", 0, 64), False, h == 3 and q < 2)
+        weave(far(2, "S"), [None] * 4 + [lambda: act(v("CR"), ix("UU", 96, w("KL", 0, 8), 88), Act.Relu)])
+        turns(PLAN[2], far(2, "V"), keys(0, 2))
+        for h in range(2): mm(v("K3", 256 + h, 512, 2), v("ID"), v("CR"), False, False)
         sums(2, True)
         weave(far(3, "S"))
-        weave([None] * LEAD[2] + keys("K1", 2, 1), far(3, "V"))
+        turns(PLAN[3], far(3, "V"), keys(2, 1) + lowest(0))
         for lo, hi in ((0, 8), (8, 12), (12, 16)): sums(3, True, lo, hi)
-        act(w("YM", 64, 64), v("Yp"), bias=-296.5, scale=0.5)
+        act(w("YM", 64, 64), YP, bias=-296.5, scale=0.5)
         act(w("YM", 0, 64), w("JI", 128, 64))
         if t == 0: for_the_choice()
         mm(w("CB", 0, 128), v("ID"), v("YM"), True, False)
@@ -309,71 +316,73 @@ def rank_program(g, core, T, topo):
         mm(w("XB0", 0, 128), one1, v("CNT"), False, False)
         mm(w("XB1", 0, 192), v("ID"), v("TRI"), True, False)
         if not last: mm(w("JI", 256, 128), one1, v("CNT"), True, False)
-        act(w("FA", W, P), need, scale=2.0, bias=-255.0)
-        for lo, names_ in ((15, w("LL", 8 * t + 4, 4)), (207, w("LL", 8 * t, 4))): act(v("ZS", lo, lo + 49, 16), names_, scale=2.0, bias=17.0)
+        act(v("FA", W, W + 4 * P, 4), need, scale=2.0, bias=-255.0)
+        for lo, own in ((15, w("LL", 8 * t + 4, 4)), (207, w("LL", 8 * t, 4))): act(v("ZS", lo, lo + 49, 16), own, scale=2.0, bias=17.0)
 
+        old = strikes(t - 1) if t else twice(1) + for_the_strikes + for_the_costs + [None]
         kf = v("KF", 7, 128, 8)
         def parts():
             ts(v("KF", 135, 256, 8), kf, 48.0, Op.add, -48.0, Op.add)
             ts(v("KF", 263, 384, 8), kf, 1536.0, Op.add, -1536.0, Op.add)
         def spread():
-            mm(w("D", 0, 64), v("ID"), w("NDG", 128, 64), True, False)
+            mm(w("K0", 0, 64), v("ID"), w("NDG", 128, 64), True, False)
             tt(v("TBf"), v("KF", 7, 256, 8), v("KF", 135, 384, 8), Op.subtract)
-            for q in range(4): mm(k3("CB", 0, 8, 1, 4 * q, 4), w("E8", 128 * q, 128), v("TBf"), False, q == 3)
-        old = strikes("YF", Op.mult, "NEG") if t else rows + twice(1) + [None]
-        weave(old[:1], plus(0, 3))
-        turn = v("SC", 3, 512, 4)
-        weave(keys("K2", 3, 1) + [lambda: do("V", g.vector.transpose, v("ST"), [turn], (turn[0],)),
-                                  lambda: scan(w("KF", 0, 128), v("RS8"), v("ST"), Op.max, Op.min), parts, spread], old[1:10])
+            for q in range(4): mm(cb(4 * q, 4), w("E8", 128 * q, 128), v("TBf"), False, q == 3)
+        def turn(lo, n):
+            src = v("SC", 4 * lo + 3, 4 * (lo + n), 4)
+            return lambda: do("V", g.vector.transpose, w("ST", lo, n), [src], (src[0],))
+        def least(lo, n): return lambda: scan(w("KF", lo, n), w("RS8", lo, n), w("ST", lo, n), Op.max, Op.min)
+        low = v("SC", 15, 384, 16)
+        early = [lambda: tt(low, low, w("CD", 64, 24), Op.add), turn(0, 96), least(0, 96)]
+        weave(lowest(1) + old[:1] + lowest(2))
+        weave(keys(3, 1) + lowest(3) + [turn(96, 32), least(96, 32), parts, spread], early + old[1:6])
         act(w("YI", 16 * t, 16), v("KF", 263, 384, 8), scale=8192.0)
-        weave(old[10:11])
+        weave(old[6:7])
         ts(v("UAW"), w("CB", 0, 128), 0.0, Op.max, 4096.0, Op.min)
         def names(bank, o):
             mm(w(bank, o, 64), v("BLK2"), w("UAW", 64, 64), False, False)
             mm(w(bank, o, 64), v("SELJ"), w("UAW", 0, 64), False, False)
             mm(w(bank, o + 64, 64), v("SELW"), w("UAW", 0, 64), False, True)
         names("XB0", 0)
-        mm(w("D", 0, 64), v("SELP"), w("UAW", 0, 64), False, True)
-        for k in range(3): mm(w("XB1", 64 * k, 64), v("SELP"), w("UAW", 0, 64), False, False)
+        mm(w("K0", 0, 64), v("SELP"), w("UAW", 0, 64), False, True)
+        for k in range(3): mm(w("XB1", 64 * k, 64), v("SELQ"), w("UAW", 0, 64), False, False)
         if not last: names("JI", 256)
-        weave(old[11:])
-        scan(w("ZS", 64, 128), w("RSM", 0, 128), w("XB0", 0, 128), Op.max, Op.min)
+        weave(old[7:8])
+        scan(w("ZS", 64, 128), v("RSM"), w("XB0", 0, 128), Op.max, Op.min)
         act(w("LS", 8 * t, 8), v("ZS", 79, 192, 16), scale=0.5, bias=-8.5)
         send("l", t, w("LL", 8 * t + 8, 8), w("LS", 8 * t, 8))
-
-        scan(v("FS"), w("RSM", 0, 64), w("D", 0, 64), Op.max, Op.min)
-        tt(v("PF"), v("ZS", 15, 192, 16), v("ZS", 79, 256, 16), Op.mult)
-        ts(v("FI"), v("PF"), 5, Op.logical_shift_right, W - 1, Op.bitwise_and)
-        act(v("TNh"), v("FI"), bias=-2048.0)
-        for k in (1, 0): tt(v("RT", 64 * k + 15, 64 * k + 64, 16), w("FI", 4 * k, 4), v("FS", 15, 64, 16), Op.max)
-        vc(v("TNf"), v("RT", 79, 128, 16))
-        tt(v("RT", 143, 192, 16), w("FI", 8, 4), v("FS", 15, 64, 16), Op.max)
-        act(w("NS", 64 * t, 64), ix("FA", W + P, v("TNf")), scale=0.5, bias=127.625)
-        vc(v("TNu"), TN)
-        send("n", t, w("MM", 64 * t + 64, 64), w("NS", 64 * t, 64))
         if not last: act(w("IS", 128 * t, 128), w("JI", 256, 128), scale=0.5)
-        if not last: send("i", t, w("IJ", 128 * t + 128, 128), w("IS", 128 * t, 128))
-        act(v("AV"), ix("YF", W + P, v("TNu")), Act.Abs)
+
+        scan(v("FS"), w("RSM", 0, 64), w("K0", 0, 64), Op.max, Op.min)
+        weave([lambda: tt(v("PF"), v("ZS", 15, 192, 16), v("ZS", 79, 256, 16), Op.mult),
+               lambda: ts(v("FI"), v("PF"), 5, Op.logical_shift_right, W - 1, Op.bitwise_and)])
+        act(v("TNh"), v("FI"), bias=-2048.0)
+        for k in (1, 0, 2): tt(w("TNu", 4 * k, 4), w("FI", 4 * k, 4), v("FS", 15, 64, 16), Op.max)
+        act(w("NS", 64 * t, 64), ix("FA", W + 4 * P, w("TNu", 4, 4)), scale=0.5, bias=127.625)
+        send("n", t, w("MM", 64 * t + 64, 64), w("NS", 64 * t, 64))
+        act(v("AV"), ix("FA", W + 4 * P, v("TNu")), bias=127.75)
+        weave(old[8:9], [lambda: vc(TN, v("TNu"))])
+        if last: minus(t)
+        else: send("i", t, w("IJ", 128 * t + 128, 128), w("IS", 128 * t, 128))
         for s in range(15): mm(v("XB1", s, 192, 16), w("DM", 128 * s, 128), v("TNh"), False, s == 14)
-        ts(v("EQ"), w("XB1", 0, 192), 0.0, Op.is_equal, 8192.0, Op.mult)
-        scan(v("FL"), v("RT"), v("EQ"), Op.add, Op.max)
-        ts(v("TS", 0, 24, 2), v("FL", 15, 192, 16), v("cP"), Op.min)
+        weave(old[9:10] + (old[11:] if last else []))
+        ts(v("EQ"), w("XB1", 0, 192), 0.0, Op.is_equal, v("cP"), Op.mult)
+        weave(old[10:11])
+        scan(w("TS", 192 * par, 192), v("RT"), v("EQ"), Op.min, Op.max, BIG)
 
     def costs():
         for k in range(16): mm(v("JI", k, 320, 16, 8), w("SY", 8 * (k // 4), 8), v("YC", k % 4, 80, 4), True, True)
-    weave(strikes("YF", Op.mult, "NEG"), [match(w("SY", 8 * q, 8), v("CI", 3, 32, 4), w("QP", q, 1)) for q in range(4)] + [
+    weave(strikes(RO - 1), [
         lambda: ts(v("YT"), v("YI"), 8192.0, Op.is_ge, -8193.0, Op.mult),
         lambda: tt(v("YC"), v("YI"), v("YT"), Op.add), costs])
-    dma("D", "out", 80, ext(T.yf[:, 0:W - ROT], "yf1"), v("YF", ROT, W))
-    dma("S", "out", 80, ext(T.yf[:, W - ROT:W], "yf2"), v("YF", 0, ROT))
+    landed("l", RO, "LL", 8); landed("n", RO, "MM", 64)
+    affine((w("YPo", 0, 4), w("LL", 44, 4), 1.0, 0.0), (w("YPo", 4, 4), w("LL", 40, 4), 1.0, -float(PAD)), (v("YZo"), w("MM", 320, 64), 1.0, -128.0))
+    dma("S", "out", 80, ext(T.yp[:], "yp"), v("YPo"))
+    dma("S", "out", 80, ext(T.yz[:], "yz"), v("YZo"))
     act(v("YO"), v("JI", 0, 320, 1, 8))
     dma("S", "out", 80, ext(T.yc[:], "yc"), v("YO"))
-    landed("l", RO, "LL", 8); landed("n", RO, "MM", 64)
-    vc(w("YPo", 0, 4), w("LL", 44, 4))
-    ts(w("YPo", 4, 4), w("LL", 40, 4), -float(PAD), Op.add)
-    ts(v("YZo"), w("MM", 320, 64), -128.0, Op.add)
-    dma("D", "out", 80, ext(T.yp[:], "yp"), v("YPo"))
-    dma("D", "out", 80, ext(T.yz[:], "yz"), v("YZo"))
+    dma("D", "out", 80, ext(T.yf[:, 0:W - ROT], "yf1"), v("YF", ROT, W))
+    dma("S", "out", 80, ext(T.yf[:, W - ROT:W], "yf2"), v("YF", 0, ROT))
     wait("P", "ls", sent[0])
     wait("D", "out", 80)
     for q in "VSTP": wait("D", q, cnt[q])

@@ -1,3 +1,4 @@
+import math
 from concourse.mybir import AluOpType as Op, ActivationFunctionType as Act
 
 W, P, RO = 4096, 64, 5
@@ -6,8 +7,10 @@ PAD = 288
 BIG = float(1 << 27)
 UNIT = 2.0 ** -13
 MASK = 3 | 15 << 9
-PLAN = ("gcgcggg", "ggcgcgcgc", "ggggccgcgcc", "gggcgcgcgc")
-FEWER = 1
+PLAN = ("cgcgcgcgcg", "ggcgcgcgc", "gcgggccgcgcc", "gggcgcgcgc")
+MORE = (1, 0, 0, 0)
+HEAD = ("ggggggcccccccccc", "gggccccgccccgccg")
+FILL = (1, 3, 5, 7, 8, 9)
 SCRATCH = {}
 
 
@@ -17,14 +20,15 @@ def _bufs(dtype, text, where="sbuf"):
         SCRATCH[f[0]] = (where, [int(f[2]) if len(f) > 2 else 128, int(f[1])], dtype)
 
 
-_bufs("bfloat16", "FA 4864, YF 4864, ND 64, MM 384, NS 320, AV 192, AY 384, EQ 192, HALF 16, YZo 64, TBf 32, E8 512, OWN 128, CNT 128 1")
-_bufs("bfloat16", "L3 128 3, IDK 640 3, RSM 128, ONE 128 2, XPRE 128 1, JPRE 192 2, DM 2048, EX 1024")
+_bufs("bfloat16", "FA 4864, YF 4864, ND 64, MM 384, NS 320, AV 192, AY 384, HALF 32, ZR 288, TRI 288, Z16 1024, YZo 64, TBf 32, E8 512, OWN 128, CNT 128 1")
+_bufs("bfloat16", "L3 128 3, IDK 640 3, RSM 128, ONE 128 2, XPRE 128 1, JPRE 192 2, EX 1024")
 _bufs("bfloat16", "CI 128, C1 128, C2 128, MS 256, MG 128, M7 128")
 _bufs("int32", "RM 1536, CM 2336, PR 8, PI 1, PB 3, Pc 608, Pi 608, II 256, MI 96, MX 512, PF 12, FI 12")
-_bufs("uint16", "LL 48, LS 40, OF 608, TNu 12, TS 384, RT 192, KL 64")
+_bufs("uint16", "LL 48, LS 40, OF 608, TNu 12, TS 800, RT 288, KL 64")
 _bufs("float16", "G 8192, G1 1024, G2 512, NR 1024, CD 96, CR 128, W16 16, WK 16, WZ 128, IJ 768, IS 640, PRh 8, SEL 2048, DUP 512, M2S 256")
-_bufs("float16", "ID 128, I2 128, I2h 256, EI 128, EJ 128, BLK2 128, SELW 128, SELJ 128, SELP 128, SELQ 128, CK 192, NDG 192, TRI 192, Xf 64, YM 128, UAW 128, TNh 12")
-_bufs("float32", "RC 32, GPf 1, SPf 1, QP 4, SY 32, SQ 16, cW 1, cS 1, cN 2, cH 3, cP 1, cL 2, cK 1, cO 1, ownA 2, ownB 3")
+_bufs("float16", "ID 128, I2 128, I2h 256, EI 128, EJ 128, BLK2 128, SELW 128, SELJ 128, SELP 128, SELQ 128, CK 192, NDG 192, Xf 64, YM 128, UAW 128, TNh 18")
+_bufs("float16", "SELN 128, NI2 128, RQ 288, RR 288, EQ 288, NQ 1024, CQ 128, ZC 128")
+_bufs("float32", "RC 32, GPf 1, SPf 1, QP 4, SY 32, SQ 16, cW 1, cS 1, cN 2, cH 4, cP 2, cL 2, cK 1, cO 1, ownA 2, ownB 3")
 _bufs("float32", "NB 64, YY 96, RS8 128, UU 96, KK 1024, SC 512, ST 128, KF 384, ZS 256, FS 64, YI 80, YT 80, YC 80, YPo 8, YO 320 8")
 _bufs("float32", "XB0 512, XB1 512, JI 512, K0 512, K1 512, K2 512, K3 512", "psum")
 SCRATCH["CB"] = ("psum", [128, 32, 16], "float32")
@@ -64,7 +68,7 @@ def rank_program(g, core, T, topo):
         for (name, lo, hi, st), write in acc:
             bank = SCRATCH[name][0] == "psum" if name in SCRATCH else False
             for a in hist.get(name, []):
-                apart = a[1] <= lo or hi <= a[0] or (a[2] == st > 1 and (a[0] - lo) % st)
+                apart = a[1] <= lo or hi <= a[0] or (a[0] - lo) % math.gcd(a[2], st)
                 if bank and a[3] != q: apart = False
                 elif not (write or a[5]) or (q == a[3] == "T"): continue
                 if not apart: need[a[3]] = max(need.get(a[3], 0), a[4])
@@ -91,6 +95,7 @@ def rank_program(g, core, T, topo):
         do("V", g.vector.tensor_scalar, out, [a] + [s for s in (s1, s2) if col(s)],
            (a[0], s1[0] if col(s1) else s1, s2[0] if col(s2) else s2, op0) + ((op1,) if op1 else ()))
     def scan(out, d0, d1, op0, op1, first=0.0): do("V", g.vector.tensor_tensor_scan, out, [d0, d1], (d0[0], d1[0], first, op0, op1))
+    def carry(out, keep, a): scan(out, keep, a, Op.mult, Op.add)
     def act(out, a, f=Act.Identity, bias=0.0, scale=1.0):
         do("S", g.scalar.activation, out, [a] + [s for s in (bias, scale) if col(s)], (a[0], f),
            bias=bias[0] if col(bias) else bias, scale=scale[0] if col(scale) else scale)
@@ -105,6 +110,7 @@ def rank_program(g, core, T, topo):
     def turns(plan, gathers, calls):
         lists = {"g": list(gathers), "c": list(calls)}
         for x in plan: lists[x].pop(0)()
+        weave(lists["g"])
 
     sent = [0]
 
@@ -146,6 +152,12 @@ def rank_program(g, core, T, topo):
     iota("QP", [[-32, 4]], 0, 1)
     iota("E8", [[0, 256], [-2, 2]], 1, 0)
     pick("E8", "E8", [[-32, 4], [-4, 8], [0, 16]], Op.is_equal, 0.0, -3, 1)
+    iota("ZR", [[0, 288]], 1, 0)
+    iota(w("TRI", 0, 96), [[0, 6], [1, 16]], 0, 0)
+    iota(v("TRI", 96), [[0, 6], [-16, 2], [1, 16]], 16, 0)
+    for lo, hi, st in ((0, 96, 16), (15, 96, 16), (96, 288, 32), (127, 288, 32)): iota(v("ZR", lo, hi, st), [[0, 6]], 0, 0)
+    iota("Z16", [[0, 1024]], 1, 0)
+    iota(v("Z16", 0, 1024, 16), [[0, 64]], 0, 0)
     SP, GP_, PI = v("SPf"), v("GPf"), w("RC", 0, 1)
     def match(out, pattern, c, k=1.0): return lambda: ts(out, pattern, c, Op.is_equal, k, Op.mult)
     def twice(p):
@@ -163,10 +175,10 @@ def rank_program(g, core, T, topo):
     match(v("SQ"), w("CI", 0, 16), SP)()
     fill(v("JPRE", 96, 128, 1, 1), 592.0)
     fill(v("CM", 0, PAD), 0)
+    fill(v("CQ"), 0.0)
     for s in range(8):
         ts(w("SEL", 128 * s, 128), v("BLK2"), row(s), Op.mult)
         act(w("SEL", 128 * s + 1024, 128), v("BLK2"), scale=row(s + 8))
-    pick("DM", "SEL", [[0, 16], [-16, 8], [-1, 16]], Op.not_equal, -2.0, 0, 1)
     vc(v("KL"), w("CI", 0, 64))
     vc(v("PRh"), v("PR"))
     ts(w("LL", 0, 4), w("PR", 0, 4), float(PAD), Op.add)
@@ -179,6 +191,7 @@ def rank_program(g, core, T, topo):
     ts(w("CK", 128, 64), w("MS", 0, 64), 15.0, Op.not_equal, row(12), Op.mult)
     for name, c in (("ID", 1.0), ("I2", 2.0)): match(v(name), v("CI"), PI, c)()
     ts(w("CK", 0, 64), w("CK", 64, 64), row(14), Op.mult)
+    ts(v("ZC"), w("MS", 0, 128), 1.0, Op.min)
     weave([match(v("EI"), v("CI"), PI, row(8)), match(v("EJ"), v("CI"), PI, row(10))] + twice(0) + [
         match(w("I2h", 128 * h, 128), v("C2"), w("RC", 16 * h, 1), 2.0) for h in range(2)])
     for out in (v("W16", 0, 16, 2), w("WK", 0, 8)): match(out, w("CI", 0, 8), GP_, v("cS"))()
@@ -194,9 +207,7 @@ def rank_program(g, core, T, topo):
         ts(w("ownB", 0, 1), SP, 8.0, Op.min, -4096.0, Op.mult)
         ts(v("cW"), SP, 8.0, Op.is_le)
         ts(w("NDG", 128, 64), w("MS", 0, 64), SP, Op.not_equal, 16384.0, Op.mult)
-        ts(v("TRI"), w("MS", 0, 192), SP, Op.is_ge, 16384.0, Op.mult)
         for h, c in ((0, 593.0), (1, 17.0)): ts(w("NDG", 64 * h, 64), w("NDG", 128, 64), c, Op.max)
-        ts(v("TRI", 15, 192, 16), w("CI", 0, 12), 0.0, Op.mult)
 
     def for_the_choice():
         affine((v("cO"), w("PB", 2, 1), -2.0, 1.0), (w("FA", W, 4 * P), w("MS", 0, 4 * P), 0.0, 1.0),
@@ -207,22 +218,26 @@ def rank_program(g, core, T, topo):
                (w("OWN", 0, 64), w("CI", 0, 64), 0.0, w("ownB", 2, 1)), (w("OWN", 64, 64), w("CI", 0, 64), 0.0, w("ownA", 1, 1)),
                (v("E8"), v("E8"), 2.0 ** 34, 0.0), (w("cH", 1, 1), row(14), 2.0, 0.0), (w("cH", 2, 1), row(12), 8192.0, 0.0),
                (v("cK"), row(12), W / 2, w("cH", 1, 1)), (v("SELW"), v("BLK2"), v("cW"), 0.0), (v("SELJ"), v("BLK2"), row(10), 0.0),
-               (v("SELP"), v("BLK2"), v("cK"), 0.0), (v("SELQ"), v("BLK2"), w("cH", 2, 1), 0.0))
+               (v("SELP"), v("BLK2"), v("cK"), 0.0), (v("SELQ"), v("BLK2"), w("cH", 2, 1), 0.0),
+               (w("cH", 3, 1), row(9), -2.0, 0.0), (v("NI2"), v("I2"), -1.0, 0.0), (v("SELN"), v("BLK2"), w("cH", 3, 1), 0.0))
 
-    for_the_strikes = [lambda: fill(v("RT"), 65535), lambda: ts(w("cH", 0, 1), row(0), 0.5, Op.mult, -128.0, Op.add),
-                       lambda: ts(v("cP"), SP, 32.0, Op.mult, W + 256.0, Op.add),
-                       lambda: ts(v("HALF"), w("CI", 0, 16), 0.0, Op.mult, w("cH", 0, 1), Op.add)]
+    for_the_strikes = [lambda: ts(v("TRI"), v("TRI"), SP, Op.is_ge, 16384.0, Op.mult),
+                       lambda: [ts(v("TRI", lo, hi, st), w("CI", 0, 6), 0.0, Op.mult) for lo, hi, st in ((15, 96, 16), (127, 288, 32))]]
+    for_the_strikes += twice(1) + [
+        lambda: [fill(v("RT"), 65535), fill(v("RQ"), 0.0)], lambda: ts(w("cH", 0, 1), row(0), 0.5, Op.mult, -128.0, Op.add),
+        lambda: [ts(w("cP", h, 1), SP, 32.0, Op.mult, W + 256.0 + 16 * h, Op.add) for h in range(2)],
+        lambda: ts(v("HALF"), w("CI", 0, 32), 0.0, Op.mult, w("cH", 0, 1), Op.add), lambda: fill(v("NQ"), 0.0),
+        lambda: weave([match(w("SY", 8 * q, 8), v("CI", 3, 32, 4), w("QP", q, 1)) for q in range(4)])]
 
-    for_the_costs = [match(w("SY", 8 * q, 8), v("CI", 3, 32, 4), w("QP", q, 1)) for q in range(4)]
-
+    def lists(t, c): return w("TS", 400 * (t % 2) + 64 * c + 60, 2)
     def marks(t):
-        return [lambda c=c: tt(ix("FA", W + 768, w("TS", 192 * (t % 2) + 16 * c + 14, 1)), w("AV", 16 * c, 16), v("HALF"), Op.add) for c in range(12)]
+        return [lambda c=c: tt(ix("FA", W + 768, lists(t, c)), w("AV", 32 * c, 32), v("HALF"), Op.add) for c in range(6)]
     def minus(t): act(w("AY", 192 * (t % 2), 192), v("AV"), scale=-1.0, bias=128.0)
     def strikes(t):
-        return [lambda c=c: vc(ix("YF", W + 768, w("TS", 192 * (t % 2) + 16 * c + 14, 1)), w("AY", 192 * (t % 2) + 16 * c, 16)) for c in range(12)]
+        return [lambda c=c: vc(ix("YF", W + 768, lists(t, c)), w("AY", 192 * (t % 2) + 32 * c, 32)) for c in range(6)]
 
     one1 = v("ONE", 0, 128, 1, 1)
-    TN, YP, old = v("RT", 0, 192, 16), w("YY", 0, 64), []
+    YP = w("YY", 0, 64)
     for t in range(RO):
         par, last = t % 2, t == RO - 1
         jw, iw = w("IJ", 128 * t, 64), w("IJ", 128 * t + 64, 64)
@@ -230,9 +245,6 @@ def rank_program(g, core, T, topo):
         if t:
             landed("l", t, "LL", 8); landed("i", t, "IJ", 128); landed("n", t, "MM", 64)
 
-        def needs():
-            act(v("NB"), need, scale=-1.0, bias=w("cN", 0, 1))
-            act(v("NR"), ix("MM", 64 * t + 64, v("KL"), 64 * t), bias=w("cN", 1, 1))
         XB = [w(bank, 64 * h, 64) for bank in ("XB0", "K1", "K2", "XB1") for h in range(2)]
         for bank in ("XB0", "K1", "K2", "XB1"): mm(w(bank, 0, 128), one1, v("XPRE"), True, False)
         act(v("Xf"), ix("CM", PAD + 2048, w("LL", 8 * t, 4)))
@@ -240,7 +252,8 @@ def rank_program(g, core, T, topo):
             act(YP, ix("RM", 1536, w("LL", 8 * t + 4, 4)), scale=2.0, bias=593.0)
             minus(t - 1)
         else:
-            needs()
+            act(v("NB"), need, scale=-1.0, bias=w("cN", 0, 1))
+            act(v("NR"), ix("MM", 64, v("KL")), bias=w("cN", 1, 1))
             ts(YP, ix("RM", 1536, w("LL", 4, 4)), 2.0, Op.mult, 593.0, Op.add)
         for b in range(8): mm(XB[b], w("SEL", 128 * (8 * par + b), 128), v("Xf"), False, b % 2 == 1)
 
@@ -248,9 +261,14 @@ def rank_program(g, core, T, topo):
         def shift(lo, hi): return lambda: ts(v("Pi", lo, hi), v("Pc", lo, hi), 5, Op.logical_shift_right, W - 1, Op.bitwise_and)
         def conv(lo, hi): return lambda: vc(v("OF", lo, hi), v("Pi", lo, hi))
 
-        weave(marks(t - 1) if t else [], ([None] * 6 if t == 1 else old[11:]) + [prod(b) for b in range(8)] + [shift(0, 128), conv(0, 128)])
-        if t: needs()
-        else: for_the_sums()
+        if t:
+            turns(HEAD[t > 1], marks(t - 1), [prod(b) for b in range(8)] + [shift(0, 128), shift(128, 512)])
+            act(v("NB"), need, scale=-1.0, bias=w("cN", 0, 1))
+            act(v("NQ", 0, 1024, 16), need, bias=w("cN", 1, 1))
+            for lo, hi in ((0, 128), (128, 512)): act(v("OF", lo, hi), v("Pi", lo, hi))
+        else:
+            weave([prod(b) for b in range(8)] + [shift(0, 128), conv(0, 128)])
+            for_the_sums()
         mm(w("JI", 0, 192), v("ONE"), v("JPRE"), True, False)
         for h in range(2): mm(w("JI", 64, 32), w("DUP", 256 * par + 128 * h, 128), v("Xf", h, 64, 2), False, False)
         mm(w("JI", 128, 64), w("M2S", 128 * par, 128), v("Xf"), False, False)
@@ -259,10 +277,10 @@ def rank_program(g, core, T, topo):
         for h in range(2): mm(w("JI", 96, 32), w("I2h", 128 * h, 128), v("IJ", 128 * t + h, 128 * t + 64, 2), False, False)
         mm(w("JI", 128, 64), v("EI"), iw, False, False)
         mm(w("JI", 128, 64), v("EJ"), jw, False, True)
-        act(w("YY", 64, 32), w("JI", 96, 32))
+        if t == 0: act(w("YY", 64, 32), w("JI", 96, 32))
 
         def far(q, eng):
-            mine = [15, 13, 11, 9, 7, 5, 3, 1][:PLAN[q].count("g") - (FEWER if t + q == 0 else 0)]
+            mine = [15, 13, 11, 9, 7, 5, 3, 1][:PLAN[q].count("g") + (MORE[q] if t else 0)]
             def one(k):
                 out, src = w("G", 128 * k, 128), ix("FA", W, w("OF", 8 * k, 8))
                 if eng == "S": act(out, src, Act.Relu, bias=w("NB", k, 1))
@@ -281,9 +299,10 @@ def rank_program(g, core, T, topo):
             return [lambda: scan(w("SC", 128 * q, 128), v("RSM"), v("KK", 256 * q + 1, 256 * q + 256, 2), Op.max, Op.min)]
 
         weave(far(0, "S"))
-        tt(w("Pc", 512, 96), w("JI", 0, 96), v("YY"), Op.mult)
-        if t: turns(PLAN[0], far(0, "V"), [shift(128, 608), conv(128, 608)])
-        else: weave([shift(128, 608), for_the_lists, conv(128, 608)] + far(0, "V"))
+        def near(): tt(w("Pc", 512, 96), w("JI", 0, 96), v("YY"), Op.mult)
+        if t: turns(PLAN[0], far(0, "V"), [lambda: carry(v("NR"), v("Z16"), v("NQ")), lambda: vc(w("YY", 64, 32), w("JI", 96, 32)),
+                                           near, shift(512, 608), conv(512, 608)])
+        else: weave([near, shift(128, 608), for_the_lists, conv(128, 608)] + far(0, "V"))
         for q in range(4): mm(w("K%d" % q, 0, 512), v("L3"), v("IDK", 0, 512), True, False)
         mm(w("CB", 0, 192), one1, v("IDK", 257, 449, 1, 1), True, False)
         tt(v("G1"), ix("FA", W, w("OF", 512, 64)), v("NR"), Op.max)
@@ -296,12 +315,13 @@ def rank_program(g, core, T, topo):
         weave(far(1, "S"))
         turns(PLAN[1], far(1, "V"), [
             lambda: ts(w("II", 0, 96), v("CB", 0, 192, 2), 510.0, Op.add), lambda: ts(v("MI"), w("II", 0, 96), MASK, Op.bitwise_and),
-            lambda: tt(v("UU"), v("MI"), v("CB", 1, 192, 2), Op.add), lambda: ts(v("CD"), v("UU"), 0.0, Op.max)])
+            lambda: tt(v("UU"), v("MI"), v("CB", 1, 192, 2), Op.add),
+            lambda: [ts(v("CD"), v("UU"), 0.0, Op.max), ts(v("CQ", 0, 128, 16), w("UU", 88, 8), 0.0, Op.max)]])
         sums(1, False)
         for q in range(4):
             for h in range(4): mm(v("K%d" % q, 256 + h, 512, 4), w("EX", 512 * (h // 2) + 128 * q, 128), w("CD", 0, 64), False, h == 3 and q < 2)
-        weave(far(2, "S"), [None] * 4 + [lambda: act(v("CR"), ix("UU", 96, w("KL", 0, 8), 88), Act.Relu)])
-        turns(PLAN[2], far(2, "V"), keys(0, 2))
+        weave(far(2, "S"))
+        turns(PLAN[2], far(2, "V"), [lambda: carry(v("CR"), v("ZC"), v("CQ"))] + keys(0, 2))
         for h in range(2): mm(v("K3", 256 + h, 512, 2), v("ID"), v("CR"), False, False)
         sums(2, True)
         weave(far(3, "S"))
@@ -314,18 +334,19 @@ def rank_program(g, core, T, topo):
         mm(w("CB", 0, 128), v("ID"), v("OWN"), False, False)
         mm(w("XB0", 0, 128), v("ID"), w("NDG", 0, 128), True, False)
         mm(w("XB0", 0, 128), one1, v("CNT"), False, False)
-        mm(w("XB1", 0, 192), v("ID"), v("TRI"), True, False)
+        if t: mm(w("XB1", 0, 288), v("ID"), v("TRI"), True, False)
         if not last: mm(w("JI", 256, 128), one1, v("CNT"), True, False)
         act(v("FA", W, W + 4 * P, 4), need, scale=2.0, bias=-255.0)
         for lo, own in ((15, w("LL", 8 * t + 4, 4)), (207, w("LL", 8 * t, 4))): act(v("ZS", lo, lo + 49, 16), own, scale=2.0, bias=17.0)
 
-        old = strikes(t - 1) if t else twice(1) + for_the_strikes + for_the_costs + [None]
+        old = [strikes(t - 1)[FILL.index(n)] if n in FILL else None for n in range(11)] if t else for_the_strikes
         kf = v("KF", 7, 128, 8)
         def parts():
             ts(v("KF", 135, 256, 8), kf, 48.0, Op.add, -48.0, Op.add)
             ts(v("KF", 263, 384, 8), kf, 1536.0, Op.add, -1536.0, Op.add)
         def spread():
             mm(w("K0", 0, 64), v("ID"), w("NDG", 128, 64), True, False)
+            if t == 0: mm(w("XB1", 0, 288), v("ID"), v("TRI"), True, False)
             tt(v("TBf"), v("KF", 7, 256, 8), v("KF", 135, 384, 8), Op.subtract)
             for q in range(4): mm(cb(4 * q, 4), w("E8", 128 * q, 128), v("TBf"), False, q == 3)
         def turn(lo, n):
@@ -345,8 +366,10 @@ def rank_program(g, core, T, topo):
             mm(w(bank, o + 64, 64), v("SELW"), w("UAW", 0, 64), False, True)
         names("XB0", 0)
         mm(w("K0", 0, 64), v("SELP"), w("UAW", 0, 64), False, True)
-        for k in range(3): mm(w("XB1", 64 * k, 64), v("SELQ"), w("UAW", 0, 64), False, False)
         if not last: names("JI", 256)
+        for n in range(6):
+            for o, sel, c in ((16 * n, "SELQ", 0), (96 + 32 * n, "SELN", 0), (112 + 32 * n, "SELQ", 1)):
+                mm(w("XB1", o, 16), v(sel), w("UAW", 32 * (n % 2) + 16 * c, 16), False, False)
         weave(old[7:8])
         scan(w("ZS", 64, 128), v("RSM"), w("XB0", 0, 128), Op.max, Op.min)
         act(w("LS", 8 * t, 8), v("ZS", 79, 192, 16), scale=0.5, bias=-8.5)
@@ -356,19 +379,28 @@ def rank_program(g, core, T, topo):
         scan(v("FS"), w("RSM", 0, 64), w("K0", 0, 64), Op.max, Op.min)
         weave([lambda: tt(v("PF"), v("ZS", 15, 192, 16), v("ZS", 79, 256, 16), Op.mult),
                lambda: ts(v("FI"), v("PF"), 5, Op.logical_shift_right, W - 1, Op.bitwise_and)])
-        act(v("TNh"), v("FI"), bias=-2048.0)
-        for k in (1, 0, 2): tt(w("TNu", 4 * k, 4), w("FI", 4 * k, 4), v("FS", 15, 64, 16), Op.max)
+        act(v("TNh", 6), v("FI"), bias=-2048.0)
+        act(w("TNh", 0, 6), v("FI", 0, 12, 2), bias=-2048.0)
+        def target(k): tt(w("TNu", 4 * k, 4), w("FI", 4 * k, 4), v("FS", 15, 64, 16), Op.max)
+        target(1)
+        for h, out in enumerate((v("RQ", 0, 96, 16), v("RQ", 96, 288, 32))): ts(out, v("FI", h, 12, 2), -2048.0, Op.add)
+        target(0); target(2)
+        carry(v("RR"), v("ZR"), v("RQ"))
         act(w("NS", 64 * t, 64), ix("FA", W + 4 * P, w("TNu", 4, 4)), scale=0.5, bias=127.625)
         send("n", t, w("MM", 64 * t + 64, 64), w("NS", 64 * t, 64))
         act(v("AV"), ix("FA", W + 4 * P, v("TNu")), bias=127.75)
-        weave(old[8:9], [lambda: vc(TN, v("TNu"))])
+        for h, out in enumerate((v("RT", 0, 96, 16), v("RT", 96, 288, 32))): vc(out, v("TNu", h, 12, 2))
+        weave(old[8:9])
         if last: minus(t)
         else: send("i", t, w("IJ", 128 * t + 128, 128), w("IS", 128 * t, 128))
-        for s in range(15): mm(v("XB1", s, 192, 16), w("DM", 128 * s, 128), v("TNh"), False, s == 14)
-        weave(old[9:10] + (old[11:] if last else []))
-        ts(v("EQ"), w("XB1", 0, 192), 0.0, Op.is_equal, v("cP"), Op.mult)
+        for s in range(15): mm(v("XB1", s, 288, 16), w("SEL", 128 * s, 128), v("TNh"), False, False)
+        mm(v("XB1", 111, 288, 32), w("SEL", 128 * 15, 128), v("TNh", 6, 18, 2), False, False)
+        mm(w("XB1", 0, 288), v("NI2"), v("RR"), False, True)
+        weave(old[9:10])
+        for h, (lo, n) in enumerate(((0, 96), (96, 192))): ts(w("EQ", lo, n), w("XB1", lo, n), 0.0, Op.is_equal, w("cP", h, 1), Op.mult)
         weave(old[10:11])
-        scan(w("TS", 192 * par, 192), v("RT"), v("EQ"), Op.min, Op.max, BIG)
+        scan(v("TS", 400 * par + 4, 400 * par + 388, 4), w("RT", 0, 96), w("EQ", 0, 96), Op.min, Op.max, BIG)
+        scan(v("TS", 400 * par + 1, 400 * par + 385, 2), v("RT", 96), v("EQ", 96), Op.min, Op.max, BIG)
 
     def costs():
         for k in range(16): mm(v("JI", k, 320, 16, 8), w("SY", 8 * (k // 4), 8), v("YC", k % 4, 80, 4), True, True)
@@ -376,13 +408,13 @@ def rank_program(g, core, T, topo):
         lambda: ts(v("YT"), v("YI"), 8192.0, Op.is_ge, -8193.0, Op.mult),
         lambda: tt(v("YC"), v("YI"), v("YT"), Op.add), costs])
     landed("l", RO, "LL", 8); landed("n", RO, "MM", 64)
+    dma("D", "out", 80, ext(T.yf[:, 0:W - ROT], "yf1"), v("YF", ROT, W))
+    dma("D", "out", 80, ext(T.yf[:, W - ROT:W], "yf2"), v("YF", 0, ROT))
     affine((w("YPo", 0, 4), w("LL", 44, 4), 1.0, 0.0), (w("YPo", 4, 4), w("LL", 40, 4), 1.0, -float(PAD)), (v("YZo"), w("MM", 320, 64), 1.0, -128.0))
     dma("S", "out", 80, ext(T.yp[:], "yp"), v("YPo"))
     dma("S", "out", 80, ext(T.yz[:], "yz"), v("YZo"))
     act(v("YO"), v("JI", 0, 320, 1, 8))
     dma("S", "out", 80, ext(T.yc[:], "yc"), v("YO"))
-    dma("D", "out", 80, ext(T.yf[:, 0:W - ROT], "yf1"), v("YF", ROT, W))
-    dma("S", "out", 80, ext(T.yf[:, W - ROT:W], "yf2"), v("YF", 0, ROT))
     wait("P", "ls", sent[0])
     wait("D", "out", 80)
     for q in "VSTP": wait("D", q, cnt[q])

import math
from concourse.mybir import AluOpType as Op, ActivationFunctionType as Act

W, P, RO = 4096, 64, 5
ROT = 315
PAD = 288
BIG = float(1 << 27)
UNIT = 2.0 ** -13
MASK = 3 | 15 << 9
PLAN = ("cgcgcgcgcg", "ggcgcgcgc", "gcgggccgcgcc", "gggcgcgcgc")
MORE = (1, 0, 0, 0)
HEAD = ("ggggggcccccccccc", "gggccccgccccgccg")
FILL = (1, 3, 5, 7, 8, 9)
SCRATCH = {}


def _bufs(dtype, text, where="sbuf"):
    for item in text.split(","):
        f = item.split()
        SCRATCH[f[0]] = (where, [int(f[2]) if len(f) > 2 else 128, int(f[1])], dtype)


_bufs("bfloat16", "FA 4864, YF 4864, ND 64, MM 384, NS 320, AV 192, AY 384, HALF 32, ZR 288, TRI 288, Z16 1024, YZo 64, TBf 32, E8 512, OWN 128, CNT 128 1")
_bufs("bfloat16", "L3 128 3, IDK 640 3, RSM 128, ONE 128 2, XPRE 128 1, JPRE 192 2, EX 1024")
_bufs("bfloat16", "CI 128, C1 128, C2 128, MS 256, MG 128, M7 128")
_bufs("int32", "RM 1536, CM 2336, PR 8, PI 1, PB 3, Pc 608, Pi 608, II 256, MI 96, MX 512, PF 12, FI 12")
_bufs("uint16", "LL 48, LS 40, OF 608, TNu 12, TS 800, RT 288, KL 64")
_bufs("float16", "G 8192, G1 1024, G2 512, NR 1024, CD 96, CR 128, W16 16, WK 16, WZ 128, IJ 768, IS 640, PRh 8, SEL 2048, DUP 512, M2S 256")
_bufs("float16", "ID 128, I2 128, I2h 256, EI 128, EJ 128, BLK2 128, SELW 128, SELJ 128, SELP 128, SELQ 128, CK 192, NDG 192, Xf 64, YM 128, UAW 128, TNh 18")
_bufs("float16", "SELN 128, NI2 128, RQ 288, RR 288, EQ 288, NQ 1024, CQ 128, ZC 128")
_bufs("float32", "RC 32, GPf 1, SPf 1, QP 4, SY 32, SQ 16, cW 1, cS 1, cN 2, cH 4, cP 2, cL 2, cK 1, cO 1, ownA 2, ownB 3")
_bufs("float32", "NB 64, YY 96, RS8 128, UU 96, KK 1024, SC 512, ST 128, KF 384, ZS 256, FS 64, YI 80, YT 80, YC 80, YPo 8, YO 320 8")
_bufs("float32", "XB0 512, XB1 512, JI 512, K0 512, K1 512, K2 512, K3 512", "psum")
SCRATCH["CB"] = ("psum", [128, 32, 16], "float32")
SEMAPHORES = ["sV", "sS", "sT", "sP", "ls", "out"] + ["ld%d" % k for k in range(9)] + ["%s%d" % (m, t) for m in "lin" for t in range(1, RO + 1)]


def rank_program(g, core, T, topo):
    rank = T.rank_of(core)
    if rank is None:
        return
    n_ranks = len(T.cores)
    QS = {"V": g.vector, "S": g.scalar, "T": g.tensor, "P": g, "D": g.sync}
    cnt = {q: 0 for q in "VSTP"}
    known = {q: {} for q in QS}
    snaps = {}
    hist = {}

    def v(name, lo=0, hi=None, st=1, r=None):
        if len(SCRATCH[name][1]) == 3:
            return T[name][:, lo // 16:hi // 16, lo % 16:16:st], [(name, lo, hi, st)]
        hi = SCRATCH[name][1][1] if hi is None else hi
        return T[name][0:(r or SCRATCH[name][1][0]), lo:hi:st], [(name, lo, hi, st)]
    def w(name, lo, n): return v(name, lo, lo + n)
    def ix(name, hi, lst, lo=0): return T[name][:, lo:hi].indirect(lst[0]), [(name, lo, hi, 1)] + lst[1]
    def cb(c, n): return T.CB[:, 0:8, c:c + n], [("CB", 0, 512, 1)]
    def ext(ap, name=None): return ap, [(name, 0, 1, 1)] if name else []

    def wait(q, ev, n):
        if known[q].get(ev, 0) < n:
            QS[q].wait_ge(T.sem["s" + ev if ev in cnt else ev], n)
            known[q][ev] = n
            for e2, n2 in snaps.get((ev, n), {}).items(): known[q][e2] = max(known[q].get(e2, 0), n2)

    def order(q, rd, wr, ev, n):
        need = {}
        acc = [(x, False) for o in rd for x in o[1]] + [(x, True) for x in wr[1]]
        for (name, lo, hi, st), write in acc:
            bank = SCRATCH[name][0] == "psum" if name in SCRATCH else False
            for a in hist.get(name, []):
                apart = a[1] <= lo or hi <= a[0] or (a[0] - lo) % math.gcd(a[2], st)
                if bank and a[3] != q: apart = False
                elif not (write or a[5]) or (q == a[3] == "T"): continue
                if not apart: need[a[3]] = max(need.get(a[3], 0), a[4])
        for e, c in sorted(need.items(), key=lambda x: (x[0] == q, x[0])): wait(q, e, c)
        snaps[(ev, n)] = dict(known[q])
        for (name, lo, hi, st), write in acc:
            bank = SCRATCH[name][0] == "psum" if name in SCRATCH else False
            hist[name] = [a for a in hist.get(name, []) if not ((bank and a[3] != q) or (lo <= a[0] and a[1] <= hi and a[2] % st == 0 and (a[0] - lo) % st == 0 and (write or (a[3] == ev and not a[5]))))]
            hist[name].append([lo, hi, st, ev, n, write])

    def do(q, fn, out, ins, args, **kw):
        order(q, ins + [(None, out[1][1:])], (None, out[1][:1]), q, cnt[q] + 1)
        cnt[q] += 1
        fn(out[0], *args, **kw).then_inc(T.sem["s" + q], 1)

    def dma(q, ev, n, out, in_, **kw):
        order(q, [in_], out, ev, n)
        QS[q].dma_start(out[0], in_[0], **kw).then_inc(T.sem[ev], 16)

    def col(x): return isinstance(x, tuple)
    def vc(out, a): do("V", g.vector.tensor_copy, out, [a], (a[0],))
    def tt(out, a, b, op): do("V", g.vector.tensor_tensor, out, [a, b], (a[0], b[0], op))
    def ts(out, a, s1, op0, s2=None, op1=None):
        do("V", g.vector.tensor_scalar, out, [a] + [s for s in (s1, s2) if col(s)],
           (a[0], s1[0] if col(s1) else s1, s2[0] if col(s2) else s2, op0) + ((op1,) if op1 else ()))
    def scan(out, d0, d1, op0, op1, first=0.0): do("V", g.vector.tensor_tensor_scan, out, [d0, d1], (d0[0], d1[0], first, op0, op1))
    def carry(out, keep, a): scan(out, keep, a, Op.mult, Op.add)
    def act(out, a, f=Act.Identity, bias=0.0, scale=1.0):
        do("S", g.scalar.activation, out, [a] + [s for s in (bias, scale) if col(s)], (a[0], f),
           bias=bias[0] if col(bias) else bias, scale=scale[0] if col(scale) else scale)
    def mm(out, l, r, st, sp): do("T", g.tensor.matmul, out, [l, r], (l[0], r[0], st, sp))
    def fill(out, c): do("V", g.vector.memset, out, [], (c,))
    def iota(out, pattern, base, cm): do("P", g.iota, out if col(out) else v(out), [], (pattern, base, cm), allow_small_or_imprecise_dtypes=True)
    def pick(name, src, pattern, op, other, base, cm): do("P", g.affine_select, v(name), [v(src)], (T[src][:], pattern, op, other, base, cm))
    def weave(first, second=()):
        for n in range(max(len(first), len(second))):
            for calls in (first, second):
                if n < len(calls) and calls[n]: calls[n]()
    def turns(plan, gathers, calls):
        lists = {"g": list(gathers), "c": list(calls)}
        for x in plan: lists[x].pop(0)()
        weave(lists["g"])

    sent = [0]

    def send(what, t, out, in_):
        dst = T.cores[(rank + 1 + t % 3) % n_ranks]
        eng = topo.engines(core, dst)[:8]
        sent[0] += len(eng)
        order("P", [in_], ext(None), "ls", sent[0])
        rid, pid, _ = topo.addr(dst)
        g.remote_dma(out[0], in_[0], T.sem["%s%d" % (what, t + 1)], T.sem.ls, pid, rid, sum(1 << e for e in eng))

    def landed(what, t, name, n):
        src = T.cores[(rank - 1 - (t - 1) % 3) % n_ranks]
        hist.setdefault(name, []).append([n * t, n * t + n, 1, "%s%d" % (what, t), len(topo.engines(src, core)[:8]), True])

    dma("D", "ld0", 16, w("PR", 0, 4), ext(T.pcol[:]))
    dma("S", "ld1", 16, w("PR", 4, 4), ext(T.prow[:]))
    dma("D", "ld2", 16, v("ND"), ext(T.need[:]))
    dma("S", "ld3", 16, v("CM", PAD), ext(T.cmate[:]))
    dma("D", "ld4", 16, v("RM"), ext(T.rmate[:]))
    for k, name, q in ((5, "FA", "S"), (7, "YF", "D")):
        if name == "YF": wait("D", "ld5", 16)
        dma("D", "ld%d" % k, 16, v(name, ROT, W), ext(T.fig[:, 0:W - ROT]))
        dma(q, "ld%d" % (k + 1), 16, v(name, 0, ROT), ext(T.fig[:, W - ROT:W]))

    do("P", g.iota, v("PI"), [], ([[0, 1]], 0, 1))
    iota("RC", [[128, 2], [-1, 16]], 0, 1)
    iota("MG", [[1, 8], [0, 16]], 0, 0)
    iota("CI", [[1, 128]], 0, 0)
    iota("MS", [[0, 16], [1, 16]], 0, 0)
    iota("C1", [[16, 8], [128, 2], [1, 8]], 0, 0)
    iota("C2", [[16, 8], [136, 2], [1, 8]], 0, 0)
    iota("M7", [[0, 16], [1, 8]], 0, 0)
    for h in range(2): iota(v("IDK", h, 640, 2), [[0, 20], [8, 8], [64, 2]], 0, 8)
    for lo, hi, st, c in ((0, 256, 1, -32768), (256, 640, 2, -2), (257, 640, 2, 0)): iota(v("IDK", lo, hi, st, 1), [[0, len(range(lo, hi, st))]], c, 0)
    iota(v("MX", 0, 512, 2), [[0, 256]], -(1 << 23), 0)
    iota("EX", [[0, 1024]], 1, 0)
    pick("EX", "EX", [[1, 2], [2, 64], [0, 8]], Op.is_equal, 0.0, 0, -1)
    iota("QP", [[-32, 4]], 0, 1)
    iota("E8", [[0, 256], [-2, 2]], 1, 0)
    pick("E8", "E8", [[-32, 4], [-4, 8], [0, 16]], Op.is_equal, 0.0, -3, 1)
    iota("ZR", [[0, 288]], 1, 0)
    iota(w("TRI", 0, 96), [[0, 6], [1, 16]], 0, 0)
    iota(v("TRI", 96), [[0, 6], [-16, 2], [1, 16]], 16, 0)
    for lo, hi, st in ((0, 96, 16), (15, 96, 16), (96, 288, 32), (127, 288, 32)): iota(v("ZR", lo, hi, st), [[0, 6]], 0, 0)
    iota("Z16", [[0, 1024]], 1, 0)
    iota(v("Z16", 0, 1024, 16), [[0, 64]], 0, 0)
    SP, GP_, PI = v("SPf"), v("GPf"), w("RC", 0, 1)
    def match(out, pattern, c, k=1.0): return lambda: ts(out, pattern, c, Op.is_equal, k, Op.mult)
    def twice(p):
        return [match(w("DUP", 256 * p + 128 * h, 128), v("C1"), w("RC", 16 * h + 8 * p, 1), 2.0) for h in range(2)] + [
            match(w("M2S", 128 * p, 128), v("C2"), w("RC", 8 * p, 1))]
    def affine(*items):
        for out, a, k, c in items: act(out, a, scale=k, bias=c)
    def row(s): return w("SQ", s, 1)
    for name, c in (("ONE", 1.0), ("XPRE", 17.0), ("JPRE", 1.0)): fill(v(name), c)
    for n, (k, m) in enumerate(((0, 15), (4, 7), (0, 1))): ts(w("PB", n, 1), v("PI"), k, Op.logical_shift_right, m, Op.bitwise_and)
    vc(SP, w("PB", 0, 1)); vc(GP_, w("PB", 1, 1))
    fill(v("JPRE", 0, 128, 1, 1), 16.0)
    fill(v("JPRE", 128, 192), 0.0)
    match(v("BLK2"), v("MG"), GP_, 2.0)()
    match(v("SQ"), w("CI", 0, 16), SP)()
    fill(v("JPRE", 96, 128, 1, 1), 592.0)
    fill(v("CM", 0, PAD), 0)
    fill(v("CQ"), 0.0)
    for s in range(8):
        ts(w("SEL", 128 * s, 128), v("BLK2"), row(s), Op.mult)
        act(w("SEL", 128 * s + 1024, 128), v("BLK2"), scale=row(s + 8))
    vc(v("KL"), w("CI", 0, 64))
    vc(v("PRh"), v("PR"))
    ts(w("LL", 0, 4), w("PR", 0, 4), float(PAD), Op.add)
    vc(w("LL", 4, 4), w("PR", 4, 4))
    for s in range(16): mm(v("K3", s, 128, 16), w("SEL", 128 * s, 128), v("PRh"), True, True)
    affine((w("cN", 0, 1), row(0), 0.1875, 128.0625), (w("cN", 1, 1), row(0), -0.1875, -128.0625), (w("MM", 0, 64), v("ND"), 1.0, 128.0),
           (v("cS"), row(0), 8188.0, -8192.0))
    ts(w("CK", 64, 64), w("MS", 0, 64), 15.0, Op.is_equal, 1024.0, Op.mult)
    tt(w("CK", 64, 64), w("CK", 64, 64), w("CI", 0, 64), Op.add)
    ts(w("CK", 128, 64), w("MS", 0, 64), 15.0, Op.not_equal, row(12), Op.mult)
    for name, c in (("ID", 1.0), ("I2", 2.0)): match(v(name), v("CI"), PI, c)()
    ts(w("CK", 0, 64), w("CK", 64, 64), row(14), Op.mult)
    ts(v("ZC"), w("MS", 0, 128), 1.0, Op.min)
    weave([match(v("EI"), v("CI"), PI, row(8)), match(v("EJ"), v("CI"), PI, row(10))] + twice(0) + [
        match(w("I2h", 128 * h, 128), v("C2"), w("RC", 16 * h, 1), 2.0) for h in range(2)])
    for out in (v("W16", 0, 16, 2), w("WK", 0, 8)): match(out, w("CI", 0, 8), GP_, v("cS"))()
    for out in (v("W16", 1, 16, 2), w("WK", 8, 8)): match(out, w("CI", 0, 8), GP_, UNIT)()

    def for_the_sums():
        affine((w("IJ", 0, 128), w("K3", 0, 128), 0.5, 0.0), (w("cL", 0, 1), PI, 2.0 ** -24, -1.5 * 2.0 ** -24),
               (w("cL", 1, 1), PI, -312.0 * 2.0 ** -25, 476.0 * 2.0 ** -25), (v("WZ"), v("BLK2"), UNIT / 2, 0.0),
               (v("L3"), v("M7", 0, 128, 1, 3), v("cL", 0, 1, 1, 3), v("cL", 1, 2, 1, 3)), (v("L3", 0, 128, 1, 1), v("CI", 0, 128, 1, 1), 0.0, 1.0),
               (v("RSM"), w("MS", 0, 128), -BIG, BIG / 2))

    def for_the_lists():
        ts(w("ownB", 0, 1), SP, 8.0, Op.min, -4096.0, Op.mult)
        ts(v("cW"), SP, 8.0, Op.is_le)
        ts(w("NDG", 128, 64), w("MS", 0, 64), SP, Op.not_equal, 16384.0, Op.mult)
        for h, c in ((0, 593.0), (1, 17.0)): ts(w("NDG", 64 * h, 64), w("NDG", 128, 64), c, Op.max)

    def for_the_choice():
        affine((v("cO"), w("PB", 2, 1), -2.0, 1.0), (w("FA", W, 4 * P), w("MS", 0, 4 * P), 0.0, 1.0),
               (w("ownA", 0, 1), SP, -65536.0, 8 * 65536.0), (w("ownB", 1, 1), w("ownB", 0, 1), 1.0, 16384.0),
               (v("RS8"), v("M7"), -BIG, 1 + 2.0 ** -15 + 2.0 ** -20),
               (w("ownA", 1, 1), w("ownA", 0, 1), v("cO"), 0.0), (w("ownB", 2, 1), w("ownB", 1, 1), v("cO"), 0.0),
               (w("CNT", 0, 64), v("CI", 0, 64, 1, 1), 0.0, -65536.0), (w("CNT", 64, 64), v("CI", 0, 64, 1, 1), 0.0, -32768.0),
               (w("OWN", 0, 64), w("CI", 0, 64), 0.0, w("ownB", 2, 1)), (w("OWN", 64, 64), w("CI", 0, 64), 0.0, w("ownA", 1, 1)),
               (v("E8"), v("E8"), 2.0 ** 34, 0.0), (w("cH", 1, 1), row(14), 2.0, 0.0), (w("cH", 2, 1), row(12), 8192.0, 0.0),
               (v("cK"), row(12), W / 2, w("cH", 1, 1)), (v("SELW"), v("BLK2"), v("cW"), 0.0), (v("SELJ"), v("BLK2"), row(10), 0.0),
               (v("SELP"), v("BLK2"), v("cK"), 0.0), (v("SELQ"), v("BLK2"), w("cH", 2, 1), 0.0),
               (w("cH", 3, 1), row(9), -2.0, 0.0), (v("NI2"), v("I2"), -1.0, 0.0), (v("SELN"), v("BLK2"), w("cH", 3, 1), 0.0))

    for_the_strikes = [lambda: ts(v("TRI"), v("TRI"), SP, Op.is_ge, 16384.0, Op.mult),
                       lambda: [ts(v("TRI", lo, hi, st), w("CI", 0, 6), 0.0, Op.mult) for lo, hi, st in ((15, 96, 16), (127, 288, 32))]]
    for_the_strikes += twice(1) + [
        lambda: [fill(v("RT"), 65535), fill(v("RQ"), 0.0)], lambda: ts(w("cH", 0, 1), row(0), 0.5, Op.mult, -128.0, Op.add),
        lambda: [ts(w("cP", h, 1), SP, 32.0, Op.mult, W + 256.0 + 16 * h, Op.add) for h in range(2)],
        lambda: ts(v("HALF"), w("CI", 0, 32), 0.0, Op.mult, w("cH", 0, 1), Op.add), lambda: fill(v("NQ"), 0.0),
        lambda: weave([match(w("SY", 8 * q, 8), v("CI", 3, 32, 4), w("QP", q, 1)) for q in range(4)])]

    def lists(t, c): return w("TS", 400 * (t % 2) + 64 * c + 60, 2)
    def marks(t):
        return [lambda c=c: tt(ix("FA", W + 768, lists(t, c)), w("AV", 32 * c, 32), v("HALF"), Op.add) for c in range(6)]
    def minus(t): act(w("AY", 192 * (t % 2), 192), v("AV"), scale=-1.0, bias=128.0)
    def strikes(t):
        return [lambda c=c: vc(ix("YF", W + 768, lists(t, c)), w("AY", 192 * (t % 2) + 32 * c, 32)) for c in range(6)]

    one1 = v("ONE", 0, 128, 1, 1)
    YP = w("YY", 0, 64)
    for t in range(RO):
        par, last = t % 2, t == RO - 1
        jw, iw = w("IJ", 128 * t, 64), w("IJ", 128 * t + 64, 64)
        need = w("MM", 64 * t, 64)
        if t:
            landed("l", t, "LL", 8); landed("i", t, "IJ", 128); landed("n", t, "MM", 64)

        XB = [w(bank, 64 * h, 64) for bank in ("XB0", "K1", "K2", "XB1") for h in range(2)]
        for bank in ("XB0", "K1", "K2", "XB1"): mm(w(bank, 0, 128), one1, v("XPRE"), True, False)
        act(v("Xf"), ix("CM", PAD + 2048, w("LL", 8 * t, 4)))
        if t:
            act(YP, ix("RM", 1536, w("LL", 8 * t + 4, 4)), scale=2.0, bias=593.0)
            minus(t - 1)
        else:
            act(v("NB"), need, scale=-1.0, bias=w("cN", 0, 1))
            act(v("NR"), ix("MM", 64, v("KL")), bias=w("cN", 1, 1))
            ts(YP, ix("RM", 1536, w("LL", 4, 4)), 2.0, Op.mult, 593.0, Op.add)
        for b in range(8): mm(XB[b], w("SEL", 128 * (8 * par + b), 128), v("Xf"), False, b % 2 == 1)

        def prod(b): return lambda: tt(v("Pc", b, 512, 8), XB[b], YP, Op.mult)
        def shift(lo, hi): return lambda: ts(v("Pi", lo, hi), v("Pc", lo, hi), 5, Op.logical_shift_right, W - 1, Op.bitwise_and)
        def conv(lo, hi): return lambda: vc(v("OF", lo, hi), v("Pi", lo, hi))

        if t:
            turns(HEAD[t > 1], marks(t - 1), [prod(b) for b in range(8)] + [shift(0, 128), shift(128, 512)])
            act(v("NB"), need, scale=-1.0, bias=w("cN", 0, 1))
            act(v("NQ", 0, 1024, 16), need, bias=w("cN", 1, 1))
            for lo, hi in ((0, 128), (128, 512)): act(v("OF", lo, hi), v("Pi", lo, hi))
        else:
            weave([prod(b) for b in range(8)] + [shift(0, 128), conv(0, 128)])
            for_the_sums()
        mm(w("JI", 0, 192), v("ONE"), v("JPRE"), True, False)
        for h in range(2): mm(w("JI", 64, 32), w("DUP", 256 * par + 128 * h, 128), v("Xf", h, 64, 2), False, False)
        mm(w("JI", 128, 64), w("M2S", 128 * par, 128), v("Xf"), False, False)
        for h in (0, 128): mm(w("JI", 128, 64), v("ID"), w("CK", h, 64), False, False)
        mm(w("JI", 0, 64), v("I2"), iw, False, False)
        for h in range(2): mm(w("JI", 96, 32), w("I2h", 128 * h, 128), v("IJ", 128 * t + h, 128 * t + 64, 2), False, False)
        mm(w("JI", 128, 64), v("EI"), iw, False, False)
        mm(w("JI", 128, 64), v("EJ"), jw, False, True)
        if t == 0: act(w("YY", 64, 32), w("JI", 96, 32))

        def far(q, eng):
            mine = [15, 13, 11, 9, 7, 5, 3, 1][:PLAN[q].count("g") + (MORE[q] if t else 0)]
            def one(k):
                out, src = w("G", 128 * k, 128), ix("FA", W, w("OF", 8 * k, 8))
                if eng == "S": act(out, src, Act.Relu, bias=w("NB", k, 1))
                else: ts(out, src, w("NB", k, 1), Op.add, 0.0, Op.max)
            return [lambda k=k: one(16 * q + k) for k in range(16) if (k in mine) == (eng == "V")]
        def sums(q, sp, lo=0, hi=16):
            for a in range(16):
                mm((T["K%d" % q][8 * lo:8 * hi, 4 * (a % 8) + 2 * (a // 8):512:32], [("K%d" % q, 0, 512, 1)]),
                   v("G", 2048 * q + 128 * lo + a, 2048 * q + 128 * hi, 16), v("WK"), False, sp and a == 15)
        def keys(q, m):
            n, on = 128 * m, range(q, q + m)
            return [lambda c=c: ts(w("II", 128 * (c - q), 128), v("K%d" % c, 0, 256, 2), 8191.0 + 32768.0, Op.add) for c in on] + [
                lambda: ts(v("MX", 1, 2 * n, 2), w("II", 0, n), MASK, Op.bitwise_and)] + [
                lambda c=c: scan(w("KK", 256 * c, 256), w("MX", 256 * (c - q), 256), w("K%d" % c, 256, 256), Op.add, Op.max) for c in on]
        def lowest(q):
            return [lambda: scan(w("SC", 128 * q, 128), v("RSM"), v("KK", 256 * q + 1, 256 * q + 256, 2), Op.max, Op.min)]

        weave(far(0, "S"))
        def near(): tt(w("Pc", 512, 96), w("JI", 0, 96), v("YY"), Op.mult)
        if t: turns(PLAN[0], far(0, "V"), [lambda: carry(v("NR"), v("Z16"), v("NQ")), lambda: vc(w("YY", 64, 32), w("JI", 96, 32)),
                                           near, shift(512, 608), conv(512, 608)])
        else: weave([near, shift(128, 608), for_the_lists, conv(128, 608)] + far(0, "V"))
        for q in range(4): mm(w("K%d" % q, 0, 512), v("L3"), v("IDK", 0, 512), True, False)
        mm(w("CB", 0, 192), one1, v("IDK", 257, 449, 1, 1), True, False)
        tt(v("G1"), ix("FA", W, w("OF", 512, 64)), v("NR"), Op.max)
        tt(v("G2"), ix("FA", W, w("OF", 576, 32)), v("NR", 0, 1024, 2), Op.max)
        for q in range(4):
            mm(v("K%d" % q, 256, 512, 2), v("NR", 256 * q, 256 * q + 256, 2), v("WZ"), False, False)
        sums(0, False)
        for a in range(8): mm(cb(2 * a, 2), v("G1", a, 1024, 8), v("W16"), False, False)
        for q in range(4): mm(w("CB", 128 + 16 * q, 16), w("G2", 128 * q, 128), v("W16"), False, q == 3)
        weave(far(1, "S"))
        turns(PLAN[1], far(1, "V"), [
            lambda: ts(w("II", 0, 96), v("CB", 0, 192, 2), 510.0, Op.add), lambda: ts(v("MI"), w("II", 0, 96), MASK, Op.bitwise_and),
            lambda: tt(v("UU"), v("MI"), v("CB", 1, 192, 2), Op.add),
            lambda: [ts(v("CD"), v("UU"), 0.0, Op.max), ts(v("CQ", 0, 128, 16), w("UU", 88, 8), 0.0, Op.max)]])
        sums(1, False)
        for q in range(4):
            for h in range(4): mm(v("K%d" % q, 256 + h, 512, 4), w("EX", 512 * (h // 2) + 128 * q, 128), w("CD", 0, 64), False, h == 3 and q < 2)
        weave(far(2, "S"))
        turns(PLAN[2], far(2, "V"), [lambda: carry(v("CR"), v("ZC"), v("CQ"))] + keys(0, 2))
        for h in range(2): mm(v("K3", 256 + h, 512, 2), v("ID"), v("CR"), False, False)
        sums(2, True)
        weave(far(3, "S"))
        turns(PLAN[3], far(3, "V"), keys(2, 1) + lowest(0))
        for lo, hi in ((0, 8), (8, 12), (12, 16)): sums(3, True, lo, hi)
        act(w("YM", 64, 64), YP, bias=-296.5, scale=0.5)
        act(w("YM", 0, 64), w("JI", 128, 64))
        if t == 0: for_the_choice()
        mm(w("CB", 0, 128), v("ID"), v("YM"), True, False)
        mm(w("CB", 0, 128), v("ID"), v("OWN"), False, False)
        mm(w("XB0", 0, 128), v("ID"), w("NDG", 0, 128), True, False)
        mm(w("XB0", 0, 128), one1, v("CNT"), False, False)
        if t: mm(w("XB1", 0, 288), v("ID"), v("TRI"), True, False)
        if not last: mm(w("JI", 256, 128), one1, v("CNT"), True, False)
        act(v("FA", W, W + 4 * P, 4), need, scale=2.0, bias=-255.0)
        for lo, own in ((15, w("LL", 8 * t + 4, 4)), (207, w("LL", 8 * t, 4))): act(v("ZS", lo, lo + 49, 16), own, scale=2.0, bias=17.0)

        old = [strikes(t - 1)[FILL.index(n)] if n in FILL else None for n in range(11)] if t else for_the_strikes
        kf = v("KF", 7, 128, 8)
        def parts():
            ts(v("KF", 135, 256, 8), kf, 48.0, Op.add, -48.0, Op.add)
            ts(v("KF", 263, 384, 8), kf, 1536.0, Op.add, -1536.0, Op.add)
        def spread():
            mm(w("K0", 0, 64), v("ID"), w("NDG", 128, 64), True, False)
            if t == 0: mm(w("XB1", 0, 288), v("ID"), v("TRI"), True, False)
            tt(v("TBf"), v("KF", 7, 256, 8), v("KF", 135, 384, 8), Op.subtract)
            for q in range(4): mm(cb(4 * q, 4), w("E8", 128 * q, 128), v("TBf"), False, q == 3)
        def turn(lo, n):
            src = v("SC", 4 * lo + 3, 4 * (lo + n), 4)
            return lambda: do("V", g.vector.transpose, w("ST", lo, n), [src], (src[0],))
        def least(lo, n): return lambda: scan(w("KF", lo, n), w("RS8", lo, n), w("ST", lo, n), Op.max, Op.min)
        low = v("SC", 15, 384, 16)
        early = [lambda: tt(low, low, w("CD", 64, 24), Op.add), turn(0, 96), least(0, 96)]
        weave(lowest(1) + old[:1] + lowest(2))
        weave(keys(3, 1) + lowest(3) + [turn(96, 32), least(96, 32), parts, spread], early + old[1:6])
        act(w("YI", 16 * t, 16), v("KF", 263, 384, 8), scale=8192.0)
        weave(old[6:7])
        ts(v("UAW"), w("CB", 0, 128), 0.0, Op.max, 4096.0, Op.min)
        def names(bank, o):
            mm(w(bank, o, 64), v("BLK2"), w("UAW", 64, 64), False, False)
            mm(w(bank, o, 64), v("SELJ"), w("UAW", 0, 64), False, False)
            mm(w(bank, o + 64, 64), v("SELW"), w("UAW", 0, 64), False, True)
        names("XB0", 0)
        mm(w("K0", 0, 64), v("SELP"), w("UAW", 0, 64), False, True)
        if not last: names("JI", 256)
        for n in range(6):
            for o, sel, c in ((16 * n, "SELQ", 0), (96 + 32 * n, "SELN", 0), (112 + 32 * n, "SELQ", 1)):
                mm(w("XB1", o, 16), v(sel), w("UAW", 32 * (n % 2) + 16 * c, 16), False, False)
        weave(old[7:8])
        scan(w("ZS", 64, 128), v("RSM"), w("XB0", 0, 128), Op.max, Op.min)
        act(w("LS", 8 * t, 8), v("ZS", 79, 192, 16), scale=0.5, bias=-8.5)
        send("l", t, w("LL", 8 * t + 8, 8), w("LS", 8 * t, 8))
        if not last: act(w("IS", 128 * t, 128), w("JI", 256, 128), scale=0.5)

        scan(v("FS"), w("RSM", 0, 64), w("K0", 0, 64), Op.max, Op.min)
        weave([lambda: tt(v("PF"), v("ZS", 15, 192, 16), v("ZS", 79, 256, 16), Op.mult),
               lambda: ts(v("FI"), v("PF"), 5, Op.logical_shift_right, W - 1, Op.bitwise_and)])
        act(v("TNh", 6), v("FI"), bias=-2048.0)
        act(w("TNh", 0, 6), v("FI", 0, 12, 2), bias=-2048.0)
        def target(k): tt(w("TNu", 4 * k, 4), w("FI", 4 * k, 4), v("FS", 15, 64, 16), Op.max)
        target(1)
        for h, out in enumerate((v("RQ", 0, 96, 16), v("RQ", 96, 288, 32))): ts(out, v("FI", h, 12, 2), -2048.0, Op.add)
        target(0); target(2)
        carry(v("RR"), v("ZR"), v("RQ"))
        act(w("NS", 64 * t, 64), ix("FA", W + 4 * P, w("TNu", 4, 4)), scale=0.5, bias=127.625)
        send("n", t, w("MM", 64 * t + 64, 64), w("NS", 64 * t, 64))
        act(v("AV"), ix("FA", W + 4 * P, v("TNu")), bias=127.75)
        for h, out in enumerate((v("RT", 0, 96, 16), v("RT", 96, 288, 32))): vc(out, v("TNu", h, 12, 2))
        weave(old[8:9])
        if last: minus(t)
        else: send("i", t, w("IJ", 128 * t + 128, 128), w("IS", 128 * t, 128))
        for s in range(15): mm(v("XB1", s, 288, 16), w("SEL", 128 * s, 128), v("TNh"), False, False)
        mm(v("XB1", 111, 288, 32), w("SEL", 128 * 15, 128), v("TNh", 6, 18, 2), False, False)
        mm(w("XB1", 0, 288), v("NI2"), v("RR"), False, True)
        weave(old[9:10])
        for h, (lo, n) in enumerate(((0, 96), (96, 192))): ts(w("EQ", lo, n), w("XB1", lo, n), 0.0, Op.is_equal, w("cP", h, 1), Op.mult)
        weave(old[10:11])
        scan(v("TS", 400 * par + 4, 400 * par + 388, 4), w("RT", 0, 96), w("EQ", 0, 96), Op.min, Op.max, BIG)
        scan(v("TS", 400 * par + 1, 400 * par + 385, 2), v("RT", 96), v("EQ", 96), Op.min, Op.max, BIG)

    def costs():
        for k in range(16): mm(v("JI", k, 320, 16, 8), w("SY", 8 * (k // 4), 8), v("YC", k % 4, 80, 4), True, True)
    weave(strikes(RO - 1), [
        lambda: ts(v("YT"), v("YI"), 8192.0, Op.is_ge, -8193.0, Op.mult),
        lambda: tt(v("YC"), v("YI"), v("YT"), Op.add), costs])
    landed("l", RO, "LL", 8); landed("n", RO, "MM", 64)
    dma("D", "out", 80, ext(T.yf[:, 0:W - ROT], "yf1"), v("YF", ROT, W))
    dma("D", "out", 80, ext(T.yf[:, W - ROT:W], "yf2"), v("YF", 0, ROT))
    affine((w("YPo", 0, 4), w("LL", 44, 4), 1.0, 0.0), (w("YPo", 4, 4), w("LL", 40, 4), 1.0, -float(PAD)), (v("YZo"), w("MM", 320, 64), 1.0, -128.0))
    dma("S", "out", 80, ext(T.yp[:], "yp"), v("YPo"))
    dma("S", "out", 80, ext(T.yz[:], "yz"), v("YZo"))
    act(v("YO"), v("JI", 0, 320, 1, 8))
    dma("S", "out", 80, ext(T.yc[:], "yc"), v("YO"))
    wait("P", "ls", sent[0])
    wait("D", "out", 80)
    for q in "VSTP": wait("D", q, cnt[q])
